import numpy as np
import ml_dtypes


def mxq(x, axis, fmt="e4m3"):
    dtype, down = {"e4m3": (ml_dtypes.float8_e4m3fn, 7), "e5m2": (ml_dtypes.float8_e5m2, 14)}[fmt]
    v = np.moveaxis(np.asarray(x, np.float32).astype(ml_dtypes.bfloat16).astype(np.float64), axis, -1)
    blocks = v.reshape(v.shape[:-1] + (-1, 32))
    amax = np.abs(blocks).max(-1, keepdims=True)
    byte = np.maximum(np.where(amax > 0, np.frexp(amax)[1] - 1 + 127, 0) - down, 1)
    scale = np.exp2(byte - 127.0)
    codes = (blocks / scale).astype(np.float32).astype(dtype).astype(np.float64)
    return np.moveaxis((codes * scale).reshape(v.shape), -1, axis)


WIDE = False


def mx_kscale(k):
    if not WIDE:
        return np.ones(k)
    levels = np.array([10, -10, 5, -5, 0])
    if k % 512:
        return np.exp2(np.random.permutation(np.resize(levels, k // 32))).repeat(32)
    a = np.empty((k // 512, 16))
    for p in range(k // 512):
        a[p, :8] = np.random.permutation(np.resize(levels, 8))
        for g in range(8):
            far = levels[np.abs(levels - a[p, g]) >= 10]
            a[p, g + 8] = far[np.random.randint(len(far))]
    return np.exp2(a.ravel()).repeat(32)


def f64(x):
    return np.asarray(x).astype(np.float64)


def striped(idx):
    return np.tile(idx.reshape(-1, 16).T, (8, 1)).astype(np.uint16)


def unstriped(offs):
    return offs[:16].T.reshape(-1).astype(np.int64)


E2M1 = np.array([0.0, 0.5, 1.0, 1.5, 2.0, 3.0, 4.0, 6.0, -0.0, -0.5, -1.0, -1.5, -2.0, -3.0, -4.0, -6.0])


def pack_weight(w, fmt):
    k, n = w.shape
    w = f64(np.asarray(w, np.float32).astype(ml_dtypes.bfloat16)).reshape(k // 32, 32, n)
    amax = np.abs(w).max(1)
    if fmt == "e4m3":
        byte = np.frexp(amax)[1] - 1 + 127 - 7
    else:
        mant, ex = np.frexp(amax / 6.0)
        byte = np.where(mant > 0.5, ex, ex - 1) + 127
    byte = np.clip(np.where(amax > 0, byte, 1), 1, 254)
    scaled = (w * np.exp2(127.0 - byte)[:, None, :]).reshape(k, n).astype(np.float32)
    by_word = np.ascontiguousarray(scaled.reshape(k // 512, 128, 4, n).transpose(0, 1, 3, 2))
    if fmt == "e4m3":
        words = by_word.astype(ml_dtypes.float8_e4m3fn).view(np.uint8)
    else:
        c = by_word.astype(ml_dtypes.float4_e2m1fn).view(np.uint8) & 0xF
        words = (c[..., 0::2] | (c[..., 1::2] << 4)).reshape(k // 512, 128, 2 * n)
    return np.ascontiguousarray(words), np.ascontiguousarray(byte.astype(np.uint8).reshape(k // 512, 16, n))


def unpack_weight(words, scales, fmt):
    g, _, n = scales.shape
    words = np.ascontiguousarray(words).reshape(g, 128, n, -1)
    if fmt == "e4m3":
        vals = words.view(ml_dtypes.float8_e4m3fn).astype(np.float64)
    else:
        nib = np.empty((g, 128, n, 4), np.uint8)
        nib[..., 0::2] = words & 0xF
        nib[..., 1::2] = words >> 4
        vals = E2M1[nib]
    vals = vals * np.repeat(np.exp2(scales.astype(np.float64) - 127.0), 8, axis=1)[..., None]
    return vals.transpose(0, 1, 3, 2).reshape(g * 512, n)


def gelu(v):
    return 0.5 * v * (1.0 + np.tanh(np.sqrt(2.0 / np.pi) * (v + 0.044715 * v**3)))


def often(T, S):
    return np.random.permutation(T)[(T * np.random.uniform(0, 1, S) ** 4).astype(np.int64)]


K, M, H, N, T, S = 1024, 512, 1024, 512, 4096, 1024

def setup_inputs():
    n = np.random.standard_normal
    s1 = mx_kscale(K)[:, None]
    s2 = mx_kscale(M)[:, None]
    u = mx_kscale(H)[:, None]
    tab_words, tab_scales = pack_weight(n((K, T)) * s1, "e4m3")
    tab2_words, tab2_scales = pack_weight(n((M, T)) * s2, "e2m1")
    w1_words, w1_scales = pack_weight(0.45 * n((K, H)) / np.sqrt(K) / s1, "e2m1")
    w2 = (0.45 * n((M, H)) / np.sqrt(M) / s2).astype(np.float32)
    w3_words, w3_scales = pack_weight(1.5 * n((H, N)) / np.sqrt(H) / u, "e4m3")
    gain = (np.random.uniform(0.7, 1.6, H) * u[:, 0]).astype(np.float32)
    phase = (0.4 * n((H, S)) * u).astype(np.float32)
    return {"tab_words": tab_words, "tab_scales": tab_scales,
            "tab2_words": tab2_words, "tab2_scales": tab2_scales,
            "offs": striped(often(T, S)), "offs2": striped(often(T, S)),
            "w1_words": w1_words, "w1_scales": w1_scales, "w2": w2,
            "w3_words": w3_words, "w3_scales": w3_scales,
            "gain": gain, "phase": phase}

def reference(tab_words, tab_scales, tab2_words, tab2_scales, offs, offs2,
              w1_words, w1_scales, w2, w3_words, w3_scales, gain, phase):
    v = unpack_weight(tab_words, tab_scales, "e4m3")[:, unstriped(offs)]
    v2 = unpack_weight(tab2_words, tab2_scales, "e2m1")[:, unstriped(offs2)]
    w1 = unpack_weight(w1_words, w1_scales, "e2m1")
    w3 = unpack_weight(w3_words, w3_scales, "e4m3")
    a = w1.T @ v
    b = mxq(f64(w2), 0, "e4m3").T @ v2
    h = f64(gain)[:, None] * (np.sin(a) * np.cos(b)) + f64(phase)
    return w3.T @ mxq(h, 0, "e4m3")

@@ -1,0 +1,260 @@
+import math
+from contextlib import ExitStack
+
+import concourse.mybir as mybir
+
+F32 = mybir.dt.float32
+BF16 = mybir.dt.bfloat16
+I32 = mybir.dt.int32
+U32 = mybir.dt.uint32
+U16 = mybir.dt.uint16
+U8 = mybir.dt.uint8
+FP8X4 = mybir.dt.float8_e4m3fn_x4
+FP4X4 = mybir.dt.float4_e2m1fn_x4
+ACT = mybir.ActivationFunctionType
+ALU = mybir.AluOpType
+
+K, M, H, N, T, S = 1024, 512, 1024, 512, 4096, 1024
+P = 128
+PACK = 4
+PASS = P * PACK
+JW = 512
+FLOPS = 2 * S * (K * H + M * H + H * N)
+
+
+def tile_list_cable_tilt_displacement_kernel(
+    tc, tab_words, tab_scales, tab2_words, tab2_scales, offs, offs2,
+    w1_words, w1_scales, w2, w3_words, w3_scales, gain, phase, out,
+):
+    nc = tc.nc
+    with ExitStack() as ctx:
+        keep = ctx.enter_context(tc.tile_pool(name="keep", bufs=1))
+        ring = ctx.enter_context(tc.tile_pool(name="ring", bufs=2))
+        psum = ctx.enter_context(tc.psum_pool(name="psum", bufs=1))
+
+        def held(shape, dtype, name, tag=None):
+            return keep.tile(shape, dtype, name=name, tag=tag or name, align_bytes=64)
+
+        list1 = keep.tile([P, S // 16], U16, name="list1")
+        list2 = keep.tile([P, S // 16], U16, name="list2")
+        tab_w = [held([P, T], U32, f"tab_w{a}") for a in range(2)]
+        tab_s = held([P, T], U8, "tab_s")
+        tab2_w = held([P, T], U16, "tab2_w")
+        tab2_s = held([P, T], U8, "tab2_s")
+        w1_w = held([P, 2, H], U16, "w1_w")
+        w1_s = held([P, H], U8, "w1_s")
+        w1p_w = [held([P, 2, PASS], U16, f"w1p_w{g}") for g in range(2)]
+        w1p_s = [held([P, H], U8, f"w1p_s{a}") for a in range(2)]
+        w2_raw0 = [held([P, PACK, PASS // 2], F32, f"w2_raw0{u}") for u in range(2)]
+        w2_raw1 = held([P, PACK, PASS], F32, "w2_raw1")
+        sin_h = held([P, PACK, JW], F32, "sin_h")
+        gain_m2 = held([P, PACK], F32, "gain_m2")
+        w2_bf = [held([P, PASS * PACK], BF16, f"w2_bf{g}") for g in range(2)]
+        w2_c = [held([P, PASS], U32, f"w2_c{g}") for g in range(2)]
+        w2_s = [held([P, PASS], U8, f"w2_s{g}") for g in range(2)]
+        gain_sb = held([P, 2, PACK], F32, "gain_sb")
+        phase_sb = {}
+        v_w = [[held([P, JW], U32, f"v_w{a}{jh}") for jh in range(2)] for a in range(2)]
+        v_s = [held([P, S], U8, f"v_s{a}") for a in range(2)]
+        v2_w = [held([P, JW], U16, f"v2_w{jh}") for jh in range(2)]
+        v2_s = [held([P, JW], U8, f"v2_s{jh}") for jh in range(2)]
+        cos_b = [[held([P, PACK, JW], F32, f"cos{g}{jh}") for jh in range(2)] for g in range(2)]
+        h_c = [[held([P, JW], U32, f"h_c{g}{jh}") for jh in range(2)] for g in range(2)]
+        h_s = [[held([P, JW], U8, f"h_s{g}{jh}") for jh in range(2)] for g in range(2)]
+        warm_in = held([P, 8], F32, "warm_in")
+        warm_out = held([P, 8], F32, "warm_out")
+
+        nc.vector.memset(warm_in[:], 0.0)
+        nc.scalar.activation(warm_out[:], warm_in[:], ACT.Sin)
+        for plane in (tab2_s, tab_s):
+            nc.vector.memset(plane[:, :T // 2].bitcast(I32), 0)
+            nc.gpsimd.memset(plane[:, T // 2:].bitcast(I32), 0)
+        nc.vector.memset(w1_s[:].bitcast(I32), 0)
+        for plane in (v_s[1], w1p_s[1]):
+            nc.gpsimd.memset(plane[:].bitcast(I32), 0)
+
+        def load_two_pass_scales(plane, scales):
+            rows = scales.bitcast(I32).rearrange("a (q r) n -> r q a n", r=4)
+            for r in range(4):
+                nc.sync.dma_start(plane[r:P:16, :].bitcast(I32), rows[r])
+
+        def load_w2(raw, c0):
+            nc.sync.dma_start(raw[:], w2[:, c0:c0 + raw.shape[2]].rearrange("(p i) c -> p i c", i=PACK))
+
+        def load_phase(g, jh, dst):
+            phase_sb[g, jh] = dst
+            nc.sync.dma_start(
+                dst,
+                phase[g * PASS:(g + 1) * PASS, jh * JW:(jh + 1) * JW].rearrange("(p t) j -> p t j", t=PACK))
+
+        def load_tab(a):
+            nc.sync.dma_start(tab_w[a][:].bitcast(I32), tab_words[a].rearrange("p t i -> p (t i)").bitcast(I32))
+
+        def shift(planes):
+            nc.sync.dma_start(planes[1][0:112, :].bitcast(I32), planes[0][16:P, :].bitcast(I32))
+
+        nc.sync.dma_start(list2[:], offs2)
+        load_w2(w2_raw0[0], 0)
+        load_w2(w2_raw0[1], PASS // 2)
+        for q in range(4):
+            nc.sync.dma_start(tab2_s[32 * q:32 * q + 4, :].bitcast(I32), tab2_scales[0, 4 * q:4 * q + 4, :].bitcast(I32))
+        nc.sync.dma_start(tab2_w[:].bitcast(I32), tab2_words[0].bitcast(I32))
+        nc.sync.dma_start(list1[:], offs)
+        load_w2(w2_raw1, PASS)
+        load_two_pass_scales(tab_s, tab_scales)
+        load_tab(0)
+        load_two_pass_scales(w1_s, w1_scales)
+        nc.sync.dma_start(w1_w[:].bitcast(I32), w1_words.bitcast(I32).rearrange("a p n -> p a n"))
+        load_tab(1)
+        nc.sync.dma_start(gain_sb[:], gain.rearrange("(g p t) -> p g t", g=2, t=PACK))
+
+        def half(lst, jh):
+            return lst[:, jh * (JW // 16):(jh + 1) * (JW // 16)]
+
+        def cast_w2(g, raw, m0):
+            nc.scalar.copy(
+                w2_bf[g][:].rearrange("p (t m i) -> p m i t", t=PACK, i=PACK)[:, m0:m0 + raw.shape[2] // PACK],
+                raw[:].rearrange("p i (m t) -> p m i t", t=PACK))
+
+        def quantise_w2(g):
+            nc.vector.quantize_mx(w2_c[g][:].bitcast(FP8X4), w2_s[g][:], w2_bf[g][:])
+
+        def cosines(g, jh, by_half_angle=False):
+            abs_b = cos_b[g][jh]
+            for t in range(PACK):
+                cols = slice(t * P, (t + 1) * P)
+                bank = psum.tile([P, JW], F32, name="b_bank", bufs=2)
+                nc.tensor.matmul_mx(
+                    bank[:], lhsT=w2_c[g][:, cols].bitcast(FP8X4), lhsT_scale=w2_s[g][:, cols],
+                    rhs=v2_w[jh][:].bitcast(FP4X4), rhs_scale=v2_s[jh][:], start=True, stop=True)
+                if by_half_angle:
+                    nc.scalar.activation(sin_h[:, t, :], bank[:], ACT.Sin, scale=0.5)
+                else:
+                    nc.scalar.activation(abs_b[:, t, :], bank[:], ACT.Abs)
+            if not by_half_angle:
+                nc.scalar.activation(cos_b[g][jh][:], abs_b[:], ACT.Sin, bias=math.pi / 2, scale=-1.0)
+
+        def strain_angles(g, jh, t):
+            bank = psum.tile([P, JW], F32, name="a_bank", bufs=4)
+            cols = slice(t * P, (t + 1) * P)
+            scols = slice(g * PASS + t * P, g * PASS + (t + 1) * P)
+            for a in range(2):
+                nc.tensor.matmul_mx(
+                    bank[:], lhsT=w1p_w[g][:, a, cols].bitcast(FP4X4), lhsT_scale=w1p_s[a][:, scols],
+                    rhs=v_w[a][jh][:].bitcast(FP8X4), rhs_scale=v_s[a][:, jh * JW:(jh + 1) * JW],
+                    start=(a == 0), stop=(a == 1))
+            return bank
+
+        def sine_times_cosine(g, jh, t, bank, js, sin_a, prod, first_op):
+            nc.scalar.activation(sin_a[:, t, js], bank[:, js], ACT.Sin)
+            nc.vector.scalar_tensor_tensor(
+                prod[:, t, js], cos_b[g][jh][:, t, js], gain_sb[:, g, t:t + 1], sin_a[:, t, js], first_op, ALU.mult)
+
+        def products(g, jh, first_op=ALU.mult):
+            sin_a = ring.tile([P, PACK, JW], F32, name="sin_a")
+            prod = ring.tile([P, PACK, JW], F32, name="prod")
+            for t in range(PACK):
+                sine_times_cosine(g, jh, t, strain_angles(g, jh, t), slice(0, JW), sin_a, prod, first_op)
+            return prod
+
+        def add_phase(g, jh, prod, js=slice(0, JW)):
+            h_bf = ring.tile([P, (js.stop - js.start) * PACK], BF16, name="h_bf", align_bytes=64)
+            nc.vector.tensor_tensor(
+                h_bf[:].rearrange("p (c i t) -> p c t i", i=2, t=PACK),
+                prod[:, :, js].rearrange("p t (c i) -> p c t i", i=2),
+                phase_sb[g, jh][:, :, js].rearrange("p t (c i) -> p c t i", i=2), ALU.add)
+            return h_bf
+
+        def quantise_h(g, jh, h_bf, js=slice(0, JW)):
+            nc.vector.quantize_mx(h_c[g][jh][:, js].bitcast(FP8X4), h_s[g][jh][:, js], h_bf[:])
+
+        def last_product(jh, js=slice(0, JW), share=False):
+            width = js.stop - js.start
+            for c in range(N // P):
+                cols = slice(c * P, (c + 1) * P)
+                bank = psum.tile([P, width], F32, name="o_bank", bufs=2)
+                for g in range(2):
+                    nc.tensor.matmul_mx(
+                        bank[:], lhsT=w3_w[:, g, cols].bitcast(FP8X4), lhsT_scale=w3_s[:, g, cols],
+                        rhs=h_c[g][jh][:, js].bitcast(FP8X4), rhs_scale=h_s[g][jh][:, js],
+                        start=(g == 0), stop=(g == 1))
+                res = ring.tile([P, width], F32, name="res", bufs=4)
+                if share and c % 2 == 1:
+                    nc.vector.tensor_copy(res[:], bank[:])
+                else:
+                    nc.scalar.copy(res[:], bank[:])
+                nc.sync.dma_start(out[cols, jh * JW + js.start:jh * JW + js.stop], res[:])
+
+        cast_w2(0, w2_raw0[0], 0)
+        cast_w2(0, w2_raw0[1], P // 2)
+        nc.vector.tensor_copy(v2_s[0][:], tab2_s[:].indirect(half(list2, 0)))
+        quantise_w2(0)
+        nc.vector.tensor_copy(v2_w[0][:], tab2_w[:].indirect(half(list2, 0)))
+        nc.vector.tensor_copy(v2_s[1][:], tab2_s[:].indirect(half(list2, 1)))
+        nc.vector.tensor_copy(v2_w[1][:], tab2_w[:].indirect(half(list2, 1)))
+        nc.vector.tensor_copy(v_s[0][:], tab_s[:].indirect(list1[:]))
+        shift(v_s)
+        cosines(0, 0)
+        cosines(0, 1, by_half_angle=True)
+        cast_w2(1, w2_raw1, 0)
+        quantise_w2(1)
+        nc.vector.tensor_copy(v_w[0][0][:], tab_w[0][:].indirect(half(list1, 0)))
+        nc.vector.tensor_copy(
+            w1p_s[0][:].rearrange("p (g t m) -> p g t m", g=2, t=PACK),
+            w1_s[:].rearrange("p (g m t) -> p g t m", g=2, t=PACK))
+        shift(w1p_s)
+        for g in range(2):
+            nc.vector.tensor_copy(
+                w1p_w[g][:].rearrange("p a (t m) -> p a t m", t=PACK),
+                w1_w[:, :, g * PASS:(g + 1) * PASS].rearrange("p a (m t) -> p a t m", t=PACK))
+        nc.vector.tensor_copy(v_w[0][1][:], tab_w[0][:].indirect(half(list1, 1)))
+        nc.vector.tensor_scalar_mul(gain_m2[:], gain_sb[:, 0, :], -2.0)
+        for t in range(PACK):
+            nc.vector.scalar_tensor_tensor(
+                cos_b[0][1][:, t, :], sin_h[:, t, :], gain_m2[:, t:t + 1], sin_h[:, t, :], ALU.mult, ALU.mult)
+        cosines(1, 0)
+        nc.vector.tensor_copy(v_w[1][0][:], tab_w[1][:].indirect(half(list1, 0)))
+        nc.vector.tensor_copy(v_w[1][1][:], tab_w[1][:].indirect(half(list1, 1)))
+
+        load_phase(0, 0, held([P, PACK, JW], F32, "phase00", tag="w1_s")[:])
+        phase_pair = held([P, 2, PACK, JW], F32, "phase_pair", tag="tab_w0")
+        load_phase(0, 1, phase_pair[:, 0])
+        load_phase(1, 0, phase_pair[:, 1])
+        w3_w = held([P, 2, N], U32, "w3_w", tag="w1_w")
+        nc.sync.dma_start(w3_w[:].bitcast(I32), w3_words.rearrange("a p c i -> p a (c i)").bitcast(I32))
+        w3_s = held([P, 2, N], U8, "w3_s", tag="tab_s")
+        nc.gpsimd.memset(w3_s[:].rearrange("p a n -> p (a n)").bitcast(I32), 0)
+        for q in range(4):
+            nc.sync.dma_start(
+                w3_s[32 * q:32 * q + 4, :, :].bitcast(I32),
+                w3_scales[:, 4 * q:4 * q + 4, :].bitcast(I32).rearrange("a r n -> r a n"))
+        load_phase(1, 1, held([P, PACK, JW], F32, "phase11", tag="tab_w1")[:])
+
+        prod = products(0, 0)
+        h00 = add_phase(0, 0, prod)
+        prod = products(0, 1, first_op=ALU.add)
+        quantise_h(0, 0, h00)
+        h01 = add_phase(0, 1, prod)
+        prod = products(1, 0)
+        cosines(1, 1)
+        quantise_h(0, 1, h01)
+        h10 = add_phase(1, 0, prod)
+        halves = [slice(0, JW // 2), slice(JW // 2, JW)]
+        sin_a = ring.tile([P, PACK, JW], F32, name="sin_a")
+        prod = ring.tile([P, PACK, JW], F32, name="prod")
+        banks = []
+        for t in range(PACK):
+            banks.append(strain_angles(1, 1, t))
+            sine_times_cosine(1, 1, t, banks[t], halves[0], sin_a, prod, ALU.mult)
+            if t == 0:
+                quantise_h(1, 0, h10)
+        h11a = add_phase(1, 1, prod, halves[0])
+        for t in range(PACK):
+            sine_times_cosine(1, 1, t, banks[t], halves[1], sin_a, prod, ALU.mult)
+            if t == 0:
+                quantise_h(1, 1, h11a, halves[0])
+        last_product(0)
+        h11b = add_phase(1, 1, prod, halves[1])
+        quantise_h(1, 1, h11b, halves[1])
+        last_product(1, halves[0])
+        last_product(1, halves[1], share=True)

@@ -37,22 +37,15 @@ def tile_list_cable_tilt_displacement_kernel(
 
         list1 = keep.tile([P, S // 16], U16, name="list1")
         list2 = keep.tile([P, S // 16], U16, name="list2")
-        tab_w = [held([P, T], U32, f"tab_w{a}") for a in range(2)]
-        tab_s = held([P, T], U8, "tab_s")
-        tab2_w = held([P, T], U16, "tab2_w")
+        tab_w = {}
         tab2_s = held([P, T], U8, "tab2_s")
-        w1_w = held([P, 2, H], U16, "w1_w")
-        w1_s = held([P, H], U8, "w1_s")
         w1p_w = [held([P, 2, PASS], U16, f"w1p_w{g}") for g in range(2)]
         w1p_s = [held([P, H], U8, f"w1p_s{a}") for a in range(2)]
-        w2_raw0 = [held([P, PACK, PASS // 2], F32, f"w2_raw0{u}") for u in range(2)]
-        w2_raw1 = held([P, PACK, PASS], F32, "w2_raw1")
-        sin_h = held([P, PACK, JW], F32, "sin_h")
-        gain_m2 = held([P, PACK], F32, "gain_m2")
-        w2_bf = [held([P, PASS * PACK], BF16, f"w2_bf{g}") for g in range(2)]
-        w2_c = [held([P, PASS], U32, f"w2_c{g}") for g in range(2)]
+        w2_raw0 = held([P, PACK, PASS], F32, "w2_raw0")
+        w2_bf0 = [held([P, PASS * 2], BF16, f"w2_bf0{u}", tag=("w1_w", "tab_w1")[u]) for u in range(2)]
+        w2_bf1 = held([P, PASS * PACK], BF16, "w2_bf1")
+        w2_c = {1: held([P, PASS], U32, "w2_c1")}
         w2_s = [held([P, PASS], U8, f"w2_s{g}") for g in range(2)]
-        gain_sb = held([P, 2, PACK], F32, "gain_sb")
         phase_sb = {}
         v_w = [[held([P, JW], U32, f"v_w{a}{jh}") for jh in range(2)] for a in range(2)]
         v_s = [held([P, S], U8, f"v_s{a}") for a in range(2)]
@@ -61,17 +54,16 @@ def tile_list_cable_tilt_displacement_kernel(
         cos_b = [[held([P, PACK, JW], F32, f"cos{g}{jh}") for jh in range(2)] for g in range(2)]
         h_c = [[held([P, JW], U32, f"h_c{g}{jh}") for jh in range(2)] for g in range(2)]
         h_s = [[held([P, JW], U8, f"h_s{g}{jh}") for jh in range(2)] for g in range(2)]
-        warm_in = held([P, 8], F32, "warm_in")
-        warm_out = held([P, 8], F32, "warm_out")
+        warm_in = held([P, 8], F32, "warm_in", tag="tab_w0")
+        warm_abs = held([P, 8], F32, "warm_abs", tag="tab_s")
+        warm_out = held([P, 8], F32, "warm_out", tag="tab2_w")
 
         nc.vector.memset(warm_in[:], 0.0)
         nc.scalar.activation(warm_out[:], warm_in[:], ACT.Sin)
-        for plane in (tab2_s, tab_s):
-            nc.vector.memset(plane[:, :T // 2].bitcast(I32), 0)
-            nc.gpsimd.memset(plane[:, T // 2:].bitcast(I32), 0)
-        nc.vector.memset(w1_s[:].bitcast(I32), 0)
-        for plane in (v_s[1], w1p_s[1]):
-            nc.gpsimd.memset(plane[:].bitcast(I32), 0)
+        nc.scalar.activation(warm_abs[:], warm_in[:], ACT.Abs)
+        tab_s = held([P, T], U8, "tab_s")
+        for plane in (tab2_s, v_s[1], w1p_s[1], tab_s):
+            nc.vector.memset(plane[:].bitcast(I32), 0)
 
         def load_two_pass_scales(plane, scales):
             rows = scales.bitcast(I32).rearrange("a (q r) n -> r q a n", r=4)
@@ -88,38 +80,27 @@ def tile_list_cable_tilt_displacement_kernel(
                 phase[g * PASS:(g + 1) * PASS, jh * JW:(jh + 1) * JW].rearrange("(p t) j -> p t j", t=PACK))
 
         def load_tab(a):
+            tab_w[a] = held([P, T], U32, f"tab_w{a}")
             nc.sync.dma_start(tab_w[a][:].bitcast(I32), tab_words[a].rearrange("p t i -> p (t i)").bitcast(I32))
 
         def shift(planes):
             nc.sync.dma_start(planes[1][0:112, :].bitcast(I32), planes[0][16:P, :].bitcast(I32))
 
         nc.sync.dma_start(list2[:], offs2)
-        load_w2(w2_raw0[0], 0)
-        load_w2(w2_raw0[1], PASS // 2)
+        nc.sync.dma_start(list1[:], offs)
+        load_w2(w2_raw0, 0)
         for q in range(4):
             nc.sync.dma_start(tab2_s[32 * q:32 * q + 4, :].bitcast(I32), tab2_scales[0, 4 * q:4 * q + 4, :].bitcast(I32))
+        tab2_w = held([P, T], U16, "tab2_w")
         nc.sync.dma_start(tab2_w[:].bitcast(I32), tab2_words[0].bitcast(I32))
-        nc.sync.dma_start(list1[:], offs)
-        load_w2(w2_raw1, PASS)
-        load_two_pass_scales(tab_s, tab_scales)
         load_tab(0)
-        load_two_pass_scales(w1_s, w1_scales)
-        nc.sync.dma_start(w1_w[:].bitcast(I32), w1_words.bitcast(I32).rearrange("a p n -> p a n"))
-        load_tab(1)
-        nc.sync.dma_start(gain_sb[:], gain.rearrange("(g p t) -> p g t", g=2, t=PACK))
+        load_two_pass_scales(tab_s, tab_scales)
+
 
         def half(lst, jh):
             return lst[:, jh * (JW // 16):(jh + 1) * (JW // 16)]
 
-        def cast_w2(g, raw, m0):
-            nc.scalar.copy(
-                w2_bf[g][:].rearrange("p (t m i) -> p m i t", t=PACK, i=PACK)[:, m0:m0 + raw.shape[2] // PACK],
-                raw[:].rearrange("p i (m t) -> p m i t", t=PACK))
-
-        def quantise_w2(g):
-            nc.vector.quantize_mx(w2_c[g][:].bitcast(FP8X4), w2_s[g][:], w2_bf[g][:])
-
-        def cosines(g, jh, by_half_angle=False):
+        def cosines(g, jh):
             abs_b = cos_b[g][jh]
             for t in range(PACK):
                 cols = slice(t * P, (t + 1) * P)
@@ -127,12 +108,8 @@ def tile_list_cable_tilt_displacement_kernel(
                 nc.tensor.matmul_mx(
                     bank[:], lhsT=w2_c[g][:, cols].bitcast(FP8X4), lhsT_scale=w2_s[g][:, cols],
                     rhs=v2_w[jh][:].bitcast(FP4X4), rhs_scale=v2_s[jh][:], start=True, stop=True)
-                if by_half_angle:
-                    nc.scalar.activation(sin_h[:, t, :], bank[:], ACT.Sin, scale=0.5)
-                else:
-                    nc.scalar.activation(abs_b[:, t, :], bank[:], ACT.Abs)
-            if not by_half_angle:
-                nc.scalar.activation(cos_b[g][jh][:], abs_b[:], ACT.Sin, bias=math.pi / 2, scale=-1.0)
+                nc.scalar.activation(abs_b[:, t, :], bank[:], ACT.Abs)
+            nc.scalar.activation(cos_b[g][jh][:], abs_b[:], ACT.Sin, bias=math.pi / 2, scale=-1.0)
 
         def strain_angles(g, jh, t):
             bank = psum.tile([P, JW], F32, name="a_bank", bufs=4)
@@ -178,61 +155,74 @@ def tile_list_cable_tilt_displacement_kernel(
                         bank[:], lhsT=w3_w[:, g, cols].bitcast(FP8X4), lhsT_scale=w3_s[:, g, cols],
                         rhs=h_c[g][jh][:, js].bitcast(FP8X4), rhs_scale=h_s[g][jh][:, js],
                         start=(g == 0), stop=(g == 1))
-                res = ring.tile([P, width], F32, name="res", bufs=4)
+                res = held([P, width], F32, f"res{jh}{js.start}{c}")
                 if share and c % 2 == 1:
                     nc.vector.tensor_copy(res[:], bank[:])
                 else:
                     nc.scalar.copy(res[:], bank[:])
                 nc.sync.dma_start(out[cols, jh * JW + js.start:jh * JW + js.stop], res[:])
 
-        cast_w2(0, w2_raw0[0], 0)
-        cast_w2(0, w2_raw0[1], P // 2)
+        for u in range(2):
+            nc.scalar.copy(
+                w2_bf0[u][:].rearrange("p (t m i) -> p m i t", t=2, i=PACK),
+                w2_raw0[:].rearrange("p i (m t) -> p m i t", t=PACK)[:, :, :, 2 * u:2 * u + 2])
+        w1_s = held([P, H], U8, "w1_s", tag="w2_raw0")
+        nc.gpsimd.memset(w1_s[:].bitcast(I32), 0)
+        load_two_pass_scales(w1_s, w1_scales)
         nc.vector.tensor_copy(v2_s[0][:], tab2_s[:].indirect(half(list2, 0)))
-        quantise_w2(0)
-        nc.vector.tensor_copy(v2_w[0][:], tab2_w[:].indirect(half(list2, 0)))
         nc.vector.tensor_copy(v2_s[1][:], tab2_s[:].indirect(half(list2, 1)))
+        w2_c[0] = held([P, PASS], U32, "w2_c0", tag="tab2_s")
+        for u in range(2):
+            cols = slice(u * 2 * P, (u + 1) * 2 * P)
+            nc.vector.quantize_mx(w2_c[0][:, cols].bitcast(FP8X4), w2_s[0][:, cols], w2_bf0[u][:])
+        w1_w = held([P, 2, H], U16, "w1_w")
+        nc.sync.dma_start(w1_w[:].bitcast(I32), w1_words.bitcast(I32).rearrange("a p n -> p a n"))
+        load_tab(1)
+        nc.vector.tensor_copy(v2_w[0][:], tab2_w[:].indirect(half(list2, 0)))
         nc.vector.tensor_copy(v2_w[1][:], tab2_w[:].indirect(half(list2, 1)))
+        gain_sb = held([P, 2, PACK], F32, "gain_sb", tag="tab2_w")
+        nc.sync.dma_start(gain_sb[:], gain.rearrange("(g p t) -> p g t", g=2, t=PACK))
+        nc.vector.tensor_copy(v_w[0][0][:], tab_w[0][:].indirect(half(list1, 0)))
         nc.vector.tensor_copy(v_s[0][:], tab_s[:].indirect(list1[:]))
         shift(v_s)
-        cosines(0, 0)
-        cosines(0, 1, by_half_angle=True)
-        cast_w2(1, w2_raw1, 0)
-        quantise_w2(1)
-        nc.vector.tensor_copy(v_w[0][0][:], tab_w[0][:].indirect(half(list1, 0)))
         nc.vector.tensor_copy(
             w1p_s[0][:].rearrange("p (g t m) -> p g t m", g=2, t=PACK),
             w1_s[:].rearrange("p (g m t) -> p g t m", g=2, t=PACK))
         shift(w1p_s)
+        w2_raw1 = held([P, PACK, PASS], F32, "w2_raw1", tag="w2_raw0")
+        load_w2(w2_raw1, PASS)
+        cosines(0, 0)
+        cosines(0, 1)
         for g in range(2):
             nc.vector.tensor_copy(
                 w1p_w[g][:].rearrange("p a (t m) -> p a t m", t=PACK),
                 w1_w[:, :, g * PASS:(g + 1) * PASS].rearrange("p a (m t) -> p a t m", t=PACK))
         nc.vector.tensor_copy(v_w[0][1][:], tab_w[0][:].indirect(half(list1, 1)))
-        nc.vector.tensor_scalar_mul(gain_m2[:], gain_sb[:, 0, :], -2.0)
-        for t in range(PACK):
-            nc.vector.scalar_tensor_tensor(
-                cos_b[0][1][:, t, :], sin_h[:, t, :], gain_m2[:, t:t + 1], sin_h[:, t, :], ALU.mult, ALU.mult)
-        cosines(1, 0)
         nc.vector.tensor_copy(v_w[1][0][:], tab_w[1][:].indirect(half(list1, 0)))
         nc.vector.tensor_copy(v_w[1][1][:], tab_w[1][:].indirect(half(list1, 1)))
 
-        load_phase(0, 0, held([P, PACK, JW], F32, "phase00", tag="w1_s")[:])
+        load_phase(0, 0, held([P, PACK, JW], F32, "phase00", tag="w1_w")[:])
         phase_pair = held([P, 2, PACK, JW], F32, "phase_pair", tag="tab_w0")
         load_phase(0, 1, phase_pair[:, 0])
         load_phase(1, 0, phase_pair[:, 1])
-        w3_w = held([P, 2, N], U32, "w3_w", tag="w1_w")
+        load_phase(1, 1, held([P, PACK, JW], F32, "phase11", tag="tab_w1")[:])
+
+        prod = products(0, 0)
+        nc.vector.tensor_copy(
+            w2_bf1[:].rearrange("p (t m i) -> p m i t", t=PACK, i=PACK),
+            w2_raw1[:].rearrange("p i (m t) -> p m i t", t=PACK))
+        h00 = add_phase(0, 0, prod)
+        nc.vector.quantize_mx(w2_c[1][:].bitcast(FP8X4), w2_s[1][:], w2_bf1[:])
+        w3_w = held([P, 2, N], U32, "w3_w", tag="w2_raw0")
         nc.sync.dma_start(w3_w[:].bitcast(I32), w3_words.rearrange("a p c i -> p a (c i)").bitcast(I32))
-        w3_s = held([P, 2, N], U8, "w3_s", tag="tab_s")
-        nc.gpsimd.memset(w3_s[:].rearrange("p a n -> p (a n)").bitcast(I32), 0)
+        w3_s = held([P, 2, N], U8, "w3_s", tag="w2_bf1")
+        nc.vector.memset(w3_s[:].rearrange("p a n -> p (a n)").bitcast(I32), 0)
         for q in range(4):
             nc.sync.dma_start(
                 w3_s[32 * q:32 * q + 4, :, :].bitcast(I32),
                 w3_scales[:, 4 * q:4 * q + 4, :].bitcast(I32).rearrange("a r n -> r a n"))
-        load_phase(1, 1, held([P, PACK, JW], F32, "phase11", tag="tab_w1")[:])
-
-        prod = products(0, 0)
-        h00 = add_phase(0, 0, prod)
-        prod = products(0, 1, first_op=ALU.add)
+        prod = products(0, 1)
+        cosines(1, 0)
         quantise_h(0, 0, h00)
         h01 = add_phase(0, 1, prod)
         prod = products(1, 0)

@@ -35,40 +35,50 @@ def tile_list_cable_tilt_displacement_kernel(
         def held(shape, dtype, name, tag=None):
             return keep.tile(shape, dtype, name=name, tag=tag or name, align_bytes=64)
 
+        shared = ctx.enter_context(tc.tile_pool(name="shared", bufs=1))
+
+        def placed(shape, dtype, name, offset):
+            return shared.tile(shape, dtype, name=name, align_bytes=64, offset=offset)
+
+        kib = 1024
+        at_tab1, at_w1s, at_tab2s, at_tabs = 8 * kib, 38 * kib, 52 * kib, 58 * kib
+        at_tab2w = 1 * kib
         list1 = keep.tile([P, S // 16], U16, name="list1")
         list2 = keep.tile([P, S // 16], U16, name="list2")
-        tab_w = {}
-        tab2_s = held([P, T], U8, "tab2_s")
+        tab2_s = placed([P, T], U8, "tab2_s", at_tab2s)
+        w2_raw0 = held([P, PACK, PASS], F32, "w2_raw0", tag="slot_e")
+        w2_bf0 = {0: placed([P, PASS * 2], BF16, "w2_bf00", at_w1s)}
         w1p_w = [held([P, 2, PASS], U16, f"w1p_w{g}") for g in range(2)]
         w1p_s = [held([P, H], U8, f"w1p_s{a}") for a in range(2)]
-        w2_raw0 = held([P, PACK, PASS], F32, "w2_raw0")
-        w2_bf0 = [held([P, PASS * 2], BF16, f"w2_bf0{u}", tag=("w1_w", "tab_w1")[u]) for u in range(2)]
-        w2_bf1 = held([P, PASS * PACK], BF16, "w2_bf1")
-        w2_c = {1: held([P, PASS], U32, "w2_c1")}
+        w2_c = {}
+        w2_c1 = held([P, PASS], U32, "w2_c1")
+        w2_c[1, 0], w2_c[1, 1] = w2_c1[:, 0:2 * P], w2_c1[:, 2 * P:PASS]
         w2_s = [held([P, PASS], U8, f"w2_s{g}") for g in range(2)]
-        phase_sb = {}
-        v_w = [[held([P, JW], U32, f"v_w{a}{jh}") for jh in range(2)] for a in range(2)]
-        v_s = [held([P, S], U8, f"v_s{a}") for a in range(2)]
-        v2_w = [held([P, JW], U16, f"v2_w{jh}") for jh in range(2)]
-        v2_s = [held([P, JW], U8, f"v2_s{jh}") for jh in range(2)]
-        cos_b = [[held([P, PACK, JW], F32, f"cos{g}{jh}") for jh in range(2)] for g in range(2)]
+        v_w1 = [held([P, JW], U32, f"v_w1{jh}") for jh in range(2)]
+        v_s = {1: held([P, S], U8, "v_s1")}
+        v2_w = {0: held([P, JW], U16, "v2_w0")}
+        v2_s = held([P, S], U8, "v2_s")
+        cos_b = {}
+        magn = {}
         h_c = [[held([P, JW], U32, f"h_c{g}{jh}") for jh in range(2)] for g in range(2)]
         h_s = [[held([P, JW], U8, f"h_s{g}{jh}") for jh in range(2)] for g in range(2)]
-        warm_in = held([P, 8], F32, "warm_in", tag="tab_w0")
-        warm_abs = held([P, 8], F32, "warm_abs", tag="tab_s")
-        warm_out = held([P, 8], F32, "warm_out", tag="tab2_w")
+        warm_in = placed([P, 8], F32, "warm_in", at_tab2w)
+        warm_bias = placed([P, 1], F32, "warm_bias", at_tabs)
+        warm_out = held([P, 8], F32, "warm_out", tag="slot_b")
+        phase_sb = {}
 
+        nc.vector.memset(tab2_s[:].bitcast(I32), 0)
         nc.vector.memset(warm_in[:], 0.0)
-        nc.scalar.activation(warm_out[:], warm_in[:], ACT.Sin)
-        nc.scalar.activation(warm_abs[:], warm_in[:], ACT.Abs)
-        tab_s = held([P, T], U8, "tab_s")
-        for plane in (tab2_s, v_s[1], w1p_s[1], tab_s):
+        nc.vector.memset(warm_bias[:], 0.0)
+        nc.scalar.activation(warm_out[:], warm_in[:], ACT.Sin, bias=warm_bias[:])
+        tab_s = placed([P, T], U8, "tab_s", at_tabs)
+        for plane in (tab_s, v_s[1], w1p_s[1]):
             nc.vector.memset(plane[:].bitcast(I32), 0)
 
-        def load_two_pass_scales(plane, scales):
+        def load_two_pass_scales(plane, scales, queue):
             rows = scales.bitcast(I32).rearrange("a (q r) n -> r q a n", r=4)
             for r in range(4):
-                nc.sync.dma_start(plane[r:P:16, :].bitcast(I32), rows[r])
+                queue.dma_start(plane[r:P:16, :].bitcast(I32), rows[r])
 
         def load_w2(raw, c0):
             nc.sync.dma_start(raw[:], w2[:, c0:c0 + raw.shape[2]].rearrange("(p i) c -> p i c", i=PACK))
@@ -79,62 +89,53 @@ def tile_list_cable_tilt_displacement_kernel(
                 dst,
                 phase[g * PASS:(g + 1) * PASS, jh * JW:(jh + 1) * JW].rearrange("(p t) j -> p t j", t=PACK))
 
-        def load_tab(a):
-            tab_w[a] = held([P, T], U32, f"tab_w{a}")
-            nc.sync.dma_start(tab_w[a][:].bitcast(I32), tab_words[a].rearrange("p t i -> p (t i)").bitcast(I32))
+        def load_tab(a, tile):
+            nc.sync.dma_start(tile[:].bitcast(I32), tab_words[a].rearrange("p t i -> p (t i)").bitcast(I32))
 
         def shift(planes):
             nc.sync.dma_start(planes[1][0:112, :].bitcast(I32), planes[0][16:P, :].bitcast(I32))
 
-        nc.sync.dma_start(list2[:], offs2)
-        nc.sync.dma_start(list1[:], offs)
-        load_w2(w2_raw0, 0)
-        for q in range(4):
-            nc.sync.dma_start(tab2_s[32 * q:32 * q + 4, :].bitcast(I32), tab2_scales[0, 4 * q:4 * q + 4, :].bitcast(I32))
-        tab2_w = held([P, T], U16, "tab2_w")
-        nc.sync.dma_start(tab2_w[:].bitcast(I32), tab2_words[0].bitcast(I32))
-        load_tab(0)
-        load_two_pass_scales(tab_s, tab_scales)
-
-
         def half(lst, jh):
             return lst[:, jh * (JW // 16):(jh + 1) * (JW // 16)]
 
-        def cosines(g, jh):
-            abs_b = cos_b[g][jh]
+        def events(jh):
+            return slice(jh * JW, (jh + 1) * JW)
+
+        def magnitudes(g, jh):
+            abs_b = ring.tile([P, PACK, JW], F32, name="abs_b", bufs=1)
+            magn[g, jh] = abs_b
             for t in range(PACK):
                 cols = slice(t * P, (t + 1) * P)
-                bank = psum.tile([P, JW], F32, name="b_bank", bufs=2)
+                bank = psum.tile([P, JW], F32, name="bo_bank", bufs=4)
                 nc.tensor.matmul_mx(
-                    bank[:], lhsT=w2_c[g][:, cols].bitcast(FP8X4), lhsT_scale=w2_s[g][:, cols],
-                    rhs=v2_w[jh][:].bitcast(FP4X4), rhs_scale=v2_s[jh][:], start=True, stop=True)
+                    bank[:], lhsT=w2_c[g, t // 2][:, t % 2 * P:(t % 2 + 1) * P].bitcast(FP8X4), lhsT_scale=w2_s[g][:, cols],
+                    rhs=v2_w[jh][:].bitcast(FP4X4), rhs_scale=v2_s[:, events(jh)], start=True, stop=True)
                 nc.scalar.activation(abs_b[:, t, :], bank[:], ACT.Abs)
-            nc.scalar.activation(cos_b[g][jh][:], abs_b[:], ACT.Sin, bias=math.pi / 2, scale=-1.0)
 
-        def strain_angles(g, jh, t):
-            bank = psum.tile([P, JW], F32, name="a_bank", bufs=4)
-            cols = slice(t * P, (t + 1) * P)
-            scols = slice(g * PASS + t * P, g * PASS + (t + 1) * P)
-            for a in range(2):
-                nc.tensor.matmul_mx(
-                    bank[:], lhsT=w1p_w[g][:, a, cols].bitcast(FP4X4), lhsT_scale=w1p_s[a][:, scols],
-                    rhs=v_w[a][jh][:].bitcast(FP8X4), rhs_scale=v_s[a][:, jh * JW:(jh + 1) * JW],
-                    start=(a == 0), stop=(a == 1))
-            return bank
+        def cosines(g, jh):
+            cos_b[g, jh] = ring.tile([P, PACK, JW], F32, name="cos_b", bufs=2)
+            nc.scalar.activation(cos_b[g, jh][:], magn[g, jh][:], ACT.Sin, bias=math.pi / 2, scale=-1.0)
 
-        def sine_times_cosine(g, jh, t, bank, js, sin_a, prod, first_op):
-            nc.scalar.activation(sin_a[:, t, js], bank[:, js], ACT.Sin)
-            nc.vector.scalar_tensor_tensor(
-                prod[:, t, js], cos_b[g][jh][:, t, js], gain_sb[:, g, t:t + 1], sin_a[:, t, js], first_op, ALU.mult)
-
-        def products(g, jh, first_op=ALU.mult):
-            sin_a = ring.tile([P, PACK, JW], F32, name="sin_a")
-            prod = ring.tile([P, PACK, JW], F32, name="prod")
+        def sines(g, jh):
+            sin_a = ring.tile([P, PACK, JW], F32, name="sin_a", bufs=3)
             for t in range(PACK):
-                sine_times_cosine(g, jh, t, strain_angles(g, jh, t), slice(0, JW), sin_a, prod, first_op)
-            return prod
+                bank = psum.tile([P, JW], F32, name="a_bank", bufs=4)
+                cols = slice(t * P, (t + 1) * P)
+                scols = slice(g * PASS + t * P, g * PASS + (t + 1) * P)
+                for a in range(2):
+                    codes = v_w0[:, events(jh)] if a == 0 else v_w1[jh][:]
+                    nc.tensor.matmul_mx(
+                        bank[:], lhsT=w1p_w[g][:, a, cols].bitcast(FP4X4), lhsT_scale=w1p_s[a][:, scols],
+                        rhs=codes.bitcast(FP8X4), rhs_scale=v_s[a][:, events(jh)],
+                        start=(a == 0), stop=(a == 1))
+                nc.scalar.activation(sin_a[:, t, :], bank[:], ACT.Sin)
+            return sin_a
 
-        def add_phase(g, jh, prod, js=slice(0, JW)):
+        def product(g, jh, t, js, sin_a, prod):
+            nc.vector.scalar_tensor_tensor(
+                prod[:, t, js], cos_b[g, jh][:, t, js], gain_sb[:, g, t:t + 1], sin_a[:, t, js], ALU.mult, ALU.mult)
+
+        def add_phase(g, jh, prod, js):
             h_bf = ring.tile([P, (js.stop - js.start) * PACK], BF16, name="h_bf", align_bytes=64)
             nc.vector.tensor_tensor(
                 h_bf[:].rearrange("p (c i t) -> p c t i", i=2, t=PACK),
@@ -142,109 +143,139 @@ def tile_list_cable_tilt_displacement_kernel(
                 phase_sb[g, jh][:, :, js].rearrange("p t (c i) -> p c t i", i=2), ALU.add)
             return h_bf
 
-        def quantise_h(g, jh, h_bf, js=slice(0, JW)):
+        def quantise_h(g, jh, h_bf, js):
             nc.vector.quantize_mx(h_c[g][jh][:, js].bitcast(FP8X4), h_s[g][jh][:, js], h_bf[:])
 
-        def last_product(jh, js=slice(0, JW), share=False):
-            width = js.stop - js.start
-            for c in range(N // P):
-                cols = slice(c * P, (c + 1) * P)
-                bank = psum.tile([P, width], F32, name="o_bank", bufs=2)
-                for g in range(2):
-                    nc.tensor.matmul_mx(
-                        bank[:], lhsT=w3_w[:, g, cols].bitcast(FP8X4), lhsT_scale=w3_s[:, g, cols],
-                        rhs=h_c[g][jh][:, js].bitcast(FP8X4), rhs_scale=h_s[g][jh][:, js],
-                        start=(g == 0), stop=(g == 1))
-                res = held([P, width], F32, f"res{jh}{js.start}{c}")
-                if share and c % 2 == 1:
-                    nc.vector.tensor_copy(res[:], bank[:])
-                else:
-                    nc.scalar.copy(res[:], bank[:])
-                nc.sync.dma_start(out[cols, jh * JW + js.start:jh * JW + js.stop], res[:])
+        def last_pass(dst, c, g, jh, js, start, stop):
+            cols = slice(c * P, (c + 1) * P)
+            nc.tensor.matmul_mx(
+                dst, lhsT=w3_w[:, g, cols].bitcast(FP8X4), lhsT_scale=w3_s[:, g, cols],
+                rhs=h_c[g][jh][:, js].bitcast(FP8X4), rhs_scale=h_s[g][jh][:, js], start=start, stop=stop)
 
-        for u in range(2):
+        def open_banks(jh, js):
+            width = js.stop - js.start
+            per = JW // width
+            banks = []
+            for c0 in range(0, N // P, per):
+                bank = psum.tile([P, per, width], F32, name="bo_bank", bufs=4)
+                for k in range(per):
+                    last_pass(bank[:, k, :], c0 + k, 0, jh, js, k == 0, False)
+                banks.append(bank)
+            return banks
+
+        def close_banks(banks, jh, js, engines):
+            width = js.stop - js.start
+            per = JW // width
+            for n, bank in enumerate(banks):
+                for k in range(per):
+                    last_pass(bank[:, k, :], n * per + k, 1, jh, js, False, k == per - 1)
+                res = held([P, per, width], F32, f"res{jh}{js.start}{n}")
+                engines[n % len(engines)](res[:], bank[:])
+                rows = out[n * per * P:(n + 1) * per * P, jh * JW + js.start:jh * JW + js.stop]
+                nc.sync.dma_start(rows.rearrange("(c p) j -> p c j", p=P), res[:])
+
+        nc.sync.dma_start(list2[:], offs2)
+        nc.sync.dma_start(list1[:], offs)
+        load_w2(w2_raw0, 0)
+        for q in range(4):
+            nc.sync.dma_start(tab2_s[32 * q:32 * q + 4, :].bitcast(I32), tab2_scales[0, 4 * q:4 * q + 4, :].bitcast(I32))
+        tab2_w = placed([P, T], U16, "tab2_w", at_tab2w)
+        nc.sync.dma_start(tab2_w[:].bitcast(I32), tab2_words[0].bitcast(I32))
+        tab_w0 = held([P, T], U32, "tab_w0", tag="slot_b")
+        load_tab(0, tab_w0)
+        load_two_pass_scales(tab_s, tab_scales, nc.scalar)
+
+        def round_first_half(u):
             nc.scalar.copy(
                 w2_bf0[u][:].rearrange("p (t m i) -> p m i t", t=2, i=PACK),
                 w2_raw0[:].rearrange("p i (m t) -> p m i t", t=PACK)[:, :, :, 2 * u:2 * u + 2])
-        w1_s = held([P, H], U8, "w1_s", tag="w2_raw0")
-        nc.gpsimd.memset(w1_s[:].bitcast(I32), 0)
-        load_two_pass_scales(w1_s, w1_scales)
-        nc.vector.tensor_copy(v2_s[0][:], tab2_s[:].indirect(half(list2, 0)))
-        nc.vector.tensor_copy(v2_s[1][:], tab2_s[:].indirect(half(list2, 1)))
-        w2_c[0] = held([P, PASS], U32, "w2_c0", tag="tab2_s")
-        for u in range(2):
-            cols = slice(u * 2 * P, (u + 1) * 2 * P)
-            nc.vector.quantize_mx(w2_c[0][:, cols].bitcast(FP8X4), w2_s[0][:, cols], w2_bf0[u][:])
-        w1_w = held([P, 2, H], U16, "w1_w")
-        nc.sync.dma_start(w1_w[:].bitcast(I32), w1_words.bitcast(I32).rearrange("a p n -> p a n"))
-        load_tab(1)
+
+        w2_bf0[1] = held([P, PASS * 2], BF16, "w2_bf01")
+        round_first_half(0)
+        round_first_half(1)
+        nc.vector.tensor_copy(v2_s[:], tab2_s[:].indirect(list2[:]))
+        w2_c[0, 0] = placed([P, 2 * P], U32, "w2_c00", at_tab2s + 64)
+        w2_raw1 = held([P, PACK, PASS], F32, "w2_raw1", tag="slot_e")
+        load_w2(w2_raw1, PASS)
         nc.vector.tensor_copy(v2_w[0][:], tab2_w[:].indirect(half(list2, 0)))
+        nc.vector.quantize_mx(w2_c[0, 0][:].bitcast(FP8X4), w2_s[0][:, 0:2 * P], w2_bf0[0][:])
+        v2_w[1] = held([P, JW], U16, "v2_w1")
+        w1_w = placed([P, 2, H], U16, "w1_w", at_tab2s - 4 * kib + 64)
+        nc.sync.dma_start(w1_w[:].bitcast(I32), w1_words.bitcast(I32).rearrange("a p n -> p a n"))
+        w1_s = placed([P, H], U8, "w1_s", at_w1s)
+        nc.vector.memset(w1_s[:].bitcast(I32), 0)
+        load_two_pass_scales(w1_s, w1_scales, nc.sync)
         nc.vector.tensor_copy(v2_w[1][:], tab2_w[:].indirect(half(list2, 1)))
-        gain_sb = held([P, 2, PACK], F32, "gain_sb", tag="tab2_w")
-        nc.sync.dma_start(gain_sb[:], gain.rearrange("(g p t) -> p g t", g=2, t=PACK))
-        nc.vector.tensor_copy(v_w[0][0][:], tab_w[0][:].indirect(half(list1, 0)))
+        w2_c[0, 1] = placed([P, 2 * P], U32, "w2_c01", at_tab2w + kib)
+        nc.vector.quantize_mx(w2_c[0, 1][:].bitcast(FP8X4), w2_s[0][:, 2 * P:PASS], w2_bf0[1][:])
+        tab_w1 = placed([P, T], U32, "tab_w1", at_tab1)
+        load_tab(1, tab_w1)
+        for jh in range(2):
+            magnitudes(0, jh)
+            cosines(0, jh)
+        v_s[0] = placed([P, S], U8, "v_s0", at_tab2w)
         nc.vector.tensor_copy(v_s[0][:], tab_s[:].indirect(list1[:]))
         shift(v_s)
+        v_w0 = placed([P, S], U32, "v_w0", at_tabs)
+        nc.vector.tensor_copy(v_w0[:], tab_w0[:].indirect(list1[:]))
+        gain_sb = held([P, 2, PACK], F32, "gain_sb", tag="slot_b")
+        nc.sync.dma_start(gain_sb[:], gain.rearrange("(g p t) -> p g t", g=2, t=PACK))
         nc.vector.tensor_copy(
             w1p_s[0][:].rearrange("p (g t m) -> p g t m", g=2, t=PACK),
             w1_s[:].rearrange("p (g m t) -> p g t m", g=2, t=PACK))
         shift(w1p_s)
-        w2_raw1 = held([P, PACK, PASS], F32, "w2_raw1", tag="w2_raw0")
-        load_w2(w2_raw1, PASS)
-        cosines(0, 0)
-        cosines(0, 1)
+        load_phase(0, 0, placed([P, PACK, JW], F32, "phase00", at_w1s + 512 - 8192)[:])
+        load_phase(0, 1, placed([P, PACK, JW], F32, "phase01", at_w1s + 512)[:])
+        w2_bf1 = held([P, PASS * PACK], BF16, "w2_bf1")
+        nc.vector.tensor_copy(
+            w2_bf1[:].rearrange("p (t m i) -> p m i t", t=PACK, i=PACK),
+            w2_raw1[:].rearrange("p i (m t) -> p m i t", t=PACK))
+        nc.vector.quantize_mx(w2_c1[:].bitcast(FP8X4), w2_s[1][:], w2_bf1[:])
+        magnitudes(1, 0)
         for g in range(2):
             nc.vector.tensor_copy(
                 w1p_w[g][:].rearrange("p a (t m) -> p a t m", t=PACK),
                 w1_w[:, :, g * PASS:(g + 1) * PASS].rearrange("p a (m t) -> p a t m", t=PACK))
-        nc.vector.tensor_copy(v_w[0][1][:], tab_w[0][:].indirect(half(list1, 1)))
-        nc.vector.tensor_copy(v_w[1][0][:], tab_w[1][:].indirect(half(list1, 0)))
-        nc.vector.tensor_copy(v_w[1][1][:], tab_w[1][:].indirect(half(list1, 1)))
-
-        load_phase(0, 0, held([P, PACK, JW], F32, "phase00", tag="w1_w")[:])
-        phase_pair = held([P, 2, PACK, JW], F32, "phase_pair", tag="tab_w0")
-        load_phase(0, 1, phase_pair[:, 0])
-        load_phase(1, 0, phase_pair[:, 1])
-        load_phase(1, 1, held([P, PACK, JW], F32, "phase11", tag="tab_w1")[:])
-
-        prod = products(0, 0)
-        nc.vector.tensor_copy(
-            w2_bf1[:].rearrange("p (t m i) -> p m i t", t=PACK, i=PACK),
-            w2_raw1[:].rearrange("p i (m t) -> p m i t", t=PACK))
-        h00 = add_phase(0, 0, prod)
-        nc.vector.quantize_mx(w2_c[1][:].bitcast(FP8X4), w2_s[1][:], w2_bf1[:])
-        w3_w = held([P, 2, N], U32, "w3_w", tag="w2_raw0")
+        for jh in range(2):
+            nc.vector.tensor_copy(v_w1[jh][:], tab_w1[:].indirect(half(list1, jh)))
+        for jh in range(2):
+            load_phase(1, jh, placed([P, PACK, JW], F32, f"phase1{jh}", at_tab1 + 4608 + 8192 * jh)[:])
+        w3_w = placed([P, 2, N], U32, "w3_w", at_tab1 + 512)
         nc.sync.dma_start(w3_w[:].bitcast(I32), w3_words.rearrange("a p c i -> p a (c i)").bitcast(I32))
-        w3_s = held([P, 2, N], U8, "w3_s", tag="w2_bf1")
+        w3_s = placed([P, 2, N], U8, "w3_s", at_tab1 - 512)
         nc.vector.memset(w3_s[:].rearrange("p a n -> p (a n)").bitcast(I32), 0)
         for q in range(4):
             nc.sync.dma_start(
                 w3_s[32 * q:32 * q + 4, :, :].bitcast(I32),
                 w3_scales[:, 4 * q:4 * q + 4, :].bitcast(I32).rearrange("a r n -> r a n"))
-        prod = products(0, 1)
-        cosines(1, 0)
-        quantise_h(0, 0, h00)
-        h01 = add_phase(0, 1, prod)
-        prod = products(1, 0)
+
+
+        whole = slice(0, JW)
+        pending = None
+        for g, jh in ((0, 0), (0, 1), (1, 0)):
+            if g == 1:
+                cosines(g, jh)
+            sin_a = sines(g, jh)
+            prod = ring.tile([P, PACK, JW], F32, name="prod")
+            for t in range(PACK):
+                product(g, jh, t, whole, sin_a, prod)
+                if t == 0 and pending is not None:
+                    quantise_h(*pending)
+            pending = (g, jh, add_phase(g, jh, prod, whole), whole)
+        magnitudes(1, 1)
         cosines(1, 1)
-        quantise_h(0, 1, h01)
-        h10 = add_phase(1, 0, prod)
-        halves = [slice(0, JW // 2), slice(JW // 2, JW)]
-        sin_a = ring.tile([P, PACK, JW], F32, name="sin_a")
+        sin_a = sines(1, 1)
         prod = ring.tile([P, PACK, JW], F32, name="prod")
-        banks = []
-        for t in range(PACK):
-            banks.append(strain_angles(1, 1, t))
-            sine_times_cosine(1, 1, t, banks[t], halves[0], sin_a, prod, ALU.mult)
-            if t == 0:
-                quantise_h(1, 0, h10)
-        h11a = add_phase(1, 1, prod, halves[0])
-        for t in range(PACK):
-            sine_times_cosine(1, 1, t, banks[t], halves[1], sin_a, prod, ALU.mult)
-            if t == 0:
-                quantise_h(1, 1, h11a, halves[0])
-        last_product(0)
-        h11b = add_phase(1, 1, prod, halves[1])
-        quantise_h(1, 1, h11b, halves[1])
-        last_product(1, halves[0])
-        last_product(1, halves[1], share=True)
+        halves = [slice(0, JW // 2), slice(JW // 2, JW)]
+        for js in halves:
+            for t in range(PACK):
+                product(1, 1, t, js, sin_a, prod)
+                if t == 0:
+                    quantise_h(*pending)
+            if js.start == 0:
+                close_banks(open_banks(0, whole), 0, whole, [nc.scalar.copy])
+            pending = (1, 1, add_phase(1, 1, prod, js), js)
+        banks = [open_banks(1, js) for js in halves]
+        close_banks(banks[0], 1, halves[0], [nc.scalar.copy])
+        quantise_h(*pending)
+        close_banks(banks[1], 1, halves[1], [nc.scalar.copy, nc.vector.tensor_copy])

@@ -138,9 +138,9 @@ def tile_list_cable_tilt_displacement_kernel(
         def add_phase(g, jh, prod, js):
             h_bf = ring.tile([P, (js.stop - js.start) * PACK], BF16, name="h_bf", align_bytes=64)
             nc.vector.tensor_tensor(
-                h_bf[:].rearrange("p (c i t) -> p c t i", i=2, t=PACK),
-                prod[:, :, js].rearrange("p t (c i) -> p c t i", i=2),
-                phase_sb[g, jh][:, :, js].rearrange("p t (c i) -> p c t i", i=2), ALU.add)
+                h_bf[:].rearrange("p (c i t) -> p c t i", i=4, t=PACK),
+                prod[:, :, js].rearrange("p t (c i) -> p c t i", i=4),
+                phase_sb[g, jh][:, :, js].rearrange("p t (c i) -> p c t i", i=4), ALU.add)
             return h_bf
 
         def quantise_h(g, jh, h_bf, js):

@@ -41,37 +41,39 @@ def tile_list_cable_tilt_displacement_kernel(
             return shared.tile(shape, dtype, name=name, align_bytes=64, offset=offset)
 
         kib = 1024
-        at_tab1, at_w1s, at_tab2s, at_tabs = 8 * kib, 38 * kib, 52 * kib, 58 * kib
-        at_tab2w = 1 * kib
+        at_tab2w, at_tab0, at_raw1, at_w1w, at_tab1 = 0, 8 * kib, 24 * kib, 40 * kib, 44 * kib
+        at_tab2s, at_tabs, at_w1s = 60 * kib, 64 * kib, 77 * kib
         list1 = keep.tile([P, S // 16], U16, name="list1")
         list2 = keep.tile([P, S // 16], U16, name="list2")
         tab2_s = placed([P, T], U8, "tab2_s", at_tab2s)
-        w2_raw0 = held([P, PACK, PASS], F32, "w2_raw0", tag="slot_e")
-        w2_bf0 = {0: placed([P, PASS * 2], BF16, "w2_bf00", at_w1s)}
-        w1p_w = [held([P, 2, PASS], U16, f"w1p_w{g}") for g in range(2)]
-        w1p_s = [held([P, H], U8, f"w1p_s{a}") for a in range(2)]
+        tab_s = placed([P, T], U8, "tab_s", at_tabs)
+        w1_s = placed([P, H], U8, "w1_s", at_w1s)
+        w2_raw0 = held([P, PACK, PASS], F32, "w2_raw0")
+        w2_bf0 = [held([P, PASS * 2], BF16, f"w2_bf0{u}") for u in range(2)]
+        w2_bf1 = held([P, PASS * PACK], BF16, "w2_bf1")
+        w1p_w = {}
+        w1p_s = {1: held([P, H], U8, "w1p_s1")}
         w2_c = {}
         w2_c1 = held([P, PASS], U32, "w2_c1")
         w2_c[1, 0], w2_c[1, 1] = w2_c1[:, 0:2 * P], w2_c1[:, 2 * P:PASS]
         w2_s = [held([P, PASS], U8, f"w2_s{g}") for g in range(2)]
         v_w1 = [held([P, JW], U32, f"v_w1{jh}") for jh in range(2)]
         v_s = {1: held([P, S], U8, "v_s1")}
-        v2_w = {0: held([P, JW], U16, "v2_w0")}
+        v2_w = [held([P, JW], U16, f"v2_w{jh}") for jh in range(2)]
         v2_s = held([P, S], U8, "v2_s")
+        gain_sb = held([P, 2, PACK], F32, "gain_sb")
         cos_b = {}
         magn = {}
         h_c = [[held([P, JW], U32, f"h_c{g}{jh}") for jh in range(2)] for g in range(2)]
         h_s = [[held([P, JW], U8, f"h_s{g}{jh}") for jh in range(2)] for g in range(2)]
-        warm_in = placed([P, 8], F32, "warm_in", at_tab2w)
-        warm_bias = placed([P, 1], F32, "warm_bias", at_tabs)
-        warm_out = held([P, 8], F32, "warm_out", tag="slot_b")
+        warm_in = held([P, 8], F32, "warm_in")
+        warm_out = placed([P, (at_tab1 + kib) // 4], F32, "warm_out", 0)
         phase_sb = {}
 
         nc.vector.memset(tab2_s[:].bitcast(I32), 0)
+        nc.vector.memset(w1_s[:].bitcast(I32), 0)
         nc.vector.memset(warm_in[:], 0.0)
-        nc.vector.memset(warm_bias[:], 0.0)
-        nc.scalar.activation(warm_out[:], warm_in[:], ACT.Sin, bias=warm_bias[:])
-        tab_s = placed([P, T], U8, "tab_s", at_tabs)
+        nc.scalar.activation(warm_out[:, 0:8], warm_in[:], ACT.Sin, bias=w1_s[:, 0:4].bitcast(F32))
         for plane in (tab_s, v_s[1], w1p_s[1]):
             nc.vector.memset(plane[:].bitcast(I32), 0)
 
@@ -136,7 +138,7 @@ def tile_list_cable_tilt_displacement_kernel(
                 prod[:, t, js], cos_b[g, jh][:, t, js], gain_sb[:, g, t:t + 1], sin_a[:, t, js], ALU.mult, ALU.mult)
 
         def add_phase(g, jh, prod, js):
-            h_bf = ring.tile([P, (js.stop - js.start) * PACK], BF16, name="h_bf", align_bytes=64)
+            h_bf = ring.tile([P, (js.stop - js.start) * PACK], BF16, name="h_bf", bufs=3, align_bytes=64)
             nc.vector.tensor_tensor(
                 h_bf[:].rearrange("p (c i t) -> p c t i", i=4, t=PACK),
                 prod[:, :, js].rearrange("p t (c i) -> p c t i", i=4),
@@ -152,27 +154,30 @@ def tile_list_cable_tilt_displacement_kernel(
                 dst, lhsT=w3_w[:, g, cols].bitcast(FP8X4), lhsT_scale=w3_s[:, g, cols],
                 rhs=h_c[g][jh][:, js].bitcast(FP8X4), rhs_scale=h_s[g][jh][:, js], start=start, stop=stop)
 
-        def open_banks(jh, js):
-            width = js.stop - js.start
-            per = JW // width
+        def open_banks(jh, js, nrows):
+            per = nrows // P
             banks = []
             for c0 in range(0, N // P, per):
-                bank = psum.tile([P, per, width], F32, name="bo_bank", bufs=4)
+                bank = psum.tile([P, per, js.stop - js.start], F32, name="bo_bank", bufs=4)
                 for k in range(per):
                     last_pass(bank[:, k, :], c0 + k, 0, jh, js, k == 0, False)
                 banks.append(bank)
             return banks
 
-        def close_banks(banks, jh, js, engines):
-            width = js.stop - js.start
-            per = JW // width
+        def close_banks(banks, jh, js, nrows, engines):
+            per = nrows // P
             for n, bank in enumerate(banks):
                 for k in range(per):
                     last_pass(bank[:, k, :], n * per + k, 1, jh, js, False, k == per - 1)
-                res = held([P, per, width], F32, f"res{jh}{js.start}{n}")
+                res = held([P, per, js.stop - js.start], F32, f"res{jh}{js.start}{n}")
                 engines[n % len(engines)](res[:], bank[:])
-                rows = out[n * per * P:(n + 1) * per * P, jh * JW + js.start:jh * JW + js.stop]
-                nc.sync.dma_start(rows.rearrange("(c p) j -> p c j", p=P), res[:])
+                dst = out[n * nrows:(n + 1) * nrows, jh * JW + js.start:jh * JW + js.stop]
+                nc.sync.dma_start(dst.rearrange("(c p) j -> p c j", p=P), res[:])
+
+        def finish(h_bf, js, nrows, engines):
+            banks = open_banks(1, js, nrows)
+            quantise_h(1, 1, h_bf, js)
+            close_banks(banks, 1, js, nrows, engines)
 
         nc.sync.dma_start(list2[:], offs2)
         nc.sync.dma_start(list1[:], offs)
@@ -181,35 +186,29 @@ def tile_list_cable_tilt_displacement_kernel(
             nc.sync.dma_start(tab2_s[32 * q:32 * q + 4, :].bitcast(I32), tab2_scales[0, 4 * q:4 * q + 4, :].bitcast(I32))
         tab2_w = placed([P, T], U16, "tab2_w", at_tab2w)
         nc.sync.dma_start(tab2_w[:].bitcast(I32), tab2_words[0].bitcast(I32))
-        tab_w0 = held([P, T], U32, "tab_w0", tag="slot_b")
+        tab_w0 = placed([P, T], U32, "tab_w0", at_tab0)
         load_tab(0, tab_w0)
-        load_two_pass_scales(tab_s, tab_scales, nc.scalar)
+        load_two_pass_scales(w1_s, w1_scales, nc.sync)
+        w2_raw1 = placed([P, PACK, PASS], F32, "w2_raw1", at_raw1)
+        load_w2(w2_raw1, PASS)
+        w1_w = placed([P, 2, H], U16, "w1_w", at_w1w)
+        nc.sync.dma_start(w1_w[:].bitcast(I32), w1_words.bitcast(I32).rearrange("a p n -> p a n"))
+        tab_w1 = placed([P, T], U32, "tab_w1", at_tab1)
+        load_tab(1, tab_w1)
+        load_two_pass_scales(tab_s, tab_scales, nc.gpsimd)
+        nc.gpsimd.dma_start(gain_sb[:], gain.rearrange("(g p t) -> p g t", g=2, t=PACK))
 
-        def round_first_half(u):
+        for u in range(2):
             nc.scalar.copy(
                 w2_bf0[u][:].rearrange("p (t m i) -> p m i t", t=2, i=PACK),
                 w2_raw0[:].rearrange("p i (m t) -> p m i t", t=PACK)[:, :, :, 2 * u:2 * u + 2])
-
-        w2_bf0[1] = held([P, PASS * 2], BF16, "w2_bf01")
-        round_first_half(0)
-        round_first_half(1)
         nc.vector.tensor_copy(v2_s[:], tab2_s[:].indirect(list2[:]))
-        w2_c[0, 0] = placed([P, 2 * P], U32, "w2_c00", at_tab2s + 64)
-        w2_raw1 = held([P, PACK, PASS], F32, "w2_raw1", tag="slot_e")
-        load_w2(w2_raw1, PASS)
+        w2_c[0, 0] = placed([P, 2 * P], U32, "w2_c00", at_tab2s)
         nc.vector.tensor_copy(v2_w[0][:], tab2_w[:].indirect(half(list2, 0)))
         nc.vector.quantize_mx(w2_c[0, 0][:].bitcast(FP8X4), w2_s[0][:, 0:2 * P], w2_bf0[0][:])
-        v2_w[1] = held([P, JW], U16, "v2_w1")
-        w1_w = placed([P, 2, H], U16, "w1_w", at_tab2s - 4 * kib + 64)
-        nc.sync.dma_start(w1_w[:].bitcast(I32), w1_words.bitcast(I32).rearrange("a p n -> p a n"))
-        w1_s = placed([P, H], U8, "w1_s", at_w1s)
-        nc.vector.memset(w1_s[:].bitcast(I32), 0)
-        load_two_pass_scales(w1_s, w1_scales, nc.sync)
         nc.vector.tensor_copy(v2_w[1][:], tab2_w[:].indirect(half(list2, 1)))
         w2_c[0, 1] = placed([P, 2 * P], U32, "w2_c01", at_tab2w + kib)
         nc.vector.quantize_mx(w2_c[0, 1][:].bitcast(FP8X4), w2_s[0][:, 2 * P:PASS], w2_bf0[1][:])
-        tab_w1 = placed([P, T], U32, "tab_w1", at_tab1)
-        load_tab(1, tab_w1)
         for jh in range(2):
             magnitudes(0, jh)
             cosines(0, jh)
@@ -218,37 +217,35 @@ def tile_list_cable_tilt_displacement_kernel(
         shift(v_s)
         v_w0 = placed([P, S], U32, "v_w0", at_tabs)
         nc.vector.tensor_copy(v_w0[:], tab_w0[:].indirect(list1[:]))
-        gain_sb = held([P, 2, PACK], F32, "gain_sb", tag="slot_b")
-        nc.sync.dma_start(gain_sb[:], gain.rearrange("(g p t) -> p g t", g=2, t=PACK))
+        w1p_s[0] = placed([P, H], U8, "w1p_s0", at_tab0)
         nc.vector.tensor_copy(
             w1p_s[0][:].rearrange("p (g t m) -> p g t m", g=2, t=PACK),
             w1_s[:].rearrange("p (g m t) -> p g t m", g=2, t=PACK))
         shift(w1p_s)
-        load_phase(0, 0, placed([P, PACK, JW], F32, "phase00", at_w1s + 512 - 8192)[:])
+        load_phase(0, 0, placed([P, PACK, JW], F32, "phase00", at_w1s + 512 - 8 * kib)[:])
         load_phase(0, 1, placed([P, PACK, JW], F32, "phase01", at_w1s + 512)[:])
-        w2_bf1 = held([P, PASS * PACK], BF16, "w2_bf1")
         nc.vector.tensor_copy(
             w2_bf1[:].rearrange("p (t m i) -> p m i t", t=PACK, i=PACK),
             w2_raw1[:].rearrange("p i (m t) -> p m i t", t=PACK))
         nc.vector.quantize_mx(w2_c1[:].bitcast(FP8X4), w2_s[1][:], w2_bf1[:])
         magnitudes(1, 0)
+        load_phase(1, 0, placed([P, PACK, JW], F32, "phase10", at_raw1 + 4 * kib)[:])
         for g in range(2):
+            w1p_w[g] = placed([P, 2, PASS], U16, f"w1p_w{g}", at_raw1 + 2 * kib * g)
             nc.vector.tensor_copy(
                 w1p_w[g][:].rearrange("p a (t m) -> p a t m", t=PACK),
                 w1_w[:, :, g * PASS:(g + 1) * PASS].rearrange("p a (m t) -> p a t m", t=PACK))
-        for jh in range(2):
-            nc.vector.tensor_copy(v_w1[jh][:], tab_w1[:].indirect(half(list1, jh)))
-        for jh in range(2):
-            load_phase(1, jh, placed([P, PACK, JW], F32, f"phase1{jh}", at_tab1 + 4608 + 8192 * jh)[:])
-        w3_w = placed([P, 2, N], U32, "w3_w", at_tab1 + 512)
+        w3_w = placed([P, 2, N], U32, "w3_w", at_w1w - 3 * kib)
         nc.sync.dma_start(w3_w[:].bitcast(I32), w3_words.rearrange("a p c i -> p a (c i)").bitcast(I32))
-        w3_s = placed([P, 2, N], U8, "w3_s", at_tab1 - 512)
+        w3_s = placed([P, 2, N], U8, "w3_s", at_w1w + kib)
         nc.vector.memset(w3_s[:].rearrange("p a n -> p (a n)").bitcast(I32), 0)
         for q in range(4):
             nc.sync.dma_start(
                 w3_s[32 * q:32 * q + 4, :, :].bitcast(I32),
                 w3_scales[:, 4 * q:4 * q + 4, :].bitcast(I32).rearrange("a r n -> r a n"))
-
+        for jh in range(2):
+            nc.vector.tensor_copy(v_w1[jh][:], tab_w1[:].indirect(half(list1, jh)))
+        load_phase(1, 1, placed([P, PACK, JW], F32, "phase11", at_tab1)[:])
 
         whole = slice(0, JW)
         pending = None
@@ -266,16 +263,17 @@ def tile_list_cable_tilt_displacement_kernel(
         cosines(1, 1)
         sin_a = sines(1, 1)
         prod = ring.tile([P, PACK, JW], F32, name="prod")
-        halves = [slice(0, JW // 2), slice(JW // 2, JW)]
-        for js in halves:
-            for t in range(PACK):
-                product(1, 1, t, js, sin_a, prod)
-                if t == 0:
-                    quantise_h(*pending)
-            if js.start == 0:
-                close_banks(open_banks(0, whole), 0, whole, [nc.scalar.copy])
-            pending = (1, 1, add_phase(1, 1, prod, js), js)
-        banks = [open_banks(1, js) for js in halves]
-        close_banks(banks[0], 1, halves[0], [nc.scalar.copy])
-        quantise_h(*pending)
-        close_banks(banks[1], 1, halves[1], [nc.scalar.copy, nc.vector.tensor_copy])
+        for t in range(PACK):
+            product(1, 1, t, whole, sin_a, prod)
+            if t == 0:
+                quantise_h(*pending)
+        close_banks(open_banks(0, whole, P), 0, whole, P, [nc.scalar.copy])
+        pieces = [slice(0, JW // 2), slice(JW // 2, 3 * JW // 4), slice(3 * JW // 4, JW)]
+        rows = [2 * P, 4 * P, 2 * P]
+        pending = None
+        for js, nrows in zip(pieces, rows):
+            h_bf = add_phase(1, 1, prod, js)
+            if pending is not None:
+                finish(*pending, [nc.scalar.copy])
+            pending = (h_bf, js, nrows)
+        finish(*pending, [nc.scalar.copy, nc.vector.tensor_copy])

@@ -42,7 +42,7 @@ def tile_list_cable_tilt_displacement_kernel(
 
         kib = 1024
         at_tab2w, at_tab0, at_raw1, at_w1w, at_tab1 = 0, 8 * kib, 24 * kib, 40 * kib, 44 * kib
-        at_tab2s, at_tabs, at_w1s = 60 * kib, 64 * kib, 77 * kib
+        at_tabs, at_tab2s, at_w1s = 58 * kib, 66 * kib, 79 * kib
         list1 = keep.tile([P, S // 16], U16, name="list1")
         list2 = keep.tile([P, S // 16], U16, name="list2")
         tab2_s = placed([P, T], U8, "tab2_s", at_tab2s)
@@ -58,10 +58,9 @@ def tile_list_cable_tilt_displacement_kernel(
         w2_c[1, 0], w2_c[1, 1] = w2_c1[:, 0:2 * P], w2_c1[:, 2 * P:PASS]
         w2_s = [held([P, PASS], U8, f"w2_s{g}") for g in range(2)]
         v_w1 = [held([P, JW], U32, f"v_w1{jh}") for jh in range(2)]
-        v_s = {1: held([P, S], U8, "v_s1")}
+        v_s = [held([P, S], U8, f"v_s{a}") for a in range(2)]
         v2_w = [held([P, JW], U16, f"v2_w{jh}") for jh in range(2)]
         v2_s = held([P, S], U8, "v2_s")
-        gain_sb = held([P, 2, PACK], F32, "gain_sb")
         cos_b = {}
         magn = {}
         h_c = [[held([P, JW], U32, f"h_c{g}{jh}") for jh in range(2)] for g in range(2)]
@@ -74,7 +73,7 @@ def tile_list_cable_tilt_displacement_kernel(
         nc.vector.memset(w1_s[:].bitcast(I32), 0)
         nc.vector.memset(warm_in[:], 0.0)
         nc.scalar.activation(warm_out[:, 0:8], warm_in[:], ACT.Sin, bias=w1_s[:, 0:4].bitcast(F32))
-        for plane in (tab_s, v_s[1], w1p_s[1]):
+        for plane in (tab_s, v_s[0], v_s[1], w1p_s[1]):
             nc.vector.memset(plane[:].bitcast(I32), 0)
 
         def load_two_pass_scales(plane, scales, queue):
@@ -103,10 +102,11 @@ def tile_list_cable_tilt_displacement_kernel(
         def events(jh):
             return slice(jh * JW, (jh + 1) * JW)
 
-        def magnitudes(g, jh):
-            abs_b = ring.tile([P, PACK, JW], F32, name="abs_b", bufs=1)
-            magn[g, jh] = abs_b
-            for t in range(PACK):
+        def magnitudes(g, jh, slices=range(PACK)):
+            if (g, jh) not in magn:
+                magn[g, jh] = held([P, PACK, JW], F32, f"abs_b{g}{jh}", tag="abs_01" if (g, jh) == (0, 1) else "abs_b")
+            abs_b = magn[g, jh]
+            for t in slices:
                 cols = slice(t * P, (t + 1) * P)
                 bank = psum.tile([P, JW], F32, name="bo_bank", bufs=4)
                 nc.tensor.matmul_mx(
@@ -115,11 +115,11 @@ def tile_list_cable_tilt_displacement_kernel(
                 nc.scalar.activation(abs_b[:, t, :], bank[:], ACT.Abs)
 
         def cosines(g, jh):
-            cos_b[g, jh] = ring.tile([P, PACK, JW], F32, name="cos_b", bufs=2)
+            cos_b[g, jh] = held([P, PACK, JW], F32, f"cos_b{g}{jh}", tag=f"cos_b{jh}")
             nc.scalar.activation(cos_b[g, jh][:], magn[g, jh][:], ACT.Sin, bias=math.pi / 2, scale=-1.0)
 
-        def sines(g, jh):
-            sin_a = ring.tile([P, PACK, JW], F32, name="sin_a", bufs=3)
+        def strain_angles(g, jh):
+            banks = []
             for t in range(PACK):
                 bank = psum.tile([P, JW], F32, name="a_bank", bufs=4)
                 cols = slice(t * P, (t + 1) * P)
@@ -130,8 +130,12 @@ def tile_list_cable_tilt_displacement_kernel(
                         bank[:], lhsT=w1p_w[g][:, a, cols].bitcast(FP4X4), lhsT_scale=w1p_s[a][:, scols],
                         rhs=codes.bitcast(FP8X4), rhs_scale=v_s[a][:, events(jh)],
                         start=(a == 0), stop=(a == 1))
-                nc.scalar.activation(sin_a[:, t, :], bank[:], ACT.Sin)
-            return sin_a
+                banks.append(bank)
+            return banks
+
+        def sines(banks, sin_a, js):
+            for t, bank in enumerate(banks):
+                nc.scalar.activation(sin_a[:, t, js], bank[:, js], ACT.Sin)
 
         def product(g, jh, t, js, sin_a, prod):
             nc.vector.scalar_tensor_tensor(
@@ -182,21 +186,18 @@ def tile_list_cable_tilt_displacement_kernel(
         nc.sync.dma_start(list2[:], offs2)
         nc.sync.dma_start(list1[:], offs)
         load_w2(w2_raw0, 0)
-        for q in range(4):
-            nc.sync.dma_start(tab2_s[32 * q:32 * q + 4, :].bitcast(I32), tab2_scales[0, 4 * q:4 * q + 4, :].bitcast(I32))
+        for r in range(4):
+            nc.sync.dma_start(tab2_s[r:P:32, :].bitcast(I32), tab2_scales[0, r:16:4, :].bitcast(I32))
         tab2_w = placed([P, T], U16, "tab2_w", at_tab2w)
         nc.sync.dma_start(tab2_w[:].bitcast(I32), tab2_words[0].bitcast(I32))
+        nc.sync.dma_start(tab_s[0:P:4, :].bitcast(I32), tab_scales.bitcast(I32).rearrange("a q n -> (a q) n"))
         tab_w0 = placed([P, T], U32, "tab_w0", at_tab0)
         load_tab(0, tab_w0)
         load_two_pass_scales(w1_s, w1_scales, nc.sync)
-        w2_raw1 = placed([P, PACK, PASS], F32, "w2_raw1", at_raw1)
-        load_w2(w2_raw1, PASS)
         w1_w = placed([P, 2, H], U16, "w1_w", at_w1w)
         nc.sync.dma_start(w1_w[:].bitcast(I32), w1_words.bitcast(I32).rearrange("a p n -> p a n"))
-        tab_w1 = placed([P, T], U32, "tab_w1", at_tab1)
-        load_tab(1, tab_w1)
-        load_two_pass_scales(tab_s, tab_scales, nc.gpsimd)
-        nc.gpsimd.dma_start(gain_sb[:], gain.rearrange("(g p t) -> p g t", g=2, t=PACK))
+        w2_raw1 = placed([P, PACK, PASS], F32, "w2_raw1", at_raw1)
+        load_w2(w2_raw1, PASS)
 
         for u in range(2):
             nc.scalar.copy(
@@ -209,19 +210,32 @@ def tile_list_cable_tilt_displacement_kernel(
         nc.vector.tensor_copy(v2_w[1][:], tab2_w[:].indirect(half(list2, 1)))
         w2_c[0, 1] = placed([P, 2 * P], U32, "w2_c01", at_tab2w + kib)
         nc.vector.quantize_mx(w2_c[0, 1][:].bitcast(FP8X4), w2_s[0][:, 2 * P:PASS], w2_bf0[1][:])
-        for jh in range(2):
-            magnitudes(0, jh)
-            cosines(0, jh)
-        v_s[0] = placed([P, S], U8, "v_s0", at_tab2w)
-        nc.vector.tensor_copy(v_s[0][:], tab_s[:].indirect(list1[:]))
-        shift(v_s)
-        v_w0 = placed([P, S], U32, "v_w0", at_tabs)
-        nc.vector.tensor_copy(v_w0[:], tab_w0[:].indirect(list1[:]))
-        w1p_s[0] = placed([P, H], U8, "w1p_s0", at_tab0)
+        magnitudes(0, 0)
+        magnitudes(0, 1, range(1))
+        cosines(0, 0)
+        magnitudes(0, 1, range(1, PACK))
+        cosines(0, 1)
+        picked_s = placed([P, S], U8, "picked_s", at_tab2w)
+        nc.vector.tensor_copy(picked_s[:], tab_s[:].indirect(list1[:]))
+
+        def deal_scale_rows(a):
+            for r in range(4):
+                first = 64 * a + 4 * r
+                nc.sync.dma_start(v_s[a][r:P:32, :].bitcast(I32), picked_s[first:first + 49:16, :].bitcast(I32))
+
+        deal_scale_rows(0)
+        tab_w1 = placed([P, T], U32, "tab_w1", at_tab1)
+        load_tab(1, tab_w1)
+        deal_scale_rows(1)
+        gain_sb = placed([P, 2, PACK], F32, "gain_sb", at_tabs + 3 * kib)
+        nc.sync.dma_start(gain_sb[:], gain.rearrange("(g p t) -> p g t", g=2, t=PACK))
+        w1p_s[0] = placed([P, H], U8, "w1p_s0", at_tabs + 2 * kib)
         nc.vector.tensor_copy(
             w1p_s[0][:].rearrange("p (g t m) -> p g t m", g=2, t=PACK),
             w1_s[:].rearrange("p (g m t) -> p g t m", g=2, t=PACK))
         shift(w1p_s)
+        v_w0 = placed([P, S], U32, "v_w0", at_tabs + 3 * kib + 64)
+        nc.vector.tensor_copy(v_w0[:], tab_w0[:].indirect(list1[:]))
         load_phase(0, 0, placed([P, PACK, JW], F32, "phase00", at_w1s + 512 - 8 * kib)[:])
         load_phase(0, 1, placed([P, PACK, JW], F32, "phase01", at_w1s + 512)[:])
         nc.vector.tensor_copy(
@@ -229,12 +243,12 @@ def tile_list_cable_tilt_displacement_kernel(
             w2_raw1[:].rearrange("p i (m t) -> p m i t", t=PACK))
         nc.vector.quantize_mx(w2_c1[:].bitcast(FP8X4), w2_s[1][:], w2_bf1[:])
         magnitudes(1, 0)
-        load_phase(1, 0, placed([P, PACK, JW], F32, "phase10", at_raw1 + 4 * kib)[:])
         for g in range(2):
             w1p_w[g] = placed([P, 2, PASS], U16, f"w1p_w{g}", at_raw1 + 2 * kib * g)
             nc.vector.tensor_copy(
                 w1p_w[g][:].rearrange("p a (t m) -> p a t m", t=PACK),
                 w1_w[:, :, g * PASS:(g + 1) * PASS].rearrange("p a (m t) -> p a t m", t=PACK))
+        load_phase(1, 0, placed([P, PACK, JW], F32, "phase10", at_raw1 + 4 * kib)[:])
         w3_w = placed([P, 2, N], U32, "w3_w", at_w1w - 3 * kib)
         nc.sync.dma_start(w3_w[:].bitcast(I32), w3_words.rearrange("a p c i -> p a (c i)").bitcast(I32))
         w3_s = placed([P, 2, N], U8, "w3_s", at_w1w + kib)
@@ -252,7 +266,8 @@ def tile_list_cable_tilt_displacement_kernel(
         for g, jh in ((0, 0), (0, 1), (1, 0)):
             if g == 1:
                 cosines(g, jh)
-            sin_a = sines(g, jh)
+            sin_a = ring.tile([P, PACK, JW], F32, name="sin_a", bufs=3)
+            sines(strain_angles(g, jh), sin_a, whole)
             prod = ring.tile([P, PACK, JW], F32, name="prod")
             for t in range(PACK):
                 product(g, jh, t, whole, sin_a, prod)
@@ -261,19 +276,20 @@ def tile_list_cable_tilt_displacement_kernel(
             pending = (g, jh, add_phase(g, jh, prod, whole), whole)
         magnitudes(1, 1)
         cosines(1, 1)
-        sin_a = sines(1, 1)
+        sin_a = ring.tile([P, PACK, JW], F32, name="sin_a", bufs=3)
         prod = ring.tile([P, PACK, JW], F32, name="prod")
+        banks = strain_angles(1, 1)
+        first, second = slice(0, JW // 2), slice(JW // 2, JW)
+        sines(banks, sin_a, first)
+        sines(banks, sin_a, second)
         for t in range(PACK):
-            product(1, 1, t, whole, sin_a, prod)
+            product(1, 1, t, first, sin_a, prod)
             if t == 0:
                 quantise_h(*pending)
         close_banks(open_banks(0, whole, P), 0, whole, P, [nc.scalar.copy])
-        pieces = [slice(0, JW // 2), slice(JW // 2, 3 * JW // 4), slice(3 * JW // 4, JW)]
-        rows = [2 * P, 4 * P, 2 * P]
-        pending = None
-        for js, nrows in zip(pieces, rows):
-            h_bf = add_phase(1, 1, prod, js)
-            if pending is not None:
-                finish(*pending, [nc.scalar.copy])
-            pending = (h_bf, js, nrows)
-        finish(*pending, [nc.scalar.copy, nc.vector.tensor_copy])
+        h_first = add_phase(1, 1, prod, first)
+        for t in range(PACK):
+            product(1, 1, t, second, sin_a, prod)
+            if t == 0:
+                finish(h_first, first, 2 * P, [nc.scalar.copy])
+        finish(add_phase(1, 1, prod, second), second, 2 * P, [nc.scalar.copy, nc.vector.tensor_copy])

@@ -41,45 +41,60 @@ def tile_list_cable_tilt_displacement_kernel(
             return shared.tile(shape, dtype, name=name, align_bytes=64, offset=offset)
 
         kib = 1024
-        at_tab2w, at_tab0, at_raw1, at_w1w, at_tab1 = 0, 8 * kib, 24 * kib, 40 * kib, 44 * kib
-        at_tabs, at_tab2s, at_w1s = 58 * kib, 66 * kib, 79 * kib
+        at_tab2w, at_tab0, at_w1s = 8 * kib, 16 * kib, 34 * kib + 256
+        at_w1a, at_tab1, at_tabs = at_w1s + 2 * kib, 38 * kib + 512, 54 * kib + 256
+        at_tab2s, at_raw0 = at_tabs + 4 * kib, at_tabs + 8 * kib
+        at_raw1 = at_tab0 + 2 * kib + 128
         list1 = keep.tile([P, S // 16], U16, name="list1")
         list2 = keep.tile([P, S // 16], U16, name="list2")
         tab2_s = placed([P, T], U8, "tab2_s", at_tab2s)
         tab_s = placed([P, T], U8, "tab_s", at_tabs)
-        w1_s = placed([P, H], U8, "w1_s", at_w1s)
-        w2_raw0 = held([P, PACK, PASS], F32, "w2_raw0")
-        w2_bf0 = [held([P, PASS * 2], BF16, f"w2_bf0{u}") for u in range(2)]
-        w2_bf1 = held([P, PASS * PACK], BF16, "w2_bf1")
         w1p_w = {}
-        w1p_s = {1: held([P, H], U8, "w1p_s1")}
-        w2_c = {}
-        w2_c1 = held([P, PASS], U32, "w2_c1")
-        w2_c[1, 0], w2_c[1, 1] = w2_c1[:, 0:2 * P], w2_c1[:, 2 * P:PASS]
-        w2_s = [held([P, PASS], U8, f"w2_s{g}") for g in range(2)]
-        v_w1 = [held([P, JW], U32, f"v_w1{jh}") for jh in range(2)]
+        w2_c = [[held([P, 2 * P], U32, f"w2_c{g}{u}") for u in range(2)] for g in range(2)]
+        w2_s = [[held([P, 2 * P], U8, f"w2_s{g}{u}") for u in range(2)] for g in range(2)]
+        v_w1 = {1: held([P, JW], U32, "v_w11")}
         v_s = [held([P, S], U8, f"v_s{a}") for a in range(2)]
-        v2_w = [held([P, JW], U16, f"v2_w{jh}") for jh in range(2)]
+        v2_w = {}
         v2_s = held([P, S], U8, "v2_s")
+        picked_s = held([P, S], U8, "picked_s")
         cos_b = {}
         magn = {}
         h_c = [[held([P, JW], U32, f"h_c{g}{jh}") for jh in range(2)] for g in range(2)]
         h_s = [[held([P, JW], U8, f"h_s{g}{jh}") for jh in range(2)] for g in range(2)]
-        warm_in = held([P, 8], F32, "warm_in")
-        warm_out = placed([P, (at_tab1 + kib) // 4], F32, "warm_out", 0)
+        zero = placed([P, 8], F32, "zero", at_raw0)
+        half_pi = held([P, 1], F32, "half_pi")
+        sine_in = placed([P, (at_tab1 + kib) // 4], F32, "sine_in", 0)
+        zero_bias = held([P, 1], F32, "zero_bias")
         phase_sb = {}
 
         nc.vector.memset(tab2_s[:].bitcast(I32), 0)
-        nc.vector.memset(w1_s[:].bitcast(I32), 0)
-        nc.vector.memset(warm_in[:], 0.0)
-        nc.scalar.activation(warm_out[:, 0:8], warm_in[:], ACT.Sin, bias=w1_s[:, 0:4].bitcast(F32))
-        for plane in (tab_s, v_s[0], v_s[1], w1p_s[1]):
+        nc.vector.memset(zero[:, 0:1], 0.0)
+        nc.vector.tensor_scalar_add(half_pi[:], zero[:, 0:1], math.pi / 2)
+        nc.vector.memset(tab_s[:].bitcast(I32), 0)
+        nc.vector.memset(sine_in[:, 0:1], 0.0)
+        nc.scalar.activation(zero_bias[:], sine_in[:, 0:1], ACT.Sin)
+        for plane in v_s:
             nc.vector.memset(plane[:].bitcast(I32), 0)
+        w1_s = placed([P, 2, H], U8, "w1_s", at_w1s)
+        nc.vector.memset(w1_s[:].rearrange("p a n -> p (a n)").bitcast(I32), 0)
 
-        def load_two_pass_scales(plane, scales, queue):
+        def load_two_pass_scales(plane, scales):
             rows = scales.bitcast(I32).rearrange("a (q r) n -> r q a n", r=4)
             for r in range(4):
-                queue.dma_start(plane[r:P:16, :].bitcast(I32), rows[r])
+                nc.sync.dma_start(plane[r:P:32, :, :].bitcast(I32), rows[r])
+
+        def round_w2(engine, raw, u, dst):
+            engine(
+                dst.rearrange("p (t m i) -> p m i t", t=2, i=PACK),
+                raw[:].rearrange("p i (m t) -> p m i t", t=PACK)[:, :, :, 2 * u:2 * u + 2])
+
+        def quantise_w2(g, u, src):
+            nc.vector.quantize_mx(w2_c[g][u][:].bitcast(FP8X4), w2_s[g][u][:], src)
+
+        def deal_scale_rows(a):
+            for r in range(4):
+                first = 64 * a + 4 * r
+                nc.sync.dma_start(v_s[a][r:P:32, :].bitcast(I32), picked_s[first:first + 49:16, :].bitcast(I32))
 
         def load_w2(raw, c0):
             nc.sync.dma_start(raw[:], w2[:, c0:c0 + raw.shape[2]].rearrange("(p i) c -> p i c", i=PACK))
@@ -90,11 +105,20 @@ def tile_list_cable_tilt_displacement_kernel(
                 dst,
                 phase[g * PASS:(g + 1) * PASS, jh * JW:(jh + 1) * JW].rearrange("(p t) j -> p t j", t=PACK))
 
-        def load_tab(a, tile):
-            nc.sync.dma_start(tile[:].bitcast(I32), tab_words[a].rearrange("p t i -> p (t i)").bitcast(I32))
+        def load_tab(a, tile, cols=slice(0, T)):
+            nc.sync.dma_start(tile[:, cols].bitcast(I32), tab_words[a].rearrange("p t i -> p (t i)").bitcast(I32)[:, cols])
 
-        def shift(planes):
-            nc.sync.dma_start(planes[1][0:112, :].bitcast(I32), planes[0][16:P, :].bitcast(I32))
+        def load_w1(g, at):
+            raw = placed([P, 2, PASS], U16, f"w1_w{g}", at)
+            words = w1_words.bitcast(I32).rearrange("a p n -> p a n")
+            nc.sync.dma_start(raw[:].bitcast(I32), words[:, :, g * PASS // 2:(g + 1) * PASS // 2])
+            return raw
+
+        def order_w1(g, raw, at):
+            w1p_w[g] = placed([P, 2, PASS], U16, f"w1p_w{g}", at)
+            nc.vector.tensor_copy(
+                w1p_w[g][:].rearrange("p a (t m) -> p a t m", t=PACK),
+                raw[:].rearrange("p a (m t) -> p a t m", t=PACK))
 
         def half(lst, jh):
             return lst[:, jh * (JW // 16):(jh + 1) * (JW // 16)]
@@ -104,38 +128,38 @@ def tile_list_cable_tilt_displacement_kernel(
 
         def magnitudes(g, jh, slices=range(PACK)):
             if (g, jh) not in magn:
-                magn[g, jh] = held([P, PACK, JW], F32, f"abs_b{g}{jh}", tag="abs_01" if (g, jh) == (0, 1) else "abs_b")
+                magn[g, jh] = held([P, PACK, JW], F32, f"abs_b{g}{jh}", tag="abs_b")
             abs_b = magn[g, jh]
             for t in slices:
-                cols = slice(t * P, (t + 1) * P)
                 bank = psum.tile([P, JW], F32, name="bo_bank", bufs=4)
                 nc.tensor.matmul_mx(
-                    bank[:], lhsT=w2_c[g, t // 2][:, t % 2 * P:(t % 2 + 1) * P].bitcast(FP8X4), lhsT_scale=w2_s[g][:, cols],
+                    bank[:], lhsT=w2_c[g][t // 2][:, t % 2 * P:(t % 2 + 1) * P].bitcast(FP8X4),
+                    lhsT_scale=w2_s[g][t // 2][:, t % 2 * P:(t % 2 + 1) * P],
                     rhs=v2_w[jh][:].bitcast(FP4X4), rhs_scale=v2_s[:, events(jh)], start=True, stop=True)
                 nc.scalar.activation(abs_b[:, t, :], bank[:], ACT.Abs)
 
         def cosines(g, jh):
             cos_b[g, jh] = held([P, PACK, JW], F32, f"cos_b{g}{jh}", tag=f"cos_b{jh}")
-            nc.scalar.activation(cos_b[g, jh][:], magn[g, jh][:], ACT.Sin, bias=math.pi / 2, scale=-1.0)
+            nc.scalar.activation(cos_b[g, jh][:], magn[g, jh][:], ACT.Sin, bias=half_pi[:], scale=-1.0)
 
         def strain_angles(g, jh):
-            banks = []
-            for t in range(PACK):
-                bank = psum.tile([P, JW], F32, name="a_bank", bufs=4)
+            banks = [psum.tile([P, JW], F32, name="a_bank", bufs=4) for t in range(PACK)]
+            steps = [(t, a) for t in range(PACK) for a in range(2)]
+            if (g, jh) == (0, 0):
+                steps = [(t, a) for a in range(2) for t in range(PACK)]
+            for t, a in steps:
                 cols = slice(t * P, (t + 1) * P)
                 scols = slice(g * PASS + t * P, g * PASS + (t + 1) * P)
-                for a in range(2):
-                    codes = v_w0[:, events(jh)] if a == 0 else v_w1[jh][:]
-                    nc.tensor.matmul_mx(
-                        bank[:], lhsT=w1p_w[g][:, a, cols].bitcast(FP4X4), lhsT_scale=w1p_s[a][:, scols],
-                        rhs=codes.bitcast(FP8X4), rhs_scale=v_s[a][:, events(jh)],
-                        start=(a == 0), stop=(a == 1))
-                banks.append(bank)
+                codes = v_w0[:, events(jh)] if a == 0 else v_w1[jh][:]
+                nc.tensor.matmul_mx(
+                    banks[t][:], lhsT=w1p_w[g][:, a, cols].bitcast(FP4X4), lhsT_scale=w1p_s[:, a, scols],
+                    rhs=codes.bitcast(FP8X4), rhs_scale=v_s[a][:, events(jh)],
+                    start=(a == 0), stop=(a == 1))
             return banks
 
         def sines(banks, sin_a, js):
             for t, bank in enumerate(banks):
-                nc.scalar.activation(sin_a[:, t, js], bank[:, js], ACT.Sin)
+                nc.scalar.activation(sin_a[:, t, js], bank[:, js], ACT.Sin, bias=zero_bias[:])
 
         def product(g, jh, t, js, sin_a, prod):
             nc.vector.scalar_tensor_tensor(
@@ -185,98 +209,92 @@ def tile_list_cable_tilt_displacement_kernel(
 
         nc.sync.dma_start(list2[:], offs2)
         nc.sync.dma_start(list1[:], offs)
-        load_w2(w2_raw0, 0)
         for r in range(4):
             nc.sync.dma_start(tab2_s[r:P:32, :].bitcast(I32), tab2_scales[0, r:16:4, :].bitcast(I32))
+        w2_raw0 = placed([P, PACK, PASS], F32, "w2_raw0", at_raw0)
+        load_w2(w2_raw0, 0)
+        nc.sync.dma_start(tab_s[0:P:4, :].bitcast(I32), tab_scales.bitcast(I32).rearrange("a q n -> (a q) n"))
         tab2_w = placed([P, T], U16, "tab2_w", at_tab2w)
         nc.sync.dma_start(tab2_w[:].bitcast(I32), tab2_words[0].bitcast(I32))
-        nc.sync.dma_start(tab_s[0:P:4, :].bitcast(I32), tab_scales.bitcast(I32).rearrange("a q n -> (a q) n"))
         tab_w0 = placed([P, T], U32, "tab_w0", at_tab0)
-        load_tab(0, tab_w0)
-        load_two_pass_scales(w1_s, w1_scales, nc.sync)
-        w1_w = placed([P, 2, H], U16, "w1_w", at_w1w)
-        nc.sync.dma_start(w1_w[:].bitcast(I32), w1_words.bitcast(I32).rearrange("a p n -> p a n"))
+        load_tab(0, tab_w0, slice(0, T // 2))
+        load_two_pass_scales(w1_s, w1_scales)
+        load_tab(0, tab_w0, slice(T // 2, T))
+        w1_w0 = load_w1(0, at_w1a)
+
+        w2_bf0 = [held([P, PASS * 2], BF16, f"w2_bf0{u}") for u in range(2)]
+        for u in range(2):
+            round_w2(nc.scalar.copy, w2_raw0, u, w2_bf0[u][:])
+        nc.vector.tensor_copy(v2_s[:], tab2_s[:].indirect(list2[:]))
+        nc.vector.tensor_copy(picked_s[:], tab_s[:].indirect(list1[:]))
+        tab_w1 = placed([P, T], U32, "tab_w1", at_tab1)
+        load_tab(1, tab_w1, slice(0, T // 2))
+        deal_scale_rows(0)
+        load_tab(1, tab_w1, slice(T // 2, T))
+        deal_scale_rows(1)
+        quantise_w2(0, 0, w2_bf0[0][:])
+        v2_w[0] = placed([P, JW], U16, "v2_w0", at_tabs + 256)
+        nc.vector.tensor_copy(v2_w[0][:], tab2_w[:].indirect(half(list2, 0)))
+        quantise_w2(0, 1, w2_bf0[1][:])
+        v2_w[1] = placed([P, JW], U16, "v2_w1", at_tabs + 2 * kib + 512)
+        nc.vector.tensor_copy(v2_w[1][:], tab2_w[:].indirect(half(list2, 1)))
+        for jh in range(2):
+            magnitudes(0, jh)
+            cosines(0, jh)
+
+        gain_sb = placed([P, 2, PACK], F32, "gain_sb", at_tab2w + 6 * kib + 64)
+        nc.sync.dma_start(gain_sb[:], gain.rearrange("(g p t) -> p g t", g=2, t=PACK))
+        load_phase(0, 0, placed([P, PACK, JW], F32, "phase00", 64)[:])
+        w1p_s = placed([P, 2, H], U8, "w1p_s", at_tab2w + 4 * kib + 64)
+        nc.vector.tensor_copy(
+            w1p_s[:].rearrange("p a (g t m) -> p (a g) t m", g=2, t=PACK),
+            w1_s[:].rearrange("p a (g m t) -> p (a g) t m", g=2, t=PACK))
+        v_w0 = placed([P, S], U32, "v_w0", at_tab2w + 64)
+        nc.vector.tensor_copy(v_w0[:], tab_w0[:].indirect(list1[:]))
+        w1_w1 = load_w1(1, at_tab2w + 6 * kib + 128)
         w2_raw1 = placed([P, PACK, PASS], F32, "w2_raw1", at_raw1)
         load_w2(w2_raw1, PASS)
-
-        for u in range(2):
-            nc.scalar.copy(
-                w2_bf0[u][:].rearrange("p (t m i) -> p m i t", t=2, i=PACK),
-                w2_raw0[:].rearrange("p i (m t) -> p m i t", t=PACK)[:, :, :, 2 * u:2 * u + 2])
-        nc.vector.tensor_copy(v2_s[:], tab2_s[:].indirect(list2[:]))
-        w2_c[0, 0] = placed([P, 2 * P], U32, "w2_c00", at_tab2s)
-        nc.vector.tensor_copy(v2_w[0][:], tab2_w[:].indirect(half(list2, 0)))
-        nc.vector.quantize_mx(w2_c[0, 0][:].bitcast(FP8X4), w2_s[0][:, 0:2 * P], w2_bf0[0][:])
-        nc.vector.tensor_copy(v2_w[1][:], tab2_w[:].indirect(half(list2, 1)))
-        w2_c[0, 1] = placed([P, 2 * P], U32, "w2_c01", at_tab2w + kib)
-        nc.vector.quantize_mx(w2_c[0, 1][:].bitcast(FP8X4), w2_s[0][:, 2 * P:PASS], w2_bf0[1][:])
-        magnitudes(0, 0)
-        magnitudes(0, 1, range(1))
-        cosines(0, 0)
-        magnitudes(0, 1, range(1, PACK))
-        cosines(0, 1)
-        picked_s = placed([P, S], U8, "picked_s", at_tab2w)
-        nc.vector.tensor_copy(picked_s[:], tab_s[:].indirect(list1[:]))
-
-        def deal_scale_rows(a):
-            for r in range(4):
-                first = 64 * a + 4 * r
-                nc.sync.dma_start(v_s[a][r:P:32, :].bitcast(I32), picked_s[first:first + 49:16, :].bitcast(I32))
-
-        deal_scale_rows(0)
-        tab_w1 = placed([P, T], U32, "tab_w1", at_tab1)
-        load_tab(1, tab_w1)
-        deal_scale_rows(1)
-        gain_sb = placed([P, 2, PACK], F32, "gain_sb", at_tabs + 3 * kib)
-        nc.sync.dma_start(gain_sb[:], gain.rearrange("(g p t) -> p g t", g=2, t=PACK))
-        w1p_s[0] = placed([P, H], U8, "w1p_s0", at_tabs + 2 * kib)
-        nc.vector.tensor_copy(
-            w1p_s[0][:].rearrange("p (g t m) -> p g t m", g=2, t=PACK),
-            w1_s[:].rearrange("p (g m t) -> p g t m", g=2, t=PACK))
-        shift(w1p_s)
-        v_w0 = placed([P, S], U32, "v_w0", at_tabs + 3 * kib + 64)
-        nc.vector.tensor_copy(v_w0[:], tab_w0[:].indirect(list1[:]))
-        load_phase(0, 0, placed([P, PACK, JW], F32, "phase00", at_w1s + 512 - 8 * kib)[:])
-        load_phase(0, 1, placed([P, PACK, JW], F32, "phase01", at_w1s + 512)[:])
-        nc.vector.tensor_copy(
-            w2_bf1[:].rearrange("p (t m i) -> p m i t", t=PACK, i=PACK),
-            w2_raw1[:].rearrange("p i (m t) -> p m i t", t=PACK))
-        nc.vector.quantize_mx(w2_c1[:].bitcast(FP8X4), w2_s[1][:], w2_bf1[:])
-        magnitudes(1, 0)
-        for g in range(2):
-            w1p_w[g] = placed([P, 2, PASS], U16, f"w1p_w{g}", at_raw1 + 2 * kib * g)
-            nc.vector.tensor_copy(
-                w1p_w[g][:].rearrange("p a (t m) -> p a t m", t=PACK),
-                w1_w[:, :, g * PASS:(g + 1) * PASS].rearrange("p a (m t) -> p a t m", t=PACK))
-        load_phase(1, 0, placed([P, PACK, JW], F32, "phase10", at_raw1 + 4 * kib)[:])
-        w3_w = placed([P, 2, N], U32, "w3_w", at_w1w - 3 * kib)
-        nc.sync.dma_start(w3_w[:].bitcast(I32), w3_words.rearrange("a p c i -> p a (c i)").bitcast(I32))
-        w3_s = placed([P, 2, N], U8, "w3_s", at_w1w + kib)
+        load_phase(0, 1, placed([P, PACK, JW], F32, "phase01", at_raw1 + 8 * kib)[:])
+        order_w1(0, w1_w0, at_tab0 + 128)
+        w3_s = placed([P, 2, N], U8, "w3_s", at_w1s)
         nc.vector.memset(w3_s[:].rearrange("p a n -> p (a n)").bitcast(I32), 0)
-        for q in range(4):
-            nc.sync.dma_start(
-                w3_s[32 * q:32 * q + 4, :, :].bitcast(I32),
-                w3_scales[:, 4 * q:4 * q + 4, :].bitcast(I32).rearrange("a r n -> r a n"))
+        v_w1[0] = placed([P, JW], U32, "v_w10", at_w1a)
         for jh in range(2):
             nc.vector.tensor_copy(v_w1[jh][:], tab_w1[:].indirect(half(list1, jh)))
-        load_phase(1, 1, placed([P, PACK, JW], F32, "phase11", at_tab1)[:])
+        order_w1(1, w1_w1, at_tab1)
+        load_phase(1, 0, placed([P, PACK, JW], F32, "phase10", at_tab1 + 2 * kib)[:])
+        load_two_pass_scales(w3_s, w3_scales)
 
         whole = slice(0, JW)
         pending = None
-        for g, jh in ((0, 0), (0, 1), (1, 0)):
-            if g == 1:
-                cosines(g, jh)
-            sin_a = ring.tile([P, PACK, JW], F32, name="sin_a", bufs=3)
+        for n, (g, jh) in enumerate(((0, 0), (0, 1), (1, 0))):
+            sin_a = held([P, PACK, JW], F32, f"sin_a{n}", tag=f"sin_{n % 2}")
             sines(strain_angles(g, jh), sin_a, whole)
+            if n == 0:
+                w2_bf1 = [placed([P, PASS * 2], BF16, "w2_bf10", at_tab2w + 6 * kib + 128),
+                          None]
+                round_w2(nc.scalar.copy, w2_raw1, 0, w2_bf1[0][:])
             prod = ring.tile([P, PACK, JW], F32, name="prod")
             for t in range(PACK):
                 product(g, jh, t, whole, sin_a, prod)
                 if t == 0 and pending is not None:
                     quantise_h(*pending)
+                if t == 0 and n == 1:
+                    quantise_w2(1, 1, w2_bf1[1][:])
             pending = (g, jh, add_phase(g, jh, prod, whole), whole)
+            if n == 0:
+                quantise_w2(1, 0, w2_bf1[0][:])
+                w2_bf1[1:] = [placed([P, PASS * 2], BF16, "w2_bf11", 64)]
+                round_w2(nc.vector.tensor_copy, w2_raw1, 1, w2_bf1[1][:])
+                w3_w = placed([P, 2, N], U32, "w3_w", at_raw1)
+                nc.sync.dma_start(w3_w[:].bitcast(I32), w3_words.rearrange("a p c i -> p a (c i)").bitcast(I32))
+            if n == 1:
+                magnitudes(1, 0)
+                cosines(1, 0)
+                load_phase(1, 1, placed([P, PACK, JW], F32, "phase11", at_tab1 + 10 * kib)[:])
         magnitudes(1, 1)
         cosines(1, 1)
-        sin_a = ring.tile([P, PACK, JW], F32, name="sin_a", bufs=3)
+        sin_a = held([P, PACK, JW], F32, "sin_a3", tag="sin_1")
         prod = ring.tile([P, PACK, JW], F32, name="prod")
         banks = strain_angles(1, 1)
         first, second = slice(0, JW // 2), slice(JW // 2, JW)

@@ -159,11 +159,11 @@ def tile_list_cable_tilt_displacement_kernel(
 
         def sines(banks, sin_a, js):
             for t, bank in enumerate(banks):
-                nc.scalar.activation(sin_a[:, t, js], bank[:, js], ACT.Sin, bias=zero_bias[:])
+                nc.scalar.activation(sin_a[t][:, js], bank[:, js], ACT.Sin, bias=zero_bias[:])
 
         def product(g, jh, t, js, sin_a, prod):
             nc.vector.scalar_tensor_tensor(
-                prod[:, t, js], cos_b[g, jh][:, t, js], gain_sb[:, g, t:t + 1], sin_a[:, t, js], ALU.mult, ALU.mult)
+                prod[:, t, js], cos_b[g, jh][:, t, js], gain_sb[:, g, t:t + 1], sin_a[t][:, js], ALU.mult, ALU.mult)
 
         def add_phase(g, jh, prod, js):
             h_bf = ring.tile([P, (js.stop - js.start) * PACK], BF16, name="h_bf", bufs=3, align_bytes=64)
@@ -244,16 +244,16 @@ def tile_list_cable_tilt_displacement_kernel(
 
         gain_sb = placed([P, 2, PACK], F32, "gain_sb", at_tab2w + 6 * kib + 64)
         nc.sync.dma_start(gain_sb[:], gain.rearrange("(g p t) -> p g t", g=2, t=PACK))
-        load_phase(0, 0, placed([P, PACK, JW], F32, "phase00", 64)[:])
+        w2_raw1 = placed([P, PACK, PASS], F32, "w2_raw1", 64)
+        load_w2(w2_raw1, PASS)
         w1p_s = placed([P, 2, H], U8, "w1p_s", at_tab2w + 4 * kib + 64)
         nc.vector.tensor_copy(
             w1p_s[:].rearrange("p a (g t m) -> p (a g) t m", g=2, t=PACK),
             w1_s[:].rearrange("p a (g m t) -> p (a g) t m", g=2, t=PACK))
         v_w0 = placed([P, S], U32, "v_w0", at_tab2w + 64)
         nc.vector.tensor_copy(v_w0[:], tab_w0[:].indirect(list1[:]))
+        load_phase(0, 0, placed([P, PACK, JW], F32, "phase00", at_raw1)[:])
         w1_w1 = load_w1(1, at_tab2w + 6 * kib + 128)
-        w2_raw1 = placed([P, PACK, PASS], F32, "w2_raw1", at_raw1)
-        load_w2(w2_raw1, PASS)
         load_phase(0, 1, placed([P, PACK, JW], F32, "phase01", at_raw1 + 8 * kib)[:])
         order_w1(0, w1_w0, at_tab0 + 128)
         w3_s = placed([P, 2, N], U8, "w3_s", at_w1s)
@@ -261,32 +261,31 @@ def tile_list_cable_tilt_displacement_kernel(
         v_w1[0] = placed([P, JW], U32, "v_w10", at_w1a)
         for jh in range(2):
             nc.vector.tensor_copy(v_w1[jh][:], tab_w1[:].indirect(half(list1, jh)))
-        order_w1(1, w1_w1, at_tab1)
+        w2_bf10 = placed([P, PASS * 2], BF16, "w2_bf10", at_tab1)
+        round_w2(nc.vector.tensor_copy, w2_raw1, 0, w2_bf10[:])
         load_phase(1, 0, placed([P, PACK, JW], F32, "phase10", at_tab1 + 2 * kib)[:])
         load_two_pass_scales(w3_s, w3_scales)
 
         whole = slice(0, JW)
         pending = None
         for n, (g, jh) in enumerate(((0, 0), (0, 1), (1, 0))):
-            sin_a = held([P, PACK, JW], F32, f"sin_a{n}", tag=f"sin_{n % 2}")
+            sin_a = [held([P, JW], F32, f"sin_a{n}{t}", tag=f"sin_{n % 2}{t}") for t in range(PACK)]
             sines(strain_angles(g, jh), sin_a, whole)
-            if n == 0:
-                w2_bf1 = [placed([P, PASS * 2], BF16, "w2_bf10", at_tab2w + 6 * kib + 128),
-                          None]
-                round_w2(nc.scalar.copy, w2_raw1, 0, w2_bf1[0][:])
             prod = ring.tile([P, PACK, JW], F32, name="prod")
             for t in range(PACK):
                 product(g, jh, t, whole, sin_a, prod)
                 if t == 0 and pending is not None:
                     quantise_h(*pending)
-                if t == 0 and n == 1:
-                    quantise_w2(1, 1, w2_bf1[1][:])
+                if t == 0 and n == 0:
+                    w2_bf11 = held([P, PASS * 2], BF16, "w2_bf11", tag="sin_00")
+                    round_w2(nc.scalar.copy, w2_raw1, 1, w2_bf11[:])
+                    quantise_w2(1, 0, w2_bf10[:])
+                if t == PACK - 1 and n == 0:
+                    quantise_w2(1, 1, w2_bf11[:])
             pending = (g, jh, add_phase(g, jh, prod, whole), whole)
             if n == 0:
-                quantise_w2(1, 0, w2_bf1[0][:])
-                w2_bf1[1:] = [placed([P, PASS * 2], BF16, "w2_bf11", 64)]
-                round_w2(nc.vector.tensor_copy, w2_raw1, 1, w2_bf1[1][:])
-                w3_w = placed([P, 2, N], U32, "w3_w", at_raw1)
+                order_w1(1, w1_w1, at_raw1 + 2 * kib)
+                w3_w = placed([P, 2, N], U32, "w3_w", 64)
                 nc.sync.dma_start(w3_w[:].bitcast(I32), w3_words.rearrange("a p c i -> p a (c i)").bitcast(I32))
             if n == 1:
                 magnitudes(1, 0)
@@ -294,7 +293,7 @@ def tile_list_cable_tilt_displacement_kernel(
                 load_phase(1, 1, placed([P, PACK, JW], F32, "phase11", at_tab1 + 10 * kib)[:])
         magnitudes(1, 1)
         cosines(1, 1)
-        sin_a = held([P, PACK, JW], F32, "sin_a3", tag="sin_1")
+        sin_a = [held([P, JW], F32, f"sin_a3{t}", tag=f"sin_1{t}") for t in range(PACK)]
         prod = ring.tile([P, PACK, JW], F32, name="prod")
         banks = strain_angles(1, 1)
         first, second = slice(0, JW // 2), slice(JW // 2, JW)

@@ -182,11 +182,11 @@ def tile_list_cable_tilt_displacement_kernel(
                 dst, lhsT=w3_w[:, g, cols].bitcast(FP8X4), lhsT_scale=w3_s[:, g, cols],
                 rhs=h_c[g][jh][:, js].bitcast(FP8X4), rhs_scale=h_s[g][jh][:, js], start=start, stop=stop)
 
-        def open_banks(jh, js, nrows):
+        def open_banks(jh, js, nrows, tag="bo_bank"):
             per = nrows // P
             banks = []
             for c0 in range(0, N // P, per):
-                bank = psum.tile([P, per, js.stop - js.start], F32, name="bo_bank", bufs=4)
+                bank = psum.tile([P, per, js.stop - js.start], F32, name=tag, bufs=4)
                 for k in range(per):
                     last_pass(bank[:, k, :], c0 + k, 0, jh, js, k == 0, False)
                 banks.append(bank)
@@ -202,8 +202,8 @@ def tile_list_cable_tilt_displacement_kernel(
                 dst = out[n * nrows:(n + 1) * nrows, jh * JW + js.start:jh * JW + js.stop]
                 nc.sync.dma_start(dst.rearrange("(c p) j -> p c j", p=P), res[:])
 
-        def finish(h_bf, js, nrows, engines):
-            banks = open_banks(1, js, nrows)
+        def finish(h_bf, js, nrows, engines, tag):
+            banks = open_banks(1, js, nrows, tag)
             quantise_h(1, 1, h_bf, js)
             close_banks(banks, 1, js, nrows, engines)
 
@@ -308,5 +308,13 @@ def tile_list_cable_tilt_displacement_kernel(
         for t in range(PACK):
             product(1, 1, t, second, sin_a, prod)
             if t == 0:
-                finish(h_first, first, 2 * P, [nc.scalar.copy])
-        finish(add_phase(1, 1, prod, second), second, 2 * P, [nc.scalar.copy, nc.vector.tensor_copy])
+                finish(h_first, first, 2 * P, [nc.scalar.copy], "a_bank")
+        third, fourth = slice(JW // 2, 3 * JW // 4), slice(3 * JW // 4, JW)
+        h_third = add_phase(1, 1, prod, third)
+        h_fourth = add_phase(1, 1, prod, fourth)
+        banks_third = open_banks(1, third, 2 * P, "a_bank")
+        banks_fourth = open_banks(1, fourth, 2 * P, "bo_bank")
+        quantise_h(1, 1, h_third, third)
+        quantise_h(1, 1, h_fourth, fourth)
+        close_banks(banks_third, 1, third, 2 * P, [nc.scalar.copy, nc.vector.tensor_copy])
+        close_banks(banks_fourth, 1, fourth, 2 * P, [nc.scalar.copy, nc.vector.tensor_copy])

@@ -41,9 +41,9 @@ def tile_list_cable_tilt_displacement_kernel(
             return shared.tile(shape, dtype, name=name, align_bytes=64, offset=offset)
 
         kib = 1024
-        at_tab2w, at_tab0, at_w1s = 8 * kib, 16 * kib, 34 * kib + 256
-        at_w1a, at_tab1, at_tabs = at_w1s + 2 * kib, 38 * kib + 512, 54 * kib + 256
-        at_tab2s, at_raw0 = at_tabs + 4 * kib, at_tabs + 8 * kib
+        at_w1a, at_low, at_tab2w, at_tab0 = 0, 2 * kib + 64, 10 * kib, 18 * kib
+        at_tab2s, at_w1s, at_tab1, at_tabs = 33 * kib, 36 * kib + 256, 38 * kib + 512, 54 * kib + 256
+        at_raw0 = at_tabs + 4 * kib
         at_raw1 = at_tab0 + 2 * kib + 128
         list1 = keep.tile([P, S // 16], U16, name="list1")
         list2 = keep.tile([P, S // 16], U16, name="list2")
@@ -57,13 +57,14 @@ def tile_list_cable_tilt_displacement_kernel(
         v2_w = {}
         v2_s = held([P, S], U8, "v2_s")
         picked_s = held([P, S], U8, "picked_s")
+        picked2_s = held([P, S], U8, "picked2_s")
         cos_b = {}
         magn = {}
         h_c = [[held([P, JW], U32, f"h_c{g}{jh}") for jh in range(2)] for g in range(2)]
         h_s = [[held([P, JW], U8, f"h_s{g}{jh}") for jh in range(2)] for g in range(2)]
         zero = placed([P, 8], F32, "zero", at_raw0)
         half_pi = held([P, 1], F32, "half_pi")
-        sine_in = placed([P, (at_tab1 + kib) // 4], F32, "sine_in", 0)
+        sine_in = placed([P, (at_tab2w + kib) // 4], F32, "sine_in", 0)
         zero_bias = held([P, 1], F32, "zero_bias")
         phase_sb = {}
 
@@ -73,10 +74,8 @@ def tile_list_cable_tilt_displacement_kernel(
         nc.vector.memset(tab_s[:].bitcast(I32), 0)
         nc.vector.memset(sine_in[:, 0:1], 0.0)
         nc.scalar.activation(zero_bias[:], sine_in[:, 0:1], ACT.Sin)
-        for plane in v_s:
+        for plane in [v2_s] + v_s:
             nc.vector.memset(plane[:].bitcast(I32), 0)
-        w1_s = placed([P, 2, H], U8, "w1_s", at_w1s)
-        nc.vector.memset(w1_s[:].rearrange("p a n -> p (a n)").bitcast(I32), 0)
 
         def load_two_pass_scales(plane, scales):
             rows = scales.bitcast(I32).rearrange("a (q r) n -> r q a n", r=4)
@@ -91,10 +90,10 @@ def tile_list_cable_tilt_displacement_kernel(
         def quantise_w2(g, u, src):
             nc.vector.quantize_mx(w2_c[g][u][:].bitcast(FP8X4), w2_s[g][u][:], src)
 
-        def deal_scale_rows(a):
+        def deal_scale_rows(plane, picked, row0):
             for r in range(4):
-                first = 64 * a + 4 * r
-                nc.sync.dma_start(v_s[a][r:P:32, :].bitcast(I32), picked_s[first:first + 49:16, :].bitcast(I32))
+                first = row0 + 4 * r
+                nc.sync.dma_start(plane[r:P:32, :].bitcast(I32), picked[first:first + 49:16, :].bitcast(I32))
 
         def load_w2(raw, c0):
             nc.sync.dma_start(raw[:], w2[:, c0:c0 + raw.shape[2]].rearrange("(p i) c -> p i c", i=PACK))
@@ -209,29 +208,31 @@ def tile_list_cable_tilt_displacement_kernel(
 
         nc.sync.dma_start(list2[:], offs2)
         nc.sync.dma_start(list1[:], offs)
-        for r in range(4):
-            nc.sync.dma_start(tab2_s[r:P:32, :].bitcast(I32), tab2_scales[0, r:16:4, :].bitcast(I32))
+        nc.sync.dma_start(tab2_s[32:96:4, :].bitcast(I32), tab2_scales[0].bitcast(I32))
         w2_raw0 = placed([P, PACK, PASS], F32, "w2_raw0", at_raw0)
         load_w2(w2_raw0, 0)
         nc.sync.dma_start(tab_s[0:P:4, :].bitcast(I32), tab_scales.bitcast(I32).rearrange("a q n -> (a q) n"))
         tab2_w = placed([P, T], U16, "tab2_w", at_tab2w)
         nc.sync.dma_start(tab2_w[:].bitcast(I32), tab2_words[0].bitcast(I32))
-        tab_w0 = placed([P, T], U32, "tab_w0", at_tab0)
-        load_tab(0, tab_w0, slice(0, T // 2))
-        load_two_pass_scales(w1_s, w1_scales)
-        load_tab(0, tab_w0, slice(T // 2, T))
         w1_w0 = load_w1(0, at_w1a)
 
         w2_bf0 = [held([P, PASS * 2], BF16, f"w2_bf0{u}") for u in range(2)]
         for u in range(2):
             round_w2(nc.scalar.copy, w2_raw0, u, w2_bf0[u][:])
-        nc.vector.tensor_copy(v2_s[:], tab2_s[:].indirect(list2[:]))
+        nc.vector.tensor_copy(picked2_s[:], tab2_s[:].indirect(list2[:]))
+        deal_scale_rows(v2_s, picked2_s, 32)
+        tab_w0 = placed([P, T], U32, "tab_w0", at_tab0)
+        load_tab(0, tab_w0, slice(0, T // 2))
+        w1_s = placed([P, 2, H], U8, "w1_s", at_w1s)
+        nc.vector.memset(w1_s[:].rearrange("p a n -> p (a n)").bitcast(I32), 0)
+        load_two_pass_scales(w1_s, w1_scales)
+        load_tab(0, tab_w0, slice(T // 2, T))
         nc.vector.tensor_copy(picked_s[:], tab_s[:].indirect(list1[:]))
         tab_w1 = placed([P, T], U32, "tab_w1", at_tab1)
         load_tab(1, tab_w1, slice(0, T // 2))
-        deal_scale_rows(0)
+        deal_scale_rows(v_s[0], picked_s, 0)
         load_tab(1, tab_w1, slice(T // 2, T))
-        deal_scale_rows(1)
+        deal_scale_rows(v_s[1], picked_s, 64)
         quantise_w2(0, 0, w2_bf0[0][:])
         v2_w[0] = placed([P, JW], U16, "v2_w0", at_tabs + 256)
         nc.vector.tensor_copy(v2_w[0][:], tab2_w[:].indirect(half(list2, 0)))
@@ -244,7 +245,7 @@ def tile_list_cable_tilt_displacement_kernel(
 
         gain_sb = placed([P, 2, PACK], F32, "gain_sb", at_tab2w + 6 * kib + 64)
         nc.sync.dma_start(gain_sb[:], gain.rearrange("(g p t) -> p g t", g=2, t=PACK))
-        w2_raw1 = placed([P, PACK, PASS], F32, "w2_raw1", 64)
+        w2_raw1 = placed([P, PACK, PASS], F32, "w2_raw1", at_low)
         load_w2(w2_raw1, PASS)
         w1p_s = placed([P, 2, H], U8, "w1p_s", at_tab2w + 4 * kib + 64)
         nc.vector.tensor_copy(
@@ -285,7 +286,7 @@ def tile_list_cable_tilt_displacement_kernel(
             pending = (g, jh, add_phase(g, jh, prod, whole), whole)
             if n == 0:
                 order_w1(1, w1_w1, at_raw1 + 2 * kib)
-                w3_w = placed([P, 2, N], U32, "w3_w", 64)
+                w3_w = placed([P, 2, N], U32, "w3_w", at_low)
                 nc.sync.dma_start(w3_w[:].bitcast(I32), w3_words.rearrange("a p c i -> p a (c i)").bitcast(I32))
             if n == 1:
                 magnitudes(1, 0)

@@ -41,8 +41,8 @@ def tile_list_cable_tilt_displacement_kernel(
             return shared.tile(shape, dtype, name=name, align_bytes=64, offset=offset)
 
         kib = 1024
-        at_w1a, at_low, at_tab2w, at_tab0 = 0, 2 * kib + 64, 10 * kib, 18 * kib
-        at_tab2s, at_w1s, at_tab1, at_tabs = 33 * kib, 36 * kib + 256, 38 * kib + 512, 54 * kib + 256
+        at_w1a, at_low, at_tab2w, at_tab0 = 0, 4 * kib + 64, 12 * kib, 20 * kib
+        at_tab2s, at_w1s, at_tab1, at_tabs = 35 * kib, 38 * kib + 256, 40 * kib + 512, 56 * kib + 256
         at_raw0 = at_tabs + 4 * kib
         at_raw1 = at_tab0 + 2 * kib + 128
         list1 = keep.tile([P, S // 16], U16, name="list1")
@@ -107,17 +107,11 @@ def tile_list_cable_tilt_displacement_kernel(
         def load_tab(a, tile, cols=slice(0, T)):
             nc.sync.dma_start(tile[:, cols].bitcast(I32), tab_words[a].rearrange("p t i -> p (t i)").bitcast(I32)[:, cols])
 
-        def load_w1(g, at):
-            raw = placed([P, 2, PASS], U16, f"w1_w{g}", at)
-            words = w1_words.bitcast(I32).rearrange("a p n -> p a n")
-            nc.sync.dma_start(raw[:].bitcast(I32), words[:, :, g * PASS // 2:(g + 1) * PASS // 2])
-            return raw
-
         def order_w1(g, raw, at):
             w1p_w[g] = placed([P, 2, PASS], U16, f"w1p_w{g}", at)
             nc.vector.tensor_copy(
                 w1p_w[g][:].rearrange("p a (t m) -> p a t m", t=PACK),
-                raw[:].rearrange("p a (m t) -> p a t m", t=PACK))
+                raw[:, :, g * PASS:(g + 1) * PASS].rearrange("p a (m t) -> p a t m", t=PACK))
 
         def half(lst, jh):
             return lst[:, jh * (JW // 16):(jh + 1) * (JW // 16)]
@@ -214,7 +208,8 @@ def tile_list_cable_tilt_displacement_kernel(
         nc.sync.dma_start(tab_s[0:P:4, :].bitcast(I32), tab_scales.bitcast(I32).rearrange("a q n -> (a q) n"))
         tab2_w = placed([P, T], U16, "tab2_w", at_tab2w)
         nc.sync.dma_start(tab2_w[:].bitcast(I32), tab2_words[0].bitcast(I32))
-        w1_w0 = load_w1(0, at_w1a)
+        w1_w = placed([P, 2, H], U16, "w1_w", at_w1a)
+        nc.sync.dma_start(w1_w[:].bitcast(I32), w1_words.bitcast(I32).rearrange("a p n -> p a n"))
 
         w2_bf0 = [held([P, PASS * 2], BF16, f"w2_bf0{u}") for u in range(2)]
         for u in range(2):
@@ -254,9 +249,9 @@ def tile_list_cable_tilt_displacement_kernel(
         v_w0 = placed([P, S], U32, "v_w0", at_tab2w + 64)
         nc.vector.tensor_copy(v_w0[:], tab_w0[:].indirect(list1[:]))
         load_phase(0, 0, placed([P, PACK, JW], F32, "phase00", at_raw1)[:])
-        w1_w1 = load_w1(1, at_tab2w + 6 * kib + 128)
         load_phase(0, 1, placed([P, PACK, JW], F32, "phase01", at_raw1 + 8 * kib)[:])
-        order_w1(0, w1_w0, at_tab0 + 128)
+        order_w1(0, w1_w, at_tab0 + 128)
+        order_w1(1, w1_w, at_tab2w + 6 * kib + 128)
         w3_s = placed([P, 2, N], U8, "w3_s", at_w1s)
         nc.vector.memset(w3_s[:].rearrange("p a n -> p (a n)").bitcast(I32), 0)
         v_w1[0] = placed([P, JW], U32, "v_w10", at_w1a)
@@ -275,7 +270,7 @@ def tile_list_cable_tilt_displacement_kernel(
             prod = ring.tile([P, PACK, JW], F32, name="prod")
             for t in range(PACK):
                 product(g, jh, t, whole, sin_a, prod)
-                if t == 0 and pending is not None:
+                if t == PACK - 1 and pending is not None:
                     quantise_h(*pending)
                 if t == 0 and n == 0:
                     w2_bf11 = held([P, PASS * 2], BF16, "w2_bf11", tag="sin_00")
@@ -285,7 +280,6 @@ def tile_list_cable_tilt_displacement_kernel(
                     quantise_w2(1, 1, w2_bf11[:])
             pending = (g, jh, add_phase(g, jh, prod, whole), whole)
             if n == 0:
-                order_w1(1, w1_w1, at_raw1 + 2 * kib)
                 w3_w = placed([P, 2, N], U32, "w3_w", at_low)
                 nc.sync.dma_start(w3_w[:].bitcast(I32), w3_words.rearrange("a p c i -> p a (c i)").bitcast(I32))
             if n == 1:

@@ -44,13 +44,14 @@ def tile_list_cable_tilt_displacement_kernel(
         at_w1a, at_low, at_tab2w, at_tab0 = 0, 4 * kib + 64, 12 * kib, 20 * kib
         at_tab2s, at_w1s, at_tab1, at_tabs = 35 * kib, 38 * kib + 256, 40 * kib + 512, 56 * kib + 256
         at_raw0 = at_tabs + 4 * kib
+        at_bf0 = at_raw0 + 8 * kib
         at_raw1 = at_tab0 + 2 * kib + 128
         list1 = keep.tile([P, S // 16], U16, name="list1")
         list2 = keep.tile([P, S // 16], U16, name="list2")
         tab2_s = placed([P, T], U8, "tab2_s", at_tab2s)
         tab_s = placed([P, T], U8, "tab_s", at_tabs)
         w1p_w = {}
-        w2_c = [[held([P, 2 * P], U32, f"w2_c{g}{u}") for u in range(2)] for g in range(2)]
+        w2_c = [[held([P, 2 * P], U32, f"w2_c{g}{u}") if (g, u) != (0, 1) else None for u in range(2)] for g in range(2)]
         w2_s = [[held([P, 2 * P], U8, f"w2_s{g}{u}") for u in range(2)] for g in range(2)]
         v_w1 = {1: held([P, JW], U32, "v_w11")}
         v_s = [held([P, S], U8, f"v_s{a}") for a in range(2)]
@@ -64,14 +65,14 @@ def tile_list_cable_tilt_displacement_kernel(
         h_s = [[held([P, JW], U8, f"h_s{g}{jh}") for jh in range(2)] for g in range(2)]
         zero = placed([P, 8], F32, "zero", at_raw0)
         half_pi = held([P, 1], F32, "half_pi")
-        sine_in = placed([P, (at_tab2w + kib) // 4], F32, "sine_in", 0)
+        sine_in = placed([P, (at_tab2w - kib) // 4], F32, "sine_in", 2 * kib)
         zero_bias = held([P, 1], F32, "zero_bias")
         phase_sb = {}
 
         nc.vector.memset(tab2_s[:].bitcast(I32), 0)
+        nc.vector.memset(tab_s[:].bitcast(I32), 0)
         nc.vector.memset(zero[:, 0:1], 0.0)
         nc.vector.tensor_scalar_add(half_pi[:], zero[:, 0:1], math.pi / 2)
-        nc.vector.memset(tab_s[:].bitcast(I32), 0)
         nc.vector.memset(sine_in[:, 0:1], 0.0)
         nc.scalar.activation(zero_bias[:], sine_in[:, 0:1], ACT.Sin)
         for plane in [v2_s] + v_s:
@@ -111,7 +112,13 @@ def tile_list_cable_tilt_displacement_kernel(
             w1p_w[g] = placed([P, 2, PASS], U16, f"w1p_w{g}", at)
             nc.vector.tensor_copy(
                 w1p_w[g][:].rearrange("p a (t m) -> p a t m", t=PACK),
-                raw[:, :, g * PASS:(g + 1) * PASS].rearrange("p a (m t) -> p a t m", t=PACK))
+                raw[:].rearrange("p a (m t) -> p a t m", t=PACK))
+
+        def load_w1(g):
+            raw = placed([P, 2, PASS], U16, f"w1_w{g}", (at_w1a, at_tab2s + kib)[g])
+            cols = slice(g * PASS // 2, (g + 1) * PASS // 2)
+            nc.sync.dma_start(raw[:].bitcast(I32), w1_words.bitcast(I32).rearrange("a p n -> p a n")[:, :, cols])
+            return raw
 
         def half(lst, jh):
             return lst[:, jh * (JW // 16):(jh + 1) * (JW // 16)]
@@ -202,26 +209,25 @@ def tile_list_cable_tilt_displacement_kernel(
 
         nc.sync.dma_start(list2[:], offs2)
         nc.sync.dma_start(list1[:], offs)
+        w1_w = [load_w1(0)]
         nc.sync.dma_start(tab2_s[32:96:4, :].bitcast(I32), tab2_scales[0].bitcast(I32))
+        nc.sync.dma_start(tab_s[0:P:4, :].bitcast(I32), tab_scales.bitcast(I32).rearrange("a q n -> (a q) n"))
         w2_raw0 = placed([P, PACK, PASS], F32, "w2_raw0", at_raw0)
         load_w2(w2_raw0, 0)
-        nc.sync.dma_start(tab_s[0:P:4, :].bitcast(I32), tab_scales.bitcast(I32).rearrange("a q n -> (a q) n"))
         tab2_w = placed([P, T], U16, "tab2_w", at_tab2w)
         nc.sync.dma_start(tab2_w[:].bitcast(I32), tab2_words[0].bitcast(I32))
-        w1_w = placed([P, 2, H], U16, "w1_w", at_w1a)
-        nc.sync.dma_start(w1_w[:].bitcast(I32), w1_words.bitcast(I32).rearrange("a p n -> p a n"))
 
-        w2_bf0 = [held([P, PASS * 2], BF16, f"w2_bf0{u}") for u in range(2)]
+        w2_bf0 = [placed([P, PASS * 2], BF16, f"w2_bf0{u}", at_bf0 + u * 2 * kib) for u in range(2)]
         for u in range(2):
             round_w2(nc.scalar.copy, w2_raw0, u, w2_bf0[u][:])
         nc.vector.tensor_copy(picked2_s[:], tab2_s[:].indirect(list2[:]))
         deal_scale_rows(v2_s, picked2_s, 32)
+        w1_w.append(load_w1(1))
         tab_w0 = placed([P, T], U32, "tab_w0", at_tab0)
-        load_tab(0, tab_w0, slice(0, T // 2))
+        load_tab(0, tab_w0)
         w1_s = placed([P, 2, H], U8, "w1_s", at_w1s)
-        nc.vector.memset(w1_s[:].rearrange("p a n -> p (a n)").bitcast(I32), 0)
+        nc.gpsimd.memset(w1_s[:].rearrange("p a n -> p (a n)").bitcast(I32), 0)
         load_two_pass_scales(w1_s, w1_scales)
-        load_tab(0, tab_w0, slice(T // 2, T))
         nc.vector.tensor_copy(picked_s[:], tab_s[:].indirect(list1[:]))
         tab_w1 = placed([P, T], U32, "tab_w1", at_tab1)
         load_tab(1, tab_w1, slice(0, T // 2))
@@ -231,14 +237,15 @@ def tile_list_cable_tilt_displacement_kernel(
         quantise_w2(0, 0, w2_bf0[0][:])
         v2_w[0] = placed([P, JW], U16, "v2_w0", at_tabs + 256)
         nc.vector.tensor_copy(v2_w[0][:], tab2_w[:].indirect(half(list2, 0)))
-        quantise_w2(0, 1, w2_bf0[1][:])
         v2_w[1] = placed([P, JW], U16, "v2_w1", at_tabs + 2 * kib + 512)
         nc.vector.tensor_copy(v2_w[1][:], tab2_w[:].indirect(half(list2, 1)))
+        w2_c[0][1] = placed([P, 2 * P], U32, "w2_c01", at_tab2w + 6 * kib + 64)
+        quantise_w2(0, 1, w2_bf0[1][:])
         for jh in range(2):
             magnitudes(0, jh)
             cosines(0, jh)
 
-        gain_sb = placed([P, 2, PACK], F32, "gain_sb", at_tab2w + 6 * kib + 64)
+        gain_sb = placed([P, 2, PACK], F32, "gain_sb", at_tab2w + 7 * kib + 128)
         nc.sync.dma_start(gain_sb[:], gain.rearrange("(g p t) -> p g t", g=2, t=PACK))
         w2_raw1 = placed([P, PACK, PASS], F32, "w2_raw1", at_low)
         load_w2(w2_raw1, PASS)
@@ -246,14 +253,14 @@ def tile_list_cable_tilt_displacement_kernel(
         nc.vector.tensor_copy(
             w1p_s[:].rearrange("p a (g t m) -> p (a g) t m", g=2, t=PACK),
             w1_s[:].rearrange("p a (g m t) -> p (a g) t m", g=2, t=PACK))
-        v_w0 = placed([P, S], U32, "v_w0", at_tab2w + 64)
+        order_w1(0, w1_w[0], at_tab2w + 64)
+        order_w1(1, w1_w[1], at_tab2w + 2 * kib + 64)
+        v_w0 = held([P, S], U32, "v_w0")
         nc.vector.tensor_copy(v_w0[:], tab_w0[:].indirect(list1[:]))
         load_phase(0, 0, placed([P, PACK, JW], F32, "phase00", at_raw1)[:])
         load_phase(0, 1, placed([P, PACK, JW], F32, "phase01", at_raw1 + 8 * kib)[:])
-        order_w1(0, w1_w, at_tab0 + 128)
-        order_w1(1, w1_w, at_tab2w + 6 * kib + 128)
         w3_s = placed([P, 2, N], U8, "w3_s", at_w1s)
-        nc.vector.memset(w3_s[:].rearrange("p a n -> p (a n)").bitcast(I32), 0)
+        nc.gpsimd.memset(w3_s[:].rearrange("p a n -> p (a n)").bitcast(I32), 0)
         v_w1[0] = placed([P, JW], U32, "v_w10", at_w1a)
         for jh in range(2):
             nc.vector.tensor_copy(v_w1[jh][:], tab_w1[:].indirect(half(list1, jh)))
@@ -286,14 +293,34 @@ def tile_list_cable_tilt_displacement_kernel(
                 magnitudes(1, 0)
                 cosines(1, 0)
                 load_phase(1, 1, placed([P, PACK, JW], F32, "phase11", at_tab1 + 10 * kib)[:])
-        magnitudes(1, 1)
-        cosines(1, 1)
-        sin_a = [held([P, JW], F32, f"sin_a3{t}", tag=f"sin_1{t}") for t in range(PACK)]
-        prod = ring.tile([P, PACK, JW], F32, name="prod")
-        banks = strain_angles(1, 1)
         first, second = slice(0, JW // 2), slice(JW // 2, JW)
-        sines(banks, sin_a, first)
-        sines(banks, sin_a, second)
+        abs_last = held([P, 2, PACK, JW // 2], F32, "abs_last", tag="abs_b")
+        cos_b[1, 1] = held([P, PACK, JW], F32, "cos_b11", tag="cos_b1")
+        sin_pair = [held([P, 2, JW], F32, f"sin_last{u}") for u in range(2)]
+        sin_a = [sin_pair[t // 2][:, t % 2, :] for t in range(PACK)]
+        prod = ring.tile([P, PACK, JW], F32, name="prod")
+        for k, js in enumerate((first, second)):
+            cols = slice(JW + js.start, JW + js.stop)
+            for u in range(2):
+                bank = psum.tile([P, 2, JW // 2], F32, name="bo_bank", bufs=4)
+                for e in range(2):
+                    nc.tensor.matmul_mx(
+                        bank[:, e, :], lhsT=w2_c[1][u][:, e * P:(e + 1) * P].bitcast(FP8X4),
+                        lhsT_scale=w2_s[1][u][:, e * P:(e + 1) * P],
+                        rhs=v2_w[1][:, js].bitcast(FP4X4), rhs_scale=v2_s[:, cols], start=True, stop=True)
+                nc.scalar.activation(abs_last[:, k, 2 * u:2 * u + 2, :], bank[:], ACT.Abs)
+            nc.scalar.activation(cos_b[1, 1][:, :, js], abs_last[:, k], ACT.Sin, bias=half_pi[:], scale=-1.0)
+            for u in range(2):
+                bank = psum.tile([P, 2, JW // 2], F32, name="a_bank", bufs=4)
+                for e in range(2):
+                    t = 2 * u + e
+                    for a in range(2):
+                        codes = v_w0[:, cols] if a == 0 else v_w1[1][:, js]
+                        scols = slice(PASS + t * P, PASS + (t + 1) * P)
+                        nc.tensor.matmul_mx(
+                            bank[:, e, :], lhsT=w1p_w[1][:, a, t * P:(t + 1) * P].bitcast(FP4X4), lhsT_scale=w1p_s[:, a, scols],
+                            rhs=codes.bitcast(FP8X4), rhs_scale=v_s[a][:, cols], start=(a == 0), stop=(a == 1))
+                nc.scalar.activation(sin_pair[u][:, :, js], bank[:], ACT.Sin, bias=zero_bias[:])
         for t in range(PACK):
             product(1, 1, t, first, sin_a, prod)
             if t == 0:

@@ -33,19 +33,19 @@ def tile_list_cable_tilt_displacement_kernel(
         psum = ctx.enter_context(tc.psum_pool(name="psum", bufs=1))
 
         def held(shape, dtype, name, tag=None):
-            return keep.tile(shape, dtype, name=name, tag=tag or name, align_bytes=64)
+            return keep.tile(shape, dtype, name=name, tag=tag or name, align_bytes=256)
 
         shared = ctx.enter_context(tc.tile_pool(name="shared", bufs=1))
 
         def placed(shape, dtype, name, offset):
-            return shared.tile(shape, dtype, name=name, align_bytes=64, offset=offset)
+            return shared.tile(shape, dtype, name=name, align_bytes=256, offset=offset)
 
         kib = 1024
-        at_w1a, at_low, at_tab2w, at_tab0 = 0, 4 * kib + 64, 12 * kib, 20 * kib
+        at_w1a, at_low, at_tab2w, at_tab0 = 0, 4 * kib + 256, 12 * kib, 20 * kib
         at_tab2s, at_w1s, at_tab1, at_tabs = 35 * kib, 38 * kib + 256, 40 * kib + 512, 56 * kib + 256
         at_raw0 = at_tabs + 4 * kib
         at_bf0 = at_raw0 + 8 * kib
-        at_raw1 = at_tab0 + 2 * kib + 128
+        at_raw1 = at_tab0 + 2 * kib + 256
         list1 = keep.tile([P, S // 16], U16, name="list1")
         list2 = keep.tile([P, S // 16], U16, name="list2")
         tab2_s = placed([P, T], U8, "tab2_s", at_tab2s)
@@ -239,22 +239,22 @@ def tile_list_cable_tilt_displacement_kernel(
         nc.vector.tensor_copy(v2_w[0][:], tab2_w[:].indirect(half(list2, 0)))
         v2_w[1] = placed([P, JW], U16, "v2_w1", at_tabs + 2 * kib + 512)
         nc.vector.tensor_copy(v2_w[1][:], tab2_w[:].indirect(half(list2, 1)))
-        w2_c[0][1] = placed([P, 2 * P], U32, "w2_c01", at_tab2w + 6 * kib + 64)
+        w2_c[0][1] = placed([P, 2 * P], U32, "w2_c01", at_tab2w + 6 * kib + 256)
         quantise_w2(0, 1, w2_bf0[1][:])
         for jh in range(2):
             magnitudes(0, jh)
             cosines(0, jh)
 
-        gain_sb = placed([P, 2, PACK], F32, "gain_sb", at_tab2w + 7 * kib + 128)
+        gain_sb = placed([P, 2, PACK], F32, "gain_sb", at_tab2w + 7 * kib + 256)
         nc.sync.dma_start(gain_sb[:], gain.rearrange("(g p t) -> p g t", g=2, t=PACK))
         w2_raw1 = placed([P, PACK, PASS], F32, "w2_raw1", at_low)
         load_w2(w2_raw1, PASS)
-        w1p_s = placed([P, 2, H], U8, "w1p_s", at_tab2w + 4 * kib + 64)
+        w1p_s = placed([P, 2, H], U8, "w1p_s", at_tab2w + 4 * kib + 256)
         nc.vector.tensor_copy(
             w1p_s[:].rearrange("p a (g t m) -> p (a g) t m", g=2, t=PACK),
             w1_s[:].rearrange("p a (g m t) -> p (a g) t m", g=2, t=PACK))
-        order_w1(0, w1_w[0], at_tab2w + 64)
-        order_w1(1, w1_w[1], at_tab2w + 2 * kib + 64)
+        order_w1(0, w1_w[0], at_tab2w + 256)
+        order_w1(1, w1_w[1], at_tab2w + 2 * kib + 256)
         v_w0 = held([P, S], U32, "v_w0")
         nc.vector.tensor_copy(v_w0[:], tab_w0[:].indirect(list1[:]))
         load_phase(0, 0, placed([P, PACK, JW], F32, "phase00", at_raw1)[:])

@@ -140,7 +140,8 @@ def tile_list_cable_tilt_displacement_kernel(
 
         def cosines(g, jh):
             cos_b[g, jh] = held([P, PACK, JW], F32, f"cos_b{g}{jh}", tag=f"cos_b{jh}")
-            nc.scalar.activation(cos_b[g, jh][:], magn[g, jh][:], ACT.Sin, bias=half_pi[:], scale=-1.0)
+            for ts in (slice(0, PACK - 1), slice(PACK - 1, PACK)):
+                nc.scalar.activation(cos_b[g, jh][:, ts, :], magn[g, jh][:, ts, :], ACT.Sin, bias=half_pi[:], scale=-1.0)
 
         def strain_angles(g, jh):
             banks = [psum.tile([P, JW], F32, name="a_bank", bufs=4) for t in range(PACK)]
@@ -309,7 +310,9 @@ def tile_list_cable_tilt_displacement_kernel(
                         lhsT_scale=w2_s[1][u][:, e * P:(e + 1) * P],
                         rhs=v2_w[1][:, js].bitcast(FP4X4), rhs_scale=v2_s[:, cols], start=True, stop=True)
                 nc.scalar.activation(abs_last[:, k, 2 * u:2 * u + 2, :], bank[:], ACT.Abs)
-            nc.scalar.activation(cos_b[1, 1][:, :, js], abs_last[:, k], ACT.Sin, bias=half_pi[:], scale=-1.0)
+            for u in range(2):
+                ts = slice(2 * u, 2 * u + 2)
+                nc.scalar.activation(cos_b[1, 1][:, ts, js], abs_last[:, k, ts, :], ACT.Sin, bias=half_pi[:], scale=-1.0)
             for u in range(2):
                 bank = psum.tile([P, 2, JW // 2], F32, name="a_bank", bufs=4)
                 for e in range(2):
@@ -323,14 +326,12 @@ def tile_list_cable_tilt_displacement_kernel(
                 nc.scalar.activation(sin_pair[u][:, :, js], bank[:], ACT.Sin, bias=zero_bias[:])
         for t in range(PACK):
             product(1, 1, t, first, sin_a, prod)
-            if t == 0:
-                quantise_h(*pending)
+        quantise_h(*pending)
         close_banks(open_banks(0, whole, P), 0, whole, P, [nc.scalar.copy])
         h_first = add_phase(1, 1, prod, first)
         for t in range(PACK):
             product(1, 1, t, second, sin_a, prod)
-            if t == 0:
-                finish(h_first, first, 2 * P, [nc.scalar.copy], "a_bank")
+        finish(h_first, first, 2 * P, [nc.scalar.copy], "a_bank")
         third, fourth = slice(JW // 2, 3 * JW // 4), slice(3 * JW // 4, JW)
         h_third = add_phase(1, 1, prod, third)
         h_fourth = add_phase(1, 1, prod, fourth)

@@ -19,6 +19,7 @@ P = 128
 PACK = 4
 PASS = P * PACK
 JW = 512
+HALF_ANGLE = 2
 FLOPS = 2 * S * (K * H + M * H + H * N)
 
 
@@ -42,10 +43,10 @@ def tile_list_cable_tilt_displacement_kernel(
 
         kib = 1024
         at_w1a, at_low, at_tab2w, at_tab0 = 0, 4 * kib + 256, 12 * kib, 20 * kib
-        at_tab2s, at_w1s, at_tab1, at_tabs = 35 * kib, 38 * kib + 256, 40 * kib + 512, 56 * kib + 256
+        at_tab2s, at_w1s, at_tab1, at_tabs = 36 * kib - 256, 39 * kib + 256, 43 * kib + 512, 59 * kib + 256
         at_raw0 = at_tabs + 4 * kib
         at_bf0 = at_raw0 + 8 * kib
-        at_raw1 = at_tab0 + 2 * kib + 256
+        at_raw1 = at_tab0
         list1 = keep.tile([P, S // 16], U16, name="list1")
         list2 = keep.tile([P, S // 16], U16, name="list2")
         tab2_s = placed([P, T], U8, "tab2_s", at_tab2s)
@@ -54,9 +55,7 @@ def tile_list_cable_tilt_displacement_kernel(
         w2_c = [[held([P, 2 * P], U32, f"w2_c{g}{u}") if (g, u) != (0, 1) else None for u in range(2)] for g in range(2)]
         w2_s = [[held([P, 2 * P], U8, f"w2_s{g}{u}") for u in range(2)] for g in range(2)]
         v_w1 = {1: held([P, JW], U32, "v_w11")}
-        v_s = [held([P, S], U8, f"v_s{a}") for a in range(2)]
         v2_w = {}
-        v2_s = held([P, S], U8, "v2_s")
         picked_s = held([P, S], U8, "picked_s")
         picked2_s = held([P, S], U8, "picked2_s")
         cos_b = {}
@@ -68,6 +67,8 @@ def tile_list_cable_tilt_displacement_kernel(
         sine_in = placed([P, (at_tab2w - kib) // 4], F32, "sine_in", 2 * kib)
         zero_bias = held([P, 1], F32, "zero_bias")
         phase_sb = {}
+        half_sine = held([P, HALF_ANGLE, JW], F32, "half_sine")
+        squares = held([P, HALF_ANGLE, JW], F32, "squares")
 
         nc.vector.memset(tab2_s[:].bitcast(I32), 0)
         nc.vector.memset(tab_s[:].bitcast(I32), 0)
@@ -75,8 +76,6 @@ def tile_list_cable_tilt_displacement_kernel(
         nc.vector.tensor_scalar_add(half_pi[:], zero[:, 0:1], math.pi / 2)
         nc.vector.memset(sine_in[:, 0:1], 0.0)
         nc.scalar.activation(zero_bias[:], sine_in[:, 0:1], ACT.Sin)
-        for plane in [v2_s] + v_s:
-            nc.vector.memset(plane[:].bitcast(I32), 0)
 
         def load_two_pass_scales(plane, scales):
             rows = scales.bitcast(I32).rearrange("a (q r) n -> r q a n", r=4)
@@ -109,13 +108,13 @@ def tile_list_cable_tilt_displacement_kernel(
             nc.sync.dma_start(tile[:, cols].bitcast(I32), tab_words[a].rearrange("p t i -> p (t i)").bitcast(I32)[:, cols])
 
         def order_w1(g, raw, at):
-            w1p_w[g] = placed([P, 2, PASS], U16, f"w1p_w{g}", at)
-            nc.vector.tensor_copy(
+            w1p_w[g] = placed([P, 2, PASS], U16, f"w1p_w{g}", at) if g else held([P, 2, PASS], U16, "w1p_w0")
+            (nc.vector.tensor_copy if g else nc.scalar.copy)(
                 w1p_w[g][:].rearrange("p a (t m) -> p a t m", t=PACK),
                 raw[:].rearrange("p a (m t) -> p a t m", t=PACK))
 
         def load_w1(g):
-            raw = placed([P, 2, PASS], U16, f"w1_w{g}", (at_w1a, at_tab2s + kib)[g])
+            raw = placed([P, 2, PASS], U16, f"w1_w{g}", (at_w1a, at_tab2w + 256)[g])
             cols = slice(g * PASS // 2, (g + 1) * PASS // 2)
             nc.sync.dma_start(raw[:].bitcast(I32), w1_words.bitcast(I32).rearrange("a p n -> p a n")[:, :, cols])
             return raw
@@ -136,26 +135,30 @@ def tile_list_cable_tilt_displacement_kernel(
                     bank[:], lhsT=w2_c[g][t // 2][:, t % 2 * P:(t % 2 + 1) * P].bitcast(FP8X4),
                     lhsT_scale=w2_s[g][t // 2][:, t % 2 * P:(t % 2 + 1) * P],
                     rhs=v2_w[jh][:].bitcast(FP4X4), rhs_scale=v2_s[:, events(jh)], start=True, stop=True)
-                nc.scalar.activation(abs_b[:, t, :], bank[:], ACT.Abs)
+                if (g, jh) == (0, 0) and t < HALF_ANGLE:
+                    nc.scalar.activation(half_sine[:, t, :], bank[:], ACT.Sin, bias=zero_bias[:], scale=0.5)
+                else:
+                    nc.scalar.activation(abs_b[:, t, :], bank[:], ACT.Abs)
 
         def cosines(g, jh):
             cos_b[g, jh] = held([P, PACK, JW], F32, f"cos_b{g}{jh}", tag=f"cos_b{jh}")
-            for ts in (slice(0, PACK - 1), slice(PACK - 1, PACK)):
+            for ts in (slice(HALF_ANGLE if (g, jh) == (0, 0) else 0, PACK - 1), slice(PACK - 1, PACK)):
                 nc.scalar.activation(cos_b[g, jh][:, ts, :], magn[g, jh][:, ts, :], ACT.Sin, bias=half_pi[:], scale=-1.0)
 
         def strain_angles(g, jh):
             banks = [psum.tile([P, JW], F32, name="a_bank", bufs=4) for t in range(PACK)]
             steps = [(t, a) for t in range(PACK) for a in range(2)]
-            if (g, jh) == (0, 0):
-                steps = [(t, a) for a in range(2) for t in range(PACK)]
             for t, a in steps:
                 cols = slice(t * P, (t + 1) * P)
-                scols = slice(g * PASS + t * P, g * PASS + (t + 1) * P)
-                codes = v_w0[:, events(jh)] if a == 0 else v_w1[jh][:]
-                nc.tensor.matmul_mx(
-                    banks[t][:], lhsT=w1p_w[g][:, a, cols].bitcast(FP4X4), lhsT_scale=w1p_s[:, a, scols],
-                    rhs=codes.bitcast(FP8X4), rhs_scale=v_s[a][:, events(jh)],
-                    start=(a == 0), stop=(a == 1))
+                if (a, jh) == (1, 0):
+                    parts = [(v_head[k][:], js) for k, js in enumerate((first, second))]
+                else:
+                    parts = [(v_w0[:, events(jh)] if a == 0 else v_w1[jh][:], whole)]
+                for codes, js in parts:
+                    nc.tensor.matmul_mx(
+                        banks[t][:, js], lhsT=w1p_w[g][:, a, cols].bitcast(FP4X4), lhsT_scale=w1p_s[g][:, a, cols],
+                        rhs=codes.bitcast(FP8X4), rhs_scale=v_s[a][:, jh * JW + js.start:jh * JW + js.stop],
+                        start=(a == 0), stop=(a == 1 and js.stop == JW))
             return banks
 
         def sines(banks, sin_a, js):
@@ -218,18 +221,20 @@ def tile_list_cable_tilt_displacement_kernel(
         tab2_w = placed([P, T], U16, "tab2_w", at_tab2w)
         nc.sync.dma_start(tab2_w[:].bitcast(I32), tab2_words[0].bitcast(I32))
 
+        order_w1(0, w1_w[0], None)
         w2_bf0 = [placed([P, PASS * 2], BF16, f"w2_bf0{u}", at_bf0 + u * 2 * kib) for u in range(2)]
         for u in range(2):
             round_w2(nc.scalar.copy, w2_raw0, u, w2_bf0[u][:])
         nc.vector.tensor_copy(picked2_s[:], tab2_s[:].indirect(list2[:]))
+        v2_s = placed([P, S], U8, "v2_s", at_tab2s + 256)
         deal_scale_rows(v2_s, picked2_s, 32)
-        w1_w.append(load_w1(1))
         tab_w0 = placed([P, T], U32, "tab_w0", at_tab0)
         load_tab(0, tab_w0)
         w1_s = placed([P, 2, H], U8, "w1_s", at_w1s)
         nc.gpsimd.memset(w1_s[:].rearrange("p a n -> p (a n)").bitcast(I32), 0)
         load_two_pass_scales(w1_s, w1_scales)
         nc.vector.tensor_copy(picked_s[:], tab_s[:].indirect(list1[:]))
+        v_s = [placed([P, S], U8, f"v_s{a}", at_tabs + (1 + 2 * a) * kib + 256) for a in range(2)]
         tab_w1 = placed([P, T], U32, "tab_w1", at_tab1)
         load_tab(1, tab_w1, slice(0, T // 2))
         deal_scale_rows(v_s[0], picked_s, 0)
@@ -238,7 +243,7 @@ def tile_list_cable_tilt_displacement_kernel(
         quantise_w2(0, 0, w2_bf0[0][:])
         v2_w[0] = placed([P, JW], U16, "v2_w0", at_tabs + 256)
         nc.vector.tensor_copy(v2_w[0][:], tab2_w[:].indirect(half(list2, 0)))
-        v2_w[1] = placed([P, JW], U16, "v2_w1", at_tabs + 2 * kib + 512)
+        v2_w[1] = placed([P, JW], U16, "v2_w1", at_tabs + 2 * kib + 256)
         nc.vector.tensor_copy(v2_w[1][:], tab2_w[:].indirect(half(list2, 1)))
         w2_c[0][1] = placed([P, 2 * P], U32, "w2_c01", at_tab2w + 6 * kib + 256)
         quantise_w2(0, 1, w2_bf0[1][:])
@@ -246,55 +251,82 @@ def tile_list_cable_tilt_displacement_kernel(
             magnitudes(0, jh)
             cosines(0, jh)
 
+        w1_w.append(load_w1(1))
         gain_sb = placed([P, 2, PACK], F32, "gain_sb", at_tab2w + 7 * kib + 256)
         nc.sync.dma_start(gain_sb[:], gain.rearrange("(g p t) -> p g t", g=2, t=PACK))
         w2_raw1 = placed([P, PACK, PASS], F32, "w2_raw1", at_low)
         load_w2(w2_raw1, PASS)
-        w1p_s = placed([P, 2, H], U8, "w1p_s", at_tab2w + 4 * kib + 256)
-        nc.vector.tensor_copy(
-            w1p_s[:].rearrange("p a (g t m) -> p (a g) t m", g=2, t=PACK),
-            w1_s[:].rearrange("p a (g m t) -> p (a g) t m", g=2, t=PACK))
-        order_w1(0, w1_w[0], at_tab2w + 256)
-        order_w1(1, w1_w[1], at_tab2w + 2 * kib + 256)
+        w1p_s = [placed([P, 2, PASS], U8, f"w1p_s{g}", at_tab2w + (4 + g) * kib + 256) for g in range(2)]
+        nc.vector.scalar_tensor_tensor(squares[:], half_sine[:], -2.0, half_sine[:], ALU.mult, ALU.mult)
+        nc.vector.tensor_scalar_add(cos_b[0, 0][:, :HALF_ANGLE, :], squares[:], 1.0)
         v_w0 = held([P, S], U32, "v_w0")
         nc.vector.tensor_copy(v_w0[:], tab_w0[:].indirect(list1[:]))
+        for g in range(2):
+            rows = slice(g * PASS, (g + 1) * PASS)
+            nc.vector.tensor_copy(
+                w1p_s[g][:].rearrange("p a (t m) -> p a t m", t=PACK),
+                w1_s[:, :, rows].rearrange("p a (m t) -> p a t m", t=PACK))
         load_phase(0, 0, placed([P, PACK, JW], F32, "phase00", at_raw1)[:])
         load_phase(0, 1, placed([P, PACK, JW], F32, "phase01", at_raw1 + 8 * kib)[:])
         w3_s = placed([P, 2, N], U8, "w3_s", at_w1s)
-        nc.gpsimd.memset(w3_s[:].rearrange("p a n -> p (a n)").bitcast(I32), 0)
-        v_w1[0] = placed([P, JW], U32, "v_w10", at_w1a)
-        for jh in range(2):
-            nc.vector.tensor_copy(v_w1[jh][:], tab_w1[:].indirect(half(list1, jh)))
-        w2_bf10 = placed([P, PASS * 2], BF16, "w2_bf10", at_tab1)
-        round_w2(nc.vector.tensor_copy, w2_raw1, 0, w2_bf10[:])
-        load_phase(1, 0, placed([P, PACK, JW], F32, "phase10", at_tab1 + 2 * kib)[:])
+        first, second = slice(0, JW // 2), slice(JW // 2, JW)
+        v_head = [placed([P, JW // 2], U32, f"v_head{k}", at_w1a + k * kib) for k in range(2)]
+        for k in range(2):
+            nc.vector.tensor_copy(v_head[k][:], tab_w1[:].indirect(list1[:, k * 16:(k + 1) * 16]))
+        nc.vector.tensor_copy(v_w1[1][:], tab_w1[:].indirect(half(list1, 1)))
+        order_w1(1, w1_w[1], at_tab1 - kib - 512)
+        load_phase(1, 0, placed([P, PACK, JW], F32, "phase10", at_tab1 + 512)[:])
         load_two_pass_scales(w3_s, w3_scales)
 
         whole = slice(0, JW)
-        pending = None
-        for n, (g, jh) in enumerate(((0, 0), (0, 1), (1, 0))):
+        pieces = [(k, u) for k in range(2) for u in range(2)]
+        banks = {ku: psum.tile([P, 2, JW // 2], F32, name="a_bank", bufs=4) for ku in pieces}
+        for a in range(2):
+            for k, u in pieces:
+                js = (first, second)[k]
+                for e in range(2):
+                    cols = slice((2 * u + e) * P, (2 * u + e + 1) * P)
+                    codes = v_w0[:, js] if a == 0 else v_head[k][:]
+                    nc.tensor.matmul_mx(
+                        banks[k, u][:, e, :], lhsT=w1p_w[0][:, a, cols].bitcast(FP4X4), lhsT_scale=w1p_s[0][:, a, cols],
+                        rhs=codes.bitcast(FP8X4), rhs_scale=v_s[a][:, js],
+                        start=(a, e) == (0, 0), stop=(a, e) == (1, 1))
+        sin_head = {(k, u): held([P, 2, JW // 2], F32, f"sin_head{k}{u}", tag=f"sin_0{2 * k + u}") for k, u in pieces}
+        for ku in pieces:
+            nc.scalar.activation(sin_head[ku][:], banks[ku][:], ACT.Sin, bias=zero_bias[:])
+        prod = ring.tile([P, PACK, JW], F32, name="prod")
+        for k, u in pieces:
+            js = (first, second)[k]
+            for e in range(2):
+                t = 2 * u + e
+                nc.vector.scalar_tensor_tensor(
+                    prod[:, t, js], cos_b[0, 0][:, t, js], gain_sb[:, 0, t:t + 1], sin_head[k, u][:, e, :],
+                    ALU.mult, ALU.mult)
+                if (k, t) == (1, 2):
+                    quantise_w2(1, 0, w2_bf10[:])
+            if (k, u) == (0, 0):
+                w2_bf11 = held([P, PASS * 2], BF16, "w2_bf11", tag="sin_00")
+                round_w2(nc.scalar.copy, w2_raw1, 1, w2_bf11[:])
+            if (k, u) == (1, 0):
+                w2_bf10 = held([P, PASS * 2], BF16, "w2_bf10", tag="sin_02")
+                round_w2(nc.vector.tensor_copy, w2_raw1, 0, w2_bf10[:])
+        quantise_w2(1, 1, w2_bf11[:])
+        pending = (0, 0, add_phase(0, 0, prod, whole), whole)
+        w3_w = placed([P, 2, N], U32, "w3_w", at_low)
+        nc.sync.dma_start(w3_w[:].bitcast(I32), w3_words.rearrange("a p c i -> p a (c i)").bitcast(I32))
+        for n, (g, jh) in ((1, (0, 1)), (2, (1, 0))):
             sin_a = [held([P, JW], F32, f"sin_a{n}{t}", tag=f"sin_{n % 2}{t}") for t in range(PACK)]
             sines(strain_angles(g, jh), sin_a, whole)
             prod = ring.tile([P, PACK, JW], F32, name="prod")
             for t in range(PACK):
                 product(g, jh, t, whole, sin_a, prod)
-                if t == PACK - 1 and pending is not None:
+                if t == PACK - 1:
                     quantise_h(*pending)
-                if t == 0 and n == 0:
-                    w2_bf11 = held([P, PASS * 2], BF16, "w2_bf11", tag="sin_00")
-                    round_w2(nc.scalar.copy, w2_raw1, 1, w2_bf11[:])
-                    quantise_w2(1, 0, w2_bf10[:])
-                if t == PACK - 1 and n == 0:
-                    quantise_w2(1, 1, w2_bf11[:])
             pending = (g, jh, add_phase(g, jh, prod, whole), whole)
-            if n == 0:
-                w3_w = placed([P, 2, N], U32, "w3_w", at_low)
-                nc.sync.dma_start(w3_w[:].bitcast(I32), w3_words.rearrange("a p c i -> p a (c i)").bitcast(I32))
             if n == 1:
                 magnitudes(1, 0)
                 cosines(1, 0)
-                load_phase(1, 1, placed([P, PACK, JW], F32, "phase11", at_tab1 + 10 * kib)[:])
-        first, second = slice(0, JW // 2), slice(JW // 2, JW)
+                load_phase(1, 1, placed([P, PACK, JW], F32, "phase11", at_tab1 + 8 * kib + 512)[:])
         abs_last = held([P, 2, PACK, JW // 2], F32, "abs_last", tag="abs_b")
         cos_b[1, 1] = held([P, PACK, JW], F32, "cos_b11", tag="cos_b1")
         sin_pair = [held([P, 2, JW], F32, f"sin_last{u}") for u in range(2)]
@@ -319,9 +351,8 @@ def tile_list_cable_tilt_displacement_kernel(
                     t = 2 * u + e
                     for a in range(2):
                         codes = v_w0[:, cols] if a == 0 else v_w1[1][:, js]
-                        scols = slice(PASS + t * P, PASS + (t + 1) * P)
                         nc.tensor.matmul_mx(
-                            bank[:, e, :], lhsT=w1p_w[1][:, a, t * P:(t + 1) * P].bitcast(FP4X4), lhsT_scale=w1p_s[:, a, scols],
+                            bank[:, e, :], lhsT=w1p_w[1][:, a, t * P:(t + 1) * P].bitcast(FP4X4), lhsT_scale=w1p_s[1][:, a, t * P:(t + 1) * P],
                             rhs=codes.bitcast(FP8X4), rhs_scale=v_s[a][:, cols], start=(a == 0), stop=(a == 1))
                 nc.scalar.activation(sin_pair[u][:, :, js], bank[:], ACT.Sin, bias=zero_bias[:])
         for t in range(PACK):

@@ -53,7 +53,7 @@ def tile_list_cable_tilt_displacement_kernel(
         tab_s = placed([P, T], U8, "tab_s", at_tabs)
         w1p_w = {}
         w2_c = [[held([P, 2 * P], U32, f"w2_c{g}{u}") if (g, u) != (0, 1) else None for u in range(2)] for g in range(2)]
-        w2_s = [[held([P, 2 * P], U8, f"w2_s{g}{u}") for u in range(2)] for g in range(2)]
+        w2_s = [[held([P, 2 * P], U8, f"w2_s{g}{u}") if (g, u) != (0, 0) else None for u in range(2)] for g in range(2)]
         v_w1 = {1: held([P, JW], U32, "v_w11")}
         v2_w = {}
         picked_s = held([P, S], U8, "picked_s")
@@ -70,11 +70,11 @@ def tile_list_cable_tilt_displacement_kernel(
         half_sine = held([P, HALF_ANGLE, JW], F32, "half_sine")
         squares = held([P, HALF_ANGLE, JW], F32, "squares")
 
-        nc.vector.memset(tab2_s[:].bitcast(I32), 0)
-        nc.vector.memset(tab_s[:].bitcast(I32), 0)
         nc.vector.memset(zero[:, 0:1], 0.0)
-        nc.vector.tensor_scalar_add(half_pi[:], zero[:, 0:1], math.pi / 2)
         nc.vector.memset(sine_in[:, 0:1], 0.0)
+        nc.vector.memset(tab2_s[:].bitcast(I32), 0)
+        nc.vector.tensor_scalar_add(half_pi[:], zero[:, 0:1], math.pi / 2)
+        nc.vector.memset(tab_s[:].bitcast(I32), 0)
         nc.scalar.activation(zero_bias[:], sine_in[:, 0:1], ACT.Sin)
 
         def load_two_pass_scales(plane, scales):
@@ -114,7 +114,7 @@ def tile_list_cable_tilt_displacement_kernel(
                 raw[:].rearrange("p a (m t) -> p a t m", t=PACK))
 
         def load_w1(g):
-            raw = placed([P, 2, PASS], U16, f"w1_w{g}", (at_w1a, at_tab2w + 256)[g])
+            raw = placed([P, 2, PASS], U16, f"w1_w{g}", (at_w1a, at_w1a + 2 * kib)[g])
             cols = slice(g * PASS // 2, (g + 1) * PASS // 2)
             nc.sync.dma_start(raw[:].bitcast(I32), w1_words.bitcast(I32).rearrange("a p n -> p a n")[:, :, cols])
             return raw
@@ -215,11 +215,12 @@ def tile_list_cable_tilt_displacement_kernel(
         nc.sync.dma_start(list1[:], offs)
         w1_w = [load_w1(0)]
         nc.sync.dma_start(tab2_s[32:96:4, :].bitcast(I32), tab2_scales[0].bitcast(I32))
-        nc.sync.dma_start(tab_s[0:P:4, :].bitcast(I32), tab_scales.bitcast(I32).rearrange("a q n -> (a q) n"))
         w2_raw0 = placed([P, PACK, PASS], F32, "w2_raw0", at_raw0)
         load_w2(w2_raw0, 0)
+        nc.sync.dma_start(tab_s[0:P:4, :].bitcast(I32), tab_scales.bitcast(I32).rearrange("a q n -> (a q) n"))
         tab2_w = placed([P, T], U16, "tab2_w", at_tab2w)
         nc.sync.dma_start(tab2_w[:].bitcast(I32), tab2_words[0].bitcast(I32))
+        w1_w.append(load_w1(1))
 
         order_w1(0, w1_w[0], None)
         w2_bf0 = [placed([P, PASS * 2], BF16, f"w2_bf0{u}", at_bf0 + u * 2 * kib) for u in range(2)]
@@ -240,10 +241,11 @@ def tile_list_cable_tilt_displacement_kernel(
         deal_scale_rows(v_s[0], picked_s, 0)
         load_tab(1, tab_w1, slice(T // 2, T))
         deal_scale_rows(v_s[1], picked_s, 64)
+        w2_s[0][0] = placed([P, 2 * P], U8, "w2_s00", at_tabs + 2 * kib + 256)
         quantise_w2(0, 0, w2_bf0[0][:])
         v2_w[0] = placed([P, JW], U16, "v2_w0", at_tabs + 256)
         nc.vector.tensor_copy(v2_w[0][:], tab2_w[:].indirect(half(list2, 0)))
-        v2_w[1] = placed([P, JW], U16, "v2_w1", at_tabs + 2 * kib + 256)
+        v2_w[1] = held([P, JW], U16, "v2_w1")
         nc.vector.tensor_copy(v2_w[1][:], tab2_w[:].indirect(half(list2, 1)))
         w2_c[0][1] = placed([P, 2 * P], U32, "w2_c01", at_tab2w + 6 * kib + 256)
         quantise_w2(0, 1, w2_bf0[1][:])
@@ -251,13 +253,13 @@ def tile_list_cable_tilt_displacement_kernel(
             magnitudes(0, jh)
             cosines(0, jh)
 
-        w1_w.append(load_w1(1))
         gain_sb = placed([P, 2, PACK], F32, "gain_sb", at_tab2w + 7 * kib + 256)
         nc.sync.dma_start(gain_sb[:], gain.rearrange("(g p t) -> p g t", g=2, t=PACK))
         w2_raw1 = placed([P, PACK, PASS], F32, "w2_raw1", at_low)
         load_w2(w2_raw1, PASS)
         w1p_s = [placed([P, 2, PASS], U8, f"w1p_s{g}", at_tab2w + (4 + g) * kib + 256) for g in range(2)]
         nc.vector.scalar_tensor_tensor(squares[:], half_sine[:], -2.0, half_sine[:], ALU.mult, ALU.mult)
+        order_w1(1, w1_w[1], at_tab2w + 2 * kib + 256)
         nc.vector.tensor_scalar_add(cos_b[0, 0][:, :HALF_ANGLE, :], squares[:], 1.0)
         v_w0 = held([P, S], U32, "v_w0")
         nc.vector.tensor_copy(v_w0[:], tab_w0[:].indirect(list1[:]))
@@ -274,7 +276,6 @@ def tile_list_cable_tilt_displacement_kernel(
         for k in range(2):
             nc.vector.tensor_copy(v_head[k][:], tab_w1[:].indirect(list1[:, k * 16:(k + 1) * 16]))
         nc.vector.tensor_copy(v_w1[1][:], tab_w1[:].indirect(half(list1, 1)))
-        order_w1(1, w1_w[1], at_tab1 - kib - 512)
         load_phase(1, 0, placed([P, PACK, JW], F32, "phase10", at_tab1 + 512)[:])
         load_two_pass_scales(w3_s, w3_scales)
 

import math
from contextlib import ExitStack

import concourse.mybir as mybir

F32 = mybir.dt.float32
BF16 = mybir.dt.bfloat16
I32 = mybir.dt.int32
U32 = mybir.dt.uint32
U16 = mybir.dt.uint16
U8 = mybir.dt.uint8
FP8X4 = mybir.dt.float8_e4m3fn_x4
FP4X4 = mybir.dt.float4_e2m1fn_x4
ACT = mybir.ActivationFunctionType
ALU = mybir.AluOpType

K, M, H, N, T, S = 1024, 512, 1024, 512, 4096, 1024
P = 128
PACK = 4
PASS = P * PACK
JW = 512
HALF_ANGLE = 2
FLOPS = 2 * S * (K * H + M * H + H * N)


def tile_list_cable_tilt_displacement_kernel(
    tc, tab_words, tab_scales, tab2_words, tab2_scales, offs, offs2,
    w1_words, w1_scales, w2, w3_words, w3_scales, gain, phase, out,
):
    nc = tc.nc
    with ExitStack() as ctx:
        keep = ctx.enter_context(tc.tile_pool(name="keep", bufs=1))
        ring = ctx.enter_context(tc.tile_pool(name="ring", bufs=2))
        psum = ctx.enter_context(tc.psum_pool(name="psum", bufs=1))

        def held(shape, dtype, name, tag=None):
            return keep.tile(shape, dtype, name=name, tag=tag or name, align_bytes=256)

        shared = ctx.enter_context(tc.tile_pool(name="shared", bufs=1))

        def placed(shape, dtype, name, offset):
            return shared.tile(shape, dtype, name=name, align_bytes=256, offset=offset)

        kib = 1024
        at_w1a, at_low, at_tab2w, at_tab0 = 0, 4 * kib + 256, 12 * kib, 20 * kib
        at_tab2s, at_w1s, at_tab1, at_tabs = 36 * kib - 256, 39 * kib + 256, 43 * kib + 512, 59 * kib + 256
        at_raw0 = at_tabs + 4 * kib
        at_bf0 = at_raw0 + 8 * kib
        at_raw1 = at_tab0
        list1 = keep.tile([P, S // 16], U16, name="list1")
        list2 = keep.tile([P, S // 16], U16, name="list2")
        tab2_s = placed([P, T], U8, "tab2_s", at_tab2s)
        tab_s = placed([P, T], U8, "tab_s", at_tabs)
        w1p_w = {}
        w2_c = [[held([P, 2 * P], U32, f"w2_c{g}{u}") if (g, u) != (0, 1) else None for u in range(2)] for g in range(2)]
        w2_s = [[held([P, 2 * P], U8, f"w2_s{g}{u}") if (g, u) != (0, 0) else None for u in range(2)] for g in range(2)]
        v_w1 = {1: held([P, JW], U32, "v_w11")}
        v2_w = {}
        picked_s = held([P, S], U8, "picked_s")
        picked2_s = held([P, S], U8, "picked2_s")
        cos_b = {}
        magn = {}
        h_c = [[held([P, JW], U32, f"h_c{g}{jh}") for jh in range(2)] for g in range(2)]
        h_s = [[held([P, JW], U8, f"h_s{g}{jh}") for jh in range(2)] for g in range(2)]
        zero = placed([P, 8], F32, "zero", at_raw0)
        half_pi = held([P, 1], F32, "half_pi")
        sine_in = placed([P, (at_tab2w - kib) // 4], F32, "sine_in", 2 * kib)
        zero_bias = held([P, 1], F32, "zero_bias")
        phase_sb = {}
        half_sine = held([P, HALF_ANGLE, JW], F32, "half_sine")
        squares = held([P, HALF_ANGLE, JW], F32, "squares")

        nc.vector.memset(zero[:, 0:1], 0.0)
        nc.vector.memset(sine_in[:, 0:1], 0.0)
        nc.vector.memset(tab2_s[:].bitcast(I32), 0)
        nc.vector.tensor_scalar_add(half_pi[:], zero[:, 0:1], math.pi / 2)
        nc.vector.memset(tab_s[:].bitcast(I32), 0)
        nc.scalar.activation(zero_bias[:], sine_in[:, 0:1], ACT.Sin)

        def load_two_pass_scales(plane, scales):
            rows = scales.bitcast(I32).rearrange("a (q r) n -> r q a n", r=4)
            for r in range(4):
                nc.sync.dma_start(plane[r:P:32, :, :].bitcast(I32), rows[r])

        def round_w2(engine, raw, u, dst):
            engine(
                dst.rearrange("p (t m i) -> p m i t", t=2, i=PACK),
                raw[:].rearrange("p i (m t) -> p m i t", t=PACK)[:, :, :, 2 * u:2 * u + 2])

        def quantise_w2(g, u, src):
            nc.vector.quantize_mx(w2_c[g][u][:].bitcast(FP8X4), w2_s[g][u][:], src)

        def deal_scale_rows(plane, picked, row0):
            for r in range(4):
                first = row0 + 4 * r
                nc.sync.dma_start(plane[r:P:32, :].bitcast(I32), picked[first:first + 49:16, :].bitcast(I32))

        def load_w2(raw, c0):
            nc.sync.dma_start(raw[:], w2[:, c0:c0 + raw.shape[2]].rearrange("(p i) c -> p i c", i=PACK))

        def load_phase(g, jh, dst):
            phase_sb[g, jh] = dst
            nc.sync.dma_start(
                dst,
                phase[g * PASS:(g + 1) * PASS, jh * JW:(jh + 1) * JW].rearrange("(p t) j -> p t j", t=PACK))

        def load_tab(a, tile, cols=slice(0, T)):
            nc.sync.dma_start(tile[:, cols].bitcast(I32), tab_words[a].rearrange("p t i -> p (t i)").bitcast(I32)[:, cols])

        def order_w1(g, raw, at):
            w1p_w[g] = placed([P, 2, PASS], U16, f"w1p_w{g}", at) if g else held([P, 2, PASS], U16, "w1p_w0")
            (nc.vector.tensor_copy if g else nc.scalar.copy)(
                w1p_w[g][:].rearrange("p a (t m) -> p a t m", t=PACK),
                raw[:].rearrange("p a (m t) -> p a t m", t=PACK))

        def load_w1(g):
            raw = placed([P, 2, PASS], U16, f"w1_w{g}", (at_w1a, at_w1a + 2 * kib)[g])
            cols = slice(g * PASS // 2, (g + 1) * PASS // 2)
            nc.sync.dma_start(raw[:].bitcast(I32), w1_words.bitcast(I32).rearrange("a p n -> p a n")[:, :, cols])
            return raw

        def half(lst, jh):
            return lst[:, jh * (JW // 16):(jh + 1) * (JW // 16)]

        def events(jh):
            return slice(jh * JW, (jh + 1) * JW)

        def magnitudes(g, jh, slices=range(PACK)):
            if (g, jh) not in magn:
                magn[g, jh] = held([P, PACK, JW], F32, f"abs_b{g}{jh}", tag="abs_b")
            abs_b = magn[g, jh]
            for t in slices:
                bank = psum.tile([P, JW], F32, name="bo_bank", bufs=4)
                nc.tensor.matmul_mx(
                    bank[:], lhsT=w2_c[g][t // 2][:, t % 2 * P:(t % 2 + 1) * P].bitcast(FP8X4),
                    lhsT_scale=w2_s[g][t // 2][:, t % 2 * P:(t % 2 + 1) * P],
                    rhs=v2_w[jh][:].bitcast(FP4X4), rhs_scale=v2_s[:, events(jh)], start=True, stop=True)
                if (g, jh) == (0, 0) and t < HALF_ANGLE:
                    nc.scalar.activation(half_sine[:, t, :], bank[:], ACT.Sin, bias=zero_bias[:], scale=0.5)
                else:
                    nc.scalar.activation(abs_b[:, t, :], bank[:], ACT.Abs)

        def cosines(g, jh):
            cos_b[g, jh] = held([P, PACK, JW], F32, f"cos_b{g}{jh}", tag=f"cos_b{jh}")
            for ts in (slice(HALF_ANGLE if (g, jh) == (0, 0) else 0, PACK - 1), slice(PACK - 1, PACK)):
                nc.scalar.activation(cos_b[g, jh][:, ts, :], magn[g, jh][:, ts, :], ACT.Sin, bias=half_pi[:], scale=-1.0)

        def strain_angles(g, jh):
            banks = [psum.tile([P, JW], F32, name="a_bank", bufs=4) for t in range(PACK)]
            steps = [(t, a) for t in range(PACK) for a in range(2)]
            for t, a in steps:
                cols = slice(t * P, (t + 1) * P)
                if (a, jh) == (1, 0):
                    parts = [(v_head[k][:], js) for k, js in enumerate((first, second))]
                else:
                    parts = [(v_w0[:, events(jh)] if a == 0 else v_w1[jh][:], whole)]
                for codes, js in parts:
                    nc.tensor.matmul_mx(
                        banks[t][:, js], lhsT=w1p_w[g][:, a, cols].bitcast(FP4X4), lhsT_scale=w1p_s[g][:, a, cols],
                        rhs=codes.bitcast(FP8X4), rhs_scale=v_s[a][:, jh * JW + js.start:jh * JW + js.stop],
                        start=(a == 0), stop=(a == 1 and js.stop == JW))
            return banks

        def sines(banks, sin_a, js):
            for t, bank in enumerate(banks):
                nc.scalar.activation(sin_a[t][:, js], bank[:, js], ACT.Sin, bias=zero_bias[:])

        def product(g, jh, t, js, sin_a, prod):
            nc.vector.scalar_tensor_tensor(
                prod[:, t, js], cos_b[g, jh][:, t, js], gain_sb[:, g, t:t + 1], sin_a[t][:, js], ALU.mult, ALU.mult)

        def add_phase(g, jh, prod, js):
            h_bf = ring.tile([P, (js.stop - js.start) * PACK], BF16, name="h_bf", bufs=3, align_bytes=64)
            nc.vector.tensor_tensor(
                h_bf[:].rearrange("p (c i t) -> p c t i", i=4, t=PACK),
                prod[:, :, js].rearrange("p t (c i) -> p c t i", i=4),
                phase_sb[g, jh][:, :, js].rearrange("p t (c i) -> p c t i", i=4), ALU.add)
            return h_bf

        def quantise_h(g, jh, h_bf, js):
            nc.vector.quantize_mx(h_c[g][jh][:, js].bitcast(FP8X4), h_s[g][jh][:, js], h_bf[:])

        def last_pass(dst, c, g, jh, js, start, stop):
            cols = slice(c * P, (c + 1) * P)
            nc.tensor.matmul_mx(
                dst, lhsT=w3_w[:, g, cols].bitcast(FP8X4), lhsT_scale=w3_s[:, g, cols],
                rhs=h_c[g][jh][:, js].bitcast(FP8X4), rhs_scale=h_s[g][jh][:, js], start=start, stop=stop)

        def open_banks(jh, js, nrows, tag="bo_bank"):
            per = nrows // P
            banks = []
            for c0 in range(0, N // P, per):
                bank = psum.tile([P, per, js.stop - js.start], F32, name=tag, bufs=4)
                for k in range(per):
                    last_pass(bank[:, k, :], c0 + k, 0, jh, js, k == 0, False)
                banks.append(bank)
            return banks

        def close_banks(banks, jh, js, nrows, engines):
            per = nrows // P
            for n, bank in enumerate(banks):
                for k in range(per):
                    last_pass(bank[:, k, :], n * per + k, 1, jh, js, False, k == per - 1)
                res = held([P, per, js.stop - js.start], F32, f"res{jh}{js.start}{n}")
                engines[n % len(engines)](res[:], bank[:])
                dst = out[n * nrows:(n + 1) * nrows, jh * JW + js.start:jh * JW + js.stop]
                nc.sync.dma_start(dst.rearrange("(c p) j -> p c j", p=P), res[:])

        def finish(h_bf, js, nrows, engines, tag):
            banks = open_banks(1, js, nrows, tag)
            quantise_h(1, 1, h_bf, js)
            close_banks(banks, 1, js, nrows, engines)

        nc.sync.dma_start(list2[:], offs2)
        nc.sync.dma_start(list1[:], offs)
        w1_w = [load_w1(0)]
        nc.sync.dma_start(tab2_s[32:96:4, :].bitcast(I32), tab2_scales[0].bitcast(I32))
        w2_raw0 = placed([P, PACK, PASS], F32, "w2_raw0", at_raw0)
        load_w2(w2_raw0, 0)
        nc.sync.dma_start(tab_s[0:P:4, :].bitcast(I32), tab_scales.bitcast(I32).rearrange("a q n -> (a q) n"))
        tab2_w = placed([P, T], U16, "tab2_w", at_tab2w)
        nc.sync.dma_start(tab2_w[:].bitcast(I32), tab2_words[0].bitcast(I32))
        w1_w.append(load_w1(1))

        order_w1(0, w1_w[0], None)
        w2_bf0 = [placed([P, PASS * 2], BF16, f"w2_bf0{u}", at_bf0 + u * 2 * kib) for u in range(2)]
        for u in range(2):
            round_w2(nc.scalar.copy, w2_raw0, u, w2_bf0[u][:])
        nc.vector.tensor_copy(picked2_s[:], tab2_s[:].indirect(list2[:]))
        v2_s = placed([P, S], U8, "v2_s", at_tab2s + 256)
        deal_scale_rows(v2_s, picked2_s, 32)
        tab_w0 = placed([P, T], U32, "tab_w0", at_tab0)
        load_tab(0, tab_w0)
        w1_s = placed([P, 2, H], U8, "w1_s", at_w1s)
        nc.gpsimd.memset(w1_s[:].rearrange("p a n -> p (a n)").bitcast(I32), 0)
        load_two_pass_scales(w1_s, w1_scales)
        nc.vector.tensor_copy(picked_s[:], tab_s[:].indirect(list1[:]))
        v_s = [placed([P, S], U8, f"v_s{a}", at_tabs + (1 + 2 * a) * kib + 256) for a in range(2)]
        tab_w1 = placed([P, T], U32, "tab_w1", at_tab1)
        load_tab(1, tab_w1, slice(0, T // 2))
        deal_scale_rows(v_s[0], picked_s, 0)
        load_tab(1, tab_w1, slice(T // 2, T))
        deal_scale_rows(v_s[1], picked_s, 64)
        w2_s[0][0] = placed([P, 2 * P], U8, "w2_s00", at_tabs + 2 * kib + 256)
        quantise_w2(0, 0, w2_bf0[0][:])
        v2_w[0] = placed([P, JW], U16, "v2_w0", at_tabs + 256)
        nc.vector.tensor_copy(v2_w[0][:], tab2_w[:].indirect(half(list2, 0)))
        v2_w[1] = held([P, JW], U16, "v2_w1")
        nc.vector.tensor_copy(v2_w[1][:], tab2_w[:].indirect(half(list2, 1)))
        w2_c[0][1] = placed([P, 2 * P], U32, "w2_c01", at_tab2w + 6 * kib + 256)
        quantise_w2(0, 1, w2_bf0[1][:])
        for jh in range(2):
            magnitudes(0, jh)
            cosines(0, jh)

        gain_sb = placed([P, 2, PACK], F32, "gain_sb", at_tab2w + 7 * kib + 256)
        nc.sync.dma_start(gain_sb[:], gain.rearrange("(g p t) -> p g t", g=2, t=PACK))
        w2_raw1 = placed([P, PACK, PASS], F32, "w2_raw1", at_low)
        load_w2(w2_raw1, PASS)
        w1p_s = [placed([P, 2, PASS], U8, f"w1p_s{g}", at_tab2w + (4 + g) * kib + 256) for g in range(2)]
        nc.vector.scalar_tensor_tensor(squares[:], half_sine[:], -2.0, half_sine[:], ALU.mult, ALU.mult)
        order_w1(1, w1_w[1], at_tab2w + 2 * kib + 256)
        nc.vector.tensor_scalar_add(cos_b[0, 0][:, :HALF_ANGLE, :], squares[:], 1.0)
        v_w0 = held([P, S], U32, "v_w0")
        nc.vector.tensor_copy(v_w0[:], tab_w0[:].indirect(list1[:]))
        for g in range(2):
            rows = slice(g * PASS, (g + 1) * PASS)
            nc.vector.tensor_copy(
                w1p_s[g][:].rearrange("p a (t m) -> p a t m", t=PACK),
                w1_s[:, :, rows].rearrange("p a (m t) -> p a t m", t=PACK))
        load_phase(0, 0, placed([P, PACK, JW], F32, "phase00", at_raw1)[:])
        load_phase(0, 1, placed([P, PACK, JW], F32, "phase01", at_raw1 + 8 * kib)[:])
        w3_s = placed([P, 2, N], U8, "w3_s", at_w1s)
        first, second = slice(0, JW // 2), slice(JW // 2, JW)
        v_head = [placed([P, JW // 2], U32, f"v_head{k}", at_w1a + k * kib) for k in range(2)]
        for k in range(2):
            nc.vector.tensor_copy(v_head[k][:], tab_w1[:].indirect(list1[:, k * 16:(k + 1) * 16]))
        nc.vector.tensor_copy(v_w1[1][:], tab_w1[:].indirect(half(list1, 1)))
        load_phase(1, 0, placed([P, PACK, JW], F32, "phase10", at_tab1 + 512)[:])
        load_two_pass_scales(w3_s, w3_scales)

        whole = slice(0, JW)
        pieces = [(k, u) for k in range(2) for u in range(2)]
        banks = {ku: psum.tile([P, 2, JW // 2], F32, name="a_bank", bufs=4) for ku in pieces}
        for a in range(2):
            for k, u in pieces:
                js = (first, second)[k]
                for e in range(2):
                    cols = slice((2 * u + e) * P, (2 * u + e + 1) * P)
                    codes = v_w0[:, js] if a == 0 else v_head[k][:]
                    nc.tensor.matmul_mx(
                        banks[k, u][:, e, :], lhsT=w1p_w[0][:, a, cols].bitcast(FP4X4), lhsT_scale=w1p_s[0][:, a, cols],
                        rhs=codes.bitcast(FP8X4), rhs_scale=v_s[a][:, js],
                        start=(a, e) == (0, 0), stop=(a, e) == (1, 1))
        sin_head = {(k, u): held([P, 2, JW // 2], F32, f"sin_head{k}{u}", tag=f"sin_0{2 * k + u}") for k, u in pieces}
        for ku in pieces:
            nc.scalar.activation(sin_head[ku][:], banks[ku][:], ACT.Sin, bias=zero_bias[:])
        prod = ring.tile([P, PACK, JW], F32, name="prod")
        for k, u in pieces:
            js = (first, second)[k]
            for e in range(2):
                t = 2 * u + e
                nc.vector.scalar_tensor_tensor(
                    prod[:, t, js], cos_b[0, 0][:, t, js], gain_sb[:, 0, t:t + 1], sin_head[k, u][:, e, :],
                    ALU.mult, ALU.mult)
                if (k, t) == (1, 2):
                    quantise_w2(1, 0, w2_bf10[:])
            if (k, u) == (0, 0):
                w2_bf11 = held([P, PASS * 2], BF16, "w2_bf11", tag="sin_00")
                round_w2(nc.scalar.copy, w2_raw1, 1, w2_bf11[:])
            if (k, u) == (1, 0):
                w2_bf10 = held([P, PASS * 2], BF16, "w2_bf10", tag="sin_02")
                round_w2(nc.vector.tensor_copy, w2_raw1, 0, w2_bf10[:])
        quantise_w2(1, 1, w2_bf11[:])
        pending = (0, 0, add_phase(0, 0, prod, whole), whole)
        w3_w = placed([P, 2, N], U32, "w3_w", at_low)
        nc.sync.dma_start(w3_w[:].bitcast(I32), w3_words.rearrange("a p c i -> p a (c i)").bitcast(I32))
        for n, (g, jh) in ((1, (0, 1)), (2, (1, 0))):
            sin_a = [held([P, JW], F32, f"sin_a{n}{t}", tag=f"sin_{n % 2}{t}") for t in range(PACK)]
            sines(strain_angles(g, jh), sin_a, whole)
            prod = ring.tile([P, PACK, JW], F32, name="prod")
            for t in range(PACK):
                product(g, jh, t, whole, sin_a, prod)
                if t == PACK - 1:
                    quantise_h(*pending)
            pending = (g, jh, add_phase(g, jh, prod, whole), whole)
            if n == 1:
                magnitudes(1, 0)
                cosines(1, 0)
                load_phase(1, 1, placed([P, PACK, JW], F32, "phase11", at_tab1 + 8 * kib + 512)[:])
        abs_last = held([P, 2, PACK, JW // 2], F32, "abs_last", tag="abs_b")
        cos_b[1, 1] = held([P, PACK, JW], F32, "cos_b11", tag="cos_b1")
        sin_pair = [held([P, 2, JW], F32, f"sin_last{u}") for u in range(2)]
        sin_a = [sin_pair[t // 2][:, t % 2, :] for t in range(PACK)]
        prod = ring.tile([P, PACK, JW], F32, name="prod")
        for k, js in enumerate((first, second)):
            cols = slice(JW + js.start, JW + js.stop)
            for u in range(2):
                bank = psum.tile([P, 2, JW // 2], F32, name="bo_bank", bufs=4)
                for e in range(2):
                    nc.tensor.matmul_mx(
                        bank[:, e, :], lhsT=w2_c[1][u][:, e * P:(e + 1) * P].bitcast(FP8X4),
                        lhsT_scale=w2_s[1][u][:, e * P:(e + 1) * P],
                        rhs=v2_w[1][:, js].bitcast(FP4X4), rhs_scale=v2_s[:, cols], start=True, stop=True)
                nc.scalar.activation(abs_last[:, k, 2 * u:2 * u + 2, :], bank[:], ACT.Abs)
            for u in range(2):
                ts = slice(2 * u, 2 * u + 2)
                nc.scalar.activation(cos_b[1, 1][:, ts, js], abs_last[:, k, ts, :], ACT.Sin, bias=half_pi[:], scale=-1.0)
            for u in range(2):
                bank = psum.tile([P, 2, JW // 2], F32, name="a_bank", bufs=4)
                for e in range(2):
                    t = 2 * u + e
                    for a in range(2):
                        codes = v_w0[:, cols] if a == 0 else v_w1[1][:, js]
                        nc.tensor.matmul_mx(
                            bank[:, e, :], lhsT=w1p_w[1][:, a, t * P:(t + 1) * P].bitcast(FP4X4), lhsT_scale=w1p_s[1][:, a, t * P:(t + 1) * P],
                            rhs=codes.bitcast(FP8X4), rhs_scale=v_s[a][:, cols], start=(a == 0), stop=(a == 1))
                nc.scalar.activation(sin_pair[u][:, :, js], bank[:], ACT.Sin, bias=zero_bias[:])
        for t in range(PACK):
            product(1, 1, t, first, sin_a, prod)
        quantise_h(*pending)
        close_banks(open_banks(0, whole, P), 0, whole, P, [nc.scalar.copy])
        h_first = add_phase(1, 1, prod, first)
        for t in range(PACK):
            product(1, 1, t, second, sin_a, prod)
        finish(h_first, first, 2 * P, [nc.scalar.copy], "a_bank")
        third, fourth = slice(JW // 2, 3 * JW // 4), slice(3 * JW // 4, JW)
        h_third = add_phase(1, 1, prod, third)
        h_fourth = add_phase(1, 1, prod, fourth)
        banks_third = open_banks(1, third, 2 * P, "a_bank")
        banks_fourth = open_banks(1, fourth, 2 * P, "bo_bank")
        quantise_h(1, 1, h_third, third)
        quantise_h(1, 1, h_fourth, fourth)
        close_banks(banks_third, 1, third, 2 * P, [nc.scalar.copy, nc.vector.tensor_copy])
        close_banks(banks_fourth, 1, fourth, 2 * P, [nc.scalar.copy, nc.vector.tensor_copy])
